import numpy as np
import ml_dtypes


def mxq(x, axis, fmt="e4m3"):
    dtype, down = {"e4m3": (ml_dtypes.float8_e4m3fn, 7), "e5m2": (ml_dtypes.float8_e5m2, 14)}[fmt]
    v = np.moveaxis(np.asarray(x, np.float32).astype(ml_dtypes.bfloat16).astype(np.float64), axis, -1)
    blocks = v.reshape(v.shape[:-1] + (-1, 32))
    amax = np.abs(blocks).max(-1, keepdims=True)
    byte = np.maximum(np.where(amax > 0, np.frexp(amax)[1] - 1 + 127, 0) - down, 1)
    scale = np.exp2(byte - 127.0)
    codes = (blocks / scale).astype(np.float32).astype(dtype).astype(np.float64)
    return np.moveaxis((codes * scale).reshape(v.shape), -1, axis)


WIDE = False


def mx_kscale(k, group=512):
    if not WIDE:
        return np.ones(k)
    levels = np.array([10, -10, 5, -5, 0])
    if group != 512:
        return np.exp2(np.random.permutation(np.resize(levels, k // group))).repeat(group)
    if k % 512:
        return np.exp2(np.random.permutation(np.resize(levels, k // 32))).repeat(32)
    a = np.empty((k // 512, 16))
    for p in range(k // 512):
        a[p, :8] = np.random.permutation(np.resize(levels, 8))
        for g in range(8):
            far = levels[np.abs(levels - a[p, g]) >= 10]
            a[p, g + 8] = far[np.random.randint(len(far))]
    return np.exp2(a.ravel()).repeat(32)


def f64(x):
    return np.asarray(x).astype(np.float64)


H, D, N = 2, 256, 512


def setup_inputs():
    n = np.random.standard_normal
    s = mx_kscale(D, 0)
    u = mx_kscale(N)
    t = np.random.uniform(0.5, 2.0, N) * u
    v = n((H, N, 128))
    v[:, :, 127] = 1.0
    return {
        "q": n((H, D, N)).astype(np.float32),
        "qa": (np.random.uniform(0.5, 2.0, D) * s)[:, None].astype(np.float32),
        "ka": np.tile(np.random.uniform(0.5, 2.0, D) / s, (128, 1)).astype(np.float32),
        "k": n((H, N, D)).astype(np.float32),
        "t": t.reshape(N, 1).astype(np.float32),
        "v": (v / t[:, None]).astype(np.float32),
        "og": n((H, N, 128)).astype(np.float32),
    }


def reference(q, qa, ka, k, t, v, og):
    fq = (np.where(f64(q) > 0, f64(q) + 1.0, np.exp(np.minimum(f64(q), 0.0)))) * f64(qa)
    fk = (np.where(f64(k) > 0, f64(k) + 1.0, np.exp(np.minimum(f64(k), 0.0)))) * f64(t) * f64(ka)[:1]
    S = (mxq(fk, 1, "e4m3").transpose(0, 2, 1) @ mxq(f64(v), 1, "e4m3")) / N
    y = mxq(fq, 1, "e4m3").transpose(0, 2, 1) @ mxq(S, 1, "e4m3")
    y = y / y[:, :, 127:128]
    y = y / (1.0 + np.exp(-f64(og)))
    return y

@@ -1,0 +1,266 @@
+from contextlib import ExitStack
+
+import concourse.mybir as mybir
+
+H, D, N, E = 2, 256, 512, 128
+FLOPS = 2 * H * (N * D * E) * 2
+
+F32 = mybir.dt.float32
+BF16 = mybir.dt.bfloat16
+U32 = mybir.dt.uint32
+U8 = mybir.dt.uint8
+FP8X4 = mybir.dt.float8_e4m3fn_x4
+ACT = mybir.ActivationFunctionType
+ALU = mybir.AluOpType
+
+P = 128
+PACK = 4
+ROWS = 64
+CHUNKS = [(0, 256), (256, 128), (384, 128)]
+
+
+def tile_rows_lin_elu1_norm_gate_kernel(tc, q, qa, ka, k, t, v, og, out):
+    nc = tc.nc
+    with ExitStack() as ctx:
+        sb = ctx.enter_context(tc.tile_pool(name="sb", bufs=1))
+        ps = ctx.enter_context(tc.psum_pool(name="ps", bufs=1))
+        ctx.enter_context(tc.manual_schedule())
+
+        def sbuf(name, shape, dtype):
+            return sb.tile(shape, dtype, name=name, align_bytes=64)
+
+        t_sb = sbuf("t_sb", [P, PACK], F32)
+        ka_sb = sbuf("ka_sb", [P, D], F32)
+        nc.scalar.dma_start(out=ka_sb[:], in_=ka)
+        nc.scalar.dma_start(out=t_sb[:], in_=t.rearrange("(p j) o -> p (j o)", j=PACK))
+
+        qa_rows = sbuf("qa_rows", [P, 32], F32)
+        nc.gpsimd.memset(qa_rows[:], 0.0)
+        qa_v = qa.rearrange("(a b x s) o -> a x b (s o)", a=2, b=4, x=4)
+        for quad in range(4):
+            nc.gpsimd.dma_start(
+                out=qa_rows[32 * quad : 32 * quad + 4, :].rearrange("p (b s) -> p b s", s=8), in_=qa_v[quad % 2]
+            )
+
+        k_raw = {}
+        for h in range(H):
+            for jj in range(2):
+                k_raw[h, jj] = sbuf("k_raw%d%d" % (h, jj), [P, 2, D], F32)
+        v_raw = sbuf("v_raw", [P, H, PACK * E], F32)
+        q_raw = sbuf("q_raw", [P, PACK, N], F32)
+        og_raw = sbuf("og_raw", [P, H, 4, E], F32)
+
+        def load_k(h, jj):
+            nc.sync.dma_start(out=k_raw[h, jj][:], in_=k[h].rearrange("(p j) d -> p j d", j=PACK)[:, 2 * jj : 2 * jj + 2, :])
+
+        load_k(0, 0)
+        load_k(0, 1)
+        nc.sync.dma_start(out=v_raw[:], in_=v.rearrange("h (p j) e -> p h (j e)", j=PACK))
+        load_k(1, 0)
+        load_k(1, 1)
+        q_v = q.rearrange("h (b x s) n -> x (h b) s n", x=4, s=8)
+        for x in range(PACK):
+            nc.sync.dma_start(out=q_raw[:, x, :], in_=q_v[x])
+        nc.sync.dma_start(out=og_raw[:].rearrange("p h r e -> p (h r) e"), in_=og.rearrange("h (r p) e -> p (h r) e", p=P))
+
+        w_sb = sbuf("w_sb", [P, D, PACK], F32)
+        qa_cols = sbuf("qa_cols", [P, 32], F32)
+        k_neg, k_exp, k_phi, k_bf = {}, {}, {}, {}
+        for h in range(H):
+            k_phi[h] = sbuf("k_phi%d" % h, [P, 2, D, 2], F32)
+            k_bf[h] = sbuf("k_bf%d" % h, [P, D * PACK], BF16)
+            for jj in range(2):
+                k_neg[h, jj] = sbuf("k_neg%d%d" % (h, jj), [P, D, 2], F32)
+                k_exp[h, jj] = sbuf("k_exp%d%d" % (h, jj), [P, D, 2], F32)
+        v_bf = sbuf("v_bf", [P, H, E * PACK], BF16)
+        kv_codes = sbuf("kv_codes", [P, 3 * D], U32)
+        kv_scales = sbuf("kv_scales", [P, 3 * D], U8)
+        s_bf = sbuf("s_bf", [P, E, PACK], BF16)
+        s_codes = sbuf("s_codes", [P, E], U32)
+        s_scales = sbuf("s_scales", [P, E], U8)
+        s_ps = [ps.tile([P, PACK, E], F32, name="s_ps%d" % h) for h in range(H)]
+        q_neg, q_exp, q_phi, q_bf, q_codes, q_scales, y_ps, gate_t, gate, rec, res = {}, {}, {}, {}, {}, {}, {}, {}, {}, {}, {}
+        for c, (n0, w) in enumerate(CHUNKS):
+            tiles = w // P
+            q_neg[c] = sbuf("q_neg%d" % c, [P, 2, w, 2], F32)
+            q_exp[c] = sbuf("q_exp%d" % c, [P, 2, w, 2], F32)
+            q_phi[c] = sbuf("q_phi%d" % c, [P, 2, w, 2], F32)
+            q_bf[c] = sbuf("q_bf%d" % c, [P, w * PACK], BF16)
+            q_codes[c] = sbuf("q_codes%d" % c, [P, w], U32)
+            q_scales[c] = sbuf("q_scales%d" % c, [P, w], U8)
+            gate_t[c] = sbuf("gate_t%d" % c, [P, H, tiles * E], F32)
+            gate[c] = sbuf("gate%d" % c, [P, H, tiles * E], F32)
+            for h in range(H):
+                y_ps[c, h] = ps.tile([P, 512], F32, name="y_ps%d%d" % (c, h))
+                rec[c, h] = sbuf("rec%d%d" % (c, h), [P, tiles], F32)
+                res[c, h] = sbuf("res%d%d" % (c, h), [P, tiles, E], F32)
+
+        def k_exp_step(h, jj):
+            nc.scalar.activation(out=k_neg[h, jj][:], in_=k_raw[h, jj][:].rearrange("p i d -> p d i"), func=ACT.Relu, scale=-1.0)
+            nc.scalar.activation(out=k_exp[h, jj][:], in_=k_neg[h, jj][:], func=ACT.Exp, scale=-1.0)
+
+        def k_phi_step(h, jj):
+            nc.vector.scalar_tensor_tensor(
+                out=k_phi[h][:, jj], in0=k_raw[h, jj][:].rearrange("p i d -> p d i"), scalar=0.0,
+                in1=k_exp[h, jj][:], op0=ALU.max, op1=ALU.add,
+            )
+
+        def k_weigh(h):
+            nc.vector.tensor_tensor(
+                out=k_bf[h][:].rearrange("p (x b s jj i) -> p b x s jj i", x=4, b=8, s=8, jj=2),
+                in0=k_phi[h][:].rearrange("p jj (b x s) i -> p b x s jj i", b=8, x=4),
+                in1=w_sb[:].rearrange("p (b x s) (jj i) -> p b x s jj i", b=8, x=4, jj=2),
+                op=ALU.mult,
+            )
+
+        def k_quant(h):
+            cols = slice(2 * D * h, 2 * D * h + D)
+            nc.vector.quantize_mx(out=kv_codes[:, cols].bitcast(FP8X4), scales=kv_scales[:, cols], in_=k_bf[h][:])
+
+        def v_cast(h):
+            nc.vector.tensor_copy(
+                out=v_bf[:, h, :].rearrange("p (c i j) -> p c j i", i=4, j=PACK),
+                in_=v_raw[:, h, :].rearrange("p (j c i) -> p c j i", j=PACK, i=4),
+            )
+
+        def v_quant():
+            cols = slice(D, 2 * D)
+            nc.vector.quantize_mx(
+                out=kv_codes[:, cols].bitcast(FP8X4), scales=kv_scales[:, cols], in_=v_bf[:].rearrange("p h c -> p (h c)")
+            )
+
+        def state_mm(h):
+            v_cols = slice(D + E * h, D + E * (h + 1))
+            for x in range(PACK):
+                first = 2 * D * h + ROWS * (x - h)
+                k_cols = slice(first, first + P)
+                nc.tensor.matmul_mx(
+                    out=s_ps[h][:, x, :],
+                    lhsT=kv_codes[:, k_cols].bitcast(FP8X4), lhsT_scale=kv_scales[:, k_cols],
+                    rhs=kv_codes[:, v_cols].bitcast(FP8X4), rhs_scale=kv_scales[:, v_cols],
+                    start=True, stop=True,
+                )
+
+        def state_copy(h):
+            rows = slice(ROWS * h, ROWS * (h + 1))
+            nc.scalar.activation(
+                out=s_bf[rows], in_=s_ps[h][rows].rearrange("p x e -> p e x"), func=ACT.Copy, scale=1.0 / N
+            )
+
+        def state_quant():
+            nc.vector.quantize_mx(out=s_codes[:].bitcast(FP8X4), scales=s_scales[:], in_=s_bf[:].rearrange("p e x -> p (e x)"))
+
+        def q_view(c):
+            n0, w = CHUNKS[c]
+            return q_raw[:, :, n0 : n0 + w].rearrange("p (xx i) n -> p xx n i", i=2)
+
+        def q_exp_step(c):
+            nc.scalar.activation(out=q_neg[c][:], in_=q_view(c), func=ACT.Relu, scale=-1.0)
+            nc.scalar.activation(out=q_exp[c][:], in_=q_neg[c][:], func=ACT.Exp, scale=-1.0)
+
+        def q_phi_step(c, xx):
+            nc.vector.scalar_tensor_tensor(
+                out=q_phi[c][:, xx], in0=q_view(c)[:, xx], scalar=0.0, in1=q_exp[c][:, xx], op0=ALU.max, op1=ALU.add
+            )
+
+        def q_weigh(c):
+            w = CHUNKS[c][1]
+            nc.vector.tensor_tensor(
+                out=q_bf[c][:].rearrange("p (n xx i) -> p n xx i", xx=2, i=2),
+                in0=q_phi[c][:].rearrange("p xx n i -> p n xx i"),
+                in1=qa_cols[:, 0:PACK].rearrange("p (xx i) -> p xx i", i=2).unsqueeze(1).to_broadcast([P, w, 2, 2]),
+                op=ALU.mult,
+            )
+
+        def q_quant(c):
+            nc.vector.quantize_mx(out=q_codes[c][:].bitcast(FP8X4), scales=q_scales[c][:], in_=q_bf[c][:])
+
+        def read_mm(c):
+            for h in range(H):
+                rows = slice(ROWS * h, ROWS * (h + 1))
+                for r in range(CHUNKS[c][1] // P):
+                    cols = slice(P * r, P * (r + 1))
+                    nc.tensor.matmul_mx(
+                        out=y_ps[c, h][:, cols],
+                        lhsT=q_codes[c][rows, cols].bitcast(FP8X4), lhsT_scale=q_scales[c][rows, cols],
+                        rhs=s_codes[rows, :].bitcast(FP8X4), rhs_scale=s_scales[rows, :],
+                        start=True, stop=True,
+                    )
+
+        def gate_step(c):
+            n0, w = CHUNKS[c]
+            src = og_raw[:, :, n0 // P : (n0 + w) // P, :].rearrange("p h r e -> p h (r e)")
+            nc.scalar.activation(out=gate_t[c][:], in_=src, func=ACT.Tanh, scale=0.5)
+            nc.scalar.activation(out=gate[c][:], in_=gate_t[c][:], func=ACT.Identity, scale=0.5, bias=0.5)
+
+        def recip(c, h):
+            w = CHUNKS[c][1]
+            nc.vector.reciprocal(out=rec[c, h][:], in_=y_ps[c, h][:, E - 1 : w : E])
+
+        def finish(c, h):
+            n0, w = CHUNKS[c]
+            for r in range(w // P):
+                cols = slice(E * r, E * (r + 1))
+                nc.vector.scalar_tensor_tensor(
+                    out=res[c, h][:, r, :], in0=y_ps[c, h][:, cols], scalar=rec[c, h][:, r : r + 1],
+                    in1=gate[c][:, h, cols], op0=ALU.mult, op1=ALU.mult,
+                )
+            nc.sync.dma_start(out=out[h, n0 : n0 + w, :].rearrange("(r p) e -> p r e", p=P), in_=res[c, h][:])
+
+        nc.vector.tensor_tensor(
+            out=w_sb[:],
+            in0=ka_sb[:].unsqueeze(2).to_broadcast([P, D, PACK]),
+            in1=t_sb[:].unsqueeze(1).to_broadcast([P, D, PACK]),
+            op=ALU.mult,
+        )
+        k_exp_step(0, 0)
+        k_phi_step(0, 0)
+        k_exp_step(0, 1)
+        v_cast(0)
+        k_phi_step(0, 1)
+        v_cast(1)
+        k_exp_step(1, 0)
+        k_weigh(0)
+        k_phi_step(1, 0)
+        k_exp_step(1, 1)
+        k_quant(0)
+        k_phi_step(1, 1)
+        v_quant()
+        state_mm(0)
+        q_exp_step(0)
+        k_weigh(1)
+        nc.vector.transpose(out=qa_cols[:], in_=qa_rows[:])
+        q_phi_step(0, 0)
+        k_quant(1)
+        state_mm(1)
+        state_copy(0)
+        q_exp_step(1)
+        state_copy(1)
+        q_phi_step(0, 1)
+        q_phi_step(1, 0)
+        q_weigh(0)
+        q_exp_step(2)
+        q_phi_step(1, 1)
+        q_quant(0)
+        state_quant()
+        read_mm(0)
+        gate_step(0)
+        q_weigh(1)
+        q_phi_step(2, 0)
+        q_quant(1)
+        read_mm(1)
+        gate_step(1)
+        q_phi_step(2, 1)
+        recip(0, 0)
+        recip(0, 1)
+        q_weigh(2)
+        finish(0, 0)
+        q_quant(2)
+        read_mm(2)
+        gate_step(2)
+        finish(0, 1)
+        for c in (1, 2):
+            recip(c, 0)
+            recip(c, 1)
+            finish(c, 0)
+            finish(c, 1)

@@ -16,7 +16,7 @@ ALU = mybir.AluOpType
 P = 128
 PACK = 4
 ROWS = 64
-CHUNKS = [(0, 256), (256, 128), (384, 128)]
+CHUNKS = [(0, 128), (128, 256), (384, 128)]
 
 
 def tile_rows_lin_elu1_norm_gate_kernel(tc, q, qa, ka, k, t, v, og, out):
@@ -31,22 +31,17 @@ def tile_rows_lin_elu1_norm_gate_kernel(tc, q, qa, ka, k, t, v, og, out):
 
         t_sb = sbuf("t_sb", [P, PACK], F32)
         ka_sb = sbuf("ka_sb", [P, D], F32)
-        nc.scalar.dma_start(out=ka_sb[:], in_=ka)
         nc.scalar.dma_start(out=t_sb[:], in_=t.rearrange("(p j) o -> p (j o)", j=PACK))
+        nc.scalar.dma_start(out=ka_sb[:], in_=ka)
 
         qa_rows = sbuf("qa_rows", [P, 32], F32)
-        nc.gpsimd.memset(qa_rows[:], 0.0)
-        qa_v = qa.rearrange("(a b x s) o -> a x b (s o)", a=2, b=4, x=4)
-        for quad in range(4):
-            nc.gpsimd.dma_start(
-                out=qa_rows[32 * quad : 32 * quad + 4, :].rearrange("p (b s) -> p b s", s=8), in_=qa_v[quad % 2]
-            )
+        nc.vector.memset(qa_rows[:], 0.0)
 
         k_raw = {}
         for h in range(H):
             for jj in range(2):
                 k_raw[h, jj] = sbuf("k_raw%d%d" % (h, jj), [P, 2, D], F32)
-        v_raw = sbuf("v_raw", [P, H, PACK * E], F32)
+        v_raw = [sbuf("v_raw%d" % h, [P, PACK * E], F32) for h in range(H)]
         q_raw = sbuf("q_raw", [P, PACK, N], F32)
         og_raw = sbuf("og_raw", [P, H, 4, E], F32)
 
@@ -55,24 +50,30 @@ def tile_rows_lin_elu1_norm_gate_kernel(tc, q, qa, ka, k, t, v, og, out):
 
         load_k(0, 0)
         load_k(0, 1)
-        nc.sync.dma_start(out=v_raw[:], in_=v.rearrange("h (p j) e -> p h (j e)", j=PACK))
+        nc.sync.dma_start(out=v_raw[0][:], in_=v[0].rearrange("(p j) e -> p (j e)", j=PACK))
         load_k(1, 0)
         load_k(1, 1)
-        q_v = q.rearrange("h (b x s) n -> x (h b) s n", x=4, s=8)
+        nc.sync.dma_start(out=v_raw[1][:], in_=v[1].rearrange("(p j) e -> p (j e)", j=PACK))
+        q_v = q.rearrange("h (c x i) n -> x (h c) i n", x=4, i=2)
         for x in range(PACK):
             nc.sync.dma_start(out=q_raw[:, x, :], in_=q_v[x])
+        qa_v = qa.rearrange("(a c x i) o -> a x c (i o)", a=2, x=4, i=2)
+        for quad in range(4):
+            nc.sync.dma_start(
+                out=qa_rows[32 * quad : 32 * quad + 4, :].rearrange("p (c i) -> p c i", i=2), in_=qa_v[quad % 2]
+            )
         nc.sync.dma_start(out=og_raw[:].rearrange("p h r e -> p (h r) e"), in_=og.rearrange("h (r p) e -> p (h r) e", p=P))
 
-        w_sb = sbuf("w_sb", [P, D, PACK], F32)
+        w_sb = sbuf("w_sb", [P, PACK, D], F32)
         qa_cols = sbuf("qa_cols", [P, 32], F32)
         k_neg, k_exp, k_phi, k_bf = {}, {}, {}, {}
         for h in range(H):
-            k_phi[h] = sbuf("k_phi%d" % h, [P, 2, D, 2], F32)
-            k_bf[h] = sbuf("k_bf%d" % h, [P, D * PACK], BF16)
+            k_phi[h] = sbuf("k_phi%d" % h, [P, PACK, D], F32)
+            k_bf[h] = sbuf("k_bf%d" % h, [P, PACK, D], BF16)
             for jj in range(2):
-                k_neg[h, jj] = sbuf("k_neg%d%d" % (h, jj), [P, D, 2], F32)
-                k_exp[h, jj] = sbuf("k_exp%d%d" % (h, jj), [P, D, 2], F32)
-        v_bf = sbuf("v_bf", [P, H, E * PACK], BF16)
+                k_neg[h, jj] = sbuf("k_neg%d%d" % (h, jj), [P, 2, D], F32)
+                k_exp[h, jj] = sbuf("k_exp%d%d" % (h, jj), [P, 2, D], F32)
+        v_bf = [sbuf("v_bf%d" % h, [P, E * PACK], BF16) for h in range(H)]
         kv_codes = sbuf("kv_codes", [P, 3 * D], U32)
         kv_scales = sbuf("kv_scales", [P, 3 * D], U8)
         s_bf = sbuf("s_bf", [P, E, PACK], BF16)
@@ -82,9 +83,9 @@ def tile_rows_lin_elu1_norm_gate_kernel(tc, q, qa, ka, k, t, v, og, out):
         q_neg, q_exp, q_phi, q_bf, q_codes, q_scales, y_ps, gate_t, gate, rec, res = {}, {}, {}, {}, {}, {}, {}, {}, {}, {}, {}
         for c, (n0, w) in enumerate(CHUNKS):
             tiles = w // P
-            q_neg[c] = sbuf("q_neg%d" % c, [P, 2, w, 2], F32)
-            q_exp[c] = sbuf("q_exp%d" % c, [P, 2, w, 2], F32)
-            q_phi[c] = sbuf("q_phi%d" % c, [P, 2, w, 2], F32)
+            q_neg[c] = sbuf("q_neg%d" % c, [P, PACK, w], F32)
+            q_exp[c] = sbuf("q_exp%d" % c, [P, PACK, w], F32)
+            q_phi[c] = sbuf("q_phi%d" % c, [P, PACK, w], F32)
             q_bf[c] = sbuf("q_bf%d" % c, [P, w * PACK], BF16)
             q_codes[c] = sbuf("q_codes%d" % c, [P, w], U32)
             q_scales[c] = sbuf("q_scales%d" % c, [P, w], U8)
@@ -95,39 +96,48 @@ def tile_rows_lin_elu1_norm_gate_kernel(tc, q, qa, ka, k, t, v, og, out):
                 rec[c, h] = sbuf("rec%d%d" % (c, h), [P, tiles], F32)
                 res[c, h] = sbuf("res%d%d" % (c, h), [P, tiles, E], F32)
 
+        def k_weight(j):
+            nc.vector.tensor_scalar(out=w_sb[:, j, :], in0=ka_sb[:], scalar1=t_sb[:, j : j + 1], scalar2=None, op0=ALU.mult)
+
+        def k_min_vector(h, jj):
+            nc.vector.tensor_scalar(out=k_neg[h, jj][:], in0=k_raw[h, jj][:], scalar1=-1.0, scalar2=0.0, op0=ALU.mult, op1=ALU.max)
+
+        def k_min_scalar(h, jj):
+            nc.scalar.activation(out=k_neg[h, jj][:], in_=k_raw[h, jj][:], func=ACT.Relu, scale=-1.0)
+
         def k_exp_step(h, jj):
-            nc.scalar.activation(out=k_neg[h, jj][:], in_=k_raw[h, jj][:].rearrange("p i d -> p d i"), func=ACT.Relu, scale=-1.0)
             nc.scalar.activation(out=k_exp[h, jj][:], in_=k_neg[h, jj][:], func=ACT.Exp, scale=-1.0)
 
         def k_phi_step(h, jj):
             nc.vector.scalar_tensor_tensor(
-                out=k_phi[h][:, jj], in0=k_raw[h, jj][:].rearrange("p i d -> p d i"), scalar=0.0,
+                out=k_phi[h][:, 2 * jj : 2 * jj + 2, :], in0=k_raw[h, jj][:], scalar=0.0,
                 in1=k_exp[h, jj][:], op0=ALU.max, op1=ALU.add,
             )
 
         def k_weigh(h):
-            nc.vector.tensor_tensor(
-                out=k_bf[h][:].rearrange("p (x b s jj i) -> p b x s jj i", x=4, b=8, s=8, jj=2),
-                in0=k_phi[h][:].rearrange("p jj (b x s) i -> p b x s jj i", b=8, x=4),
-                in1=w_sb[:].rearrange("p (b x s) (jj i) -> p b x s jj i", b=8, x=4, jj=2),
-                op=ALU.mult,
-            )
+            for x in range(PACK):
+                nc.vector.tensor_tensor(
+                    out=k_bf[h][:, x, :].rearrange("p (c i j) -> p c j i", i=2, j=PACK),
+                    in0=k_phi[h][:].rearrange("p j (c x i) -> p x c j i", x=PACK, i=2)[:, x],
+                    in1=w_sb[:].rearrange("p j (c x i) -> p x c j i", x=PACK, i=2)[:, x],
+                    op=ALU.mult,
+                )
 
         def k_quant(h):
             cols = slice(2 * D * h, 2 * D * h + D)
-            nc.vector.quantize_mx(out=kv_codes[:, cols].bitcast(FP8X4), scales=kv_scales[:, cols], in_=k_bf[h][:])
+            nc.vector.quantize_mx(
+                out=kv_codes[:, cols].bitcast(FP8X4), scales=kv_scales[:, cols], in_=k_bf[h][:].rearrange("p x c -> p (x c)")
+            )
 
         def v_cast(h):
-            nc.vector.tensor_copy(
-                out=v_bf[:, h, :].rearrange("p (c i j) -> p c j i", i=4, j=PACK),
-                in_=v_raw[:, h, :].rearrange("p (j c i) -> p c j i", j=PACK, i=4),
+            nc.scalar.copy(
+                out=v_bf[h][:].rearrange("p (c i j) -> p c j i", i=4, j=PACK),
+                in_=v_raw[h][:].rearrange("p (j c i) -> p c j i", j=PACK, i=4),
             )
 
-        def v_quant():
-            cols = slice(D, 2 * D)
-            nc.vector.quantize_mx(
-                out=kv_codes[:, cols].bitcast(FP8X4), scales=kv_scales[:, cols], in_=v_bf[:].rearrange("p h c -> p (h c)")
-            )
+        def v_quant(h):
+            cols = slice(D + E * h, D + E * (h + 1))
+            nc.vector.quantize_mx(out=kv_codes[:, cols].bitcast(FP8X4), scales=kv_scales[:, cols], in_=v_bf[h][:])
 
         def state_mm(h):
             v_cols = slice(D + E * h, D + E * (h + 1))
@@ -152,23 +162,23 @@ def tile_rows_lin_elu1_norm_gate_kernel(tc, q, qa, ka, k, t, v, og, out):
 
         def q_view(c):
             n0, w = CHUNKS[c]
-            return q_raw[:, :, n0 : n0 + w].rearrange("p (xx i) n -> p xx n i", i=2)
+            return q_raw[:, :, n0 : n0 + w]
 
         def q_exp_step(c):
             nc.scalar.activation(out=q_neg[c][:], in_=q_view(c), func=ACT.Relu, scale=-1.0)
             nc.scalar.activation(out=q_exp[c][:], in_=q_neg[c][:], func=ACT.Exp, scale=-1.0)
 
-        def q_phi_step(c, xx):
+        def q_phi_step(c):
             nc.vector.scalar_tensor_tensor(
-                out=q_phi[c][:, xx], in0=q_view(c)[:, xx], scalar=0.0, in1=q_exp[c][:, xx], op0=ALU.max, op1=ALU.add
+                out=q_phi[c][:], in0=q_view(c), scalar=0.0, in1=q_exp[c][:], op0=ALU.max, op1=ALU.add
             )
 
         def q_weigh(c):
             w = CHUNKS[c][1]
             nc.vector.tensor_tensor(
-                out=q_bf[c][:].rearrange("p (n xx i) -> p n xx i", xx=2, i=2),
-                in0=q_phi[c][:].rearrange("p xx n i -> p n xx i"),
-                in1=qa_cols[:, 0:PACK].rearrange("p (xx i) -> p xx i", i=2).unsqueeze(1).to_broadcast([P, w, 2, 2]),
+                out=q_bf[c][:].rearrange("p (m i x) -> p m x i", i=2, x=PACK),
+                in0=q_phi[c][:].rearrange("p x (m i) -> p m x i", i=2),
+                in1=qa_cols[:, 0:PACK].unsqueeze(1).unsqueeze(3).to_broadcast([P, w // 2, PACK, 2]),
                 op=ALU.mult,
             )
 
@@ -207,58 +217,58 @@ def tile_rows_lin_elu1_norm_gate_kernel(tc, q, qa, ka, k, t, v, og, out):
                 )
             nc.sync.dma_start(out=out[h, n0 : n0 + w, :].rearrange("(r p) e -> p r e", p=P), in_=res[c, h][:])
 
-        nc.vector.tensor_tensor(
-            out=w_sb[:],
-            in0=ka_sb[:].unsqueeze(2).to_broadcast([P, D, PACK]),
-            in1=t_sb[:].unsqueeze(1).to_broadcast([P, D, PACK]),
-            op=ALU.mult,
-        )
+        k_weight(0)
+        k_weight(1)
+        k_min_vector(0, 0)
         k_exp_step(0, 0)
-        k_phi_step(0, 0)
+        k_weight(2)
+        k_weight(3)
+        k_min_vector(0, 1)
         k_exp_step(0, 1)
-        v_cast(0)
+        k_phi_step(0, 0)
         k_phi_step(0, 1)
-        v_cast(1)
+        v_cast(0)
+        k_min_vector(1, 0)
         k_exp_step(1, 0)
         k_weigh(0)
-        k_phi_step(1, 0)
+        k_min_scalar(1, 1)
         k_exp_step(1, 1)
+        k_phi_step(1, 0)
         k_quant(0)
         k_phi_step(1, 1)
-        v_quant()
+        v_quant(0)
         state_mm(0)
-        q_exp_step(0)
+        v_cast(1)
         k_weigh(1)
-        nc.vector.transpose(out=qa_cols[:], in_=qa_rows[:])
-        q_phi_step(0, 0)
+        v_quant(1)
         k_quant(1)
         state_mm(1)
-        state_copy(0)
+        q_exp_step(0)
         q_exp_step(1)
+        state_copy(0)
         state_copy(1)
-        q_phi_step(0, 1)
-        q_phi_step(1, 0)
+        q_phi_step(0)
+        nc.vector.transpose(out=qa_cols[:], in_=qa_rows[:])
+        q_phi_step(1)
         q_weigh(0)
-        q_exp_step(2)
-        q_phi_step(1, 1)
-        q_quant(0)
         state_quant()
+        q_quant(0)
         read_mm(0)
+        q_exp_step(2)
         gate_step(0)
         q_weigh(1)
-        q_phi_step(2, 0)
+        q_phi_step(2)
         q_quant(1)
         read_mm(1)
         gate_step(1)
-        q_phi_step(2, 1)
+        gate_step(2)
         recip(0, 0)
         recip(0, 1)
         q_weigh(2)
         finish(0, 0)
+        finish(0, 1)
         q_quant(2)
         read_mm(2)
-        gate_step(2)
-        finish(0, 1)
         for c in (1, 2):
             recip(c, 0)
             recip(c, 1)

@@ -16,7 +16,7 @@ ALU = mybir.AluOpType
 P = 128
 PACK = 4
 ROWS = 64
-CHUNKS = [(0, 128), (128, 256), (384, 128)]
+CHUNKS = [(0, 256), (256, 256)]
 
 
 def tile_rows_lin_elu1_norm_gate_kernel(tc, q, qa, ka, k, t, v, og, out):
@@ -31,8 +31,6 @@ def tile_rows_lin_elu1_norm_gate_kernel(tc, q, qa, ka, k, t, v, og, out):
 
         t_sb = sbuf("t_sb", [P, PACK], F32)
         ka_sb = sbuf("ka_sb", [P, D], F32)
-        nc.scalar.dma_start(out=t_sb[:], in_=t.rearrange("(p j) o -> p (j o)", j=PACK))
-        nc.scalar.dma_start(out=ka_sb[:], in_=ka)
 
         qa_rows = sbuf("qa_rows", [P, 32], F32)
         nc.vector.memset(qa_rows[:], 0.0)
@@ -41,22 +39,25 @@ def tile_rows_lin_elu1_norm_gate_kernel(tc, q, qa, ka, k, t, v, og, out):
         for h in range(H):
             for jj in range(2):
                 k_raw[h, jj] = sbuf("k_raw%d%d" % (h, jj), [P, 2, D], F32)
-        v_raw = [sbuf("v_raw%d" % h, [P, PACK * E], F32) for h in range(H)]
-        q_raw = sbuf("q_raw", [P, PACK, N], F32)
+        v_raw = sbuf("v_raw", [P, H, PACK * E], F32)
+        q_raw = [sbuf("q_raw%d" % x, [P, N], F32) for x in range(PACK)]
         og_raw = sbuf("og_raw", [P, H, 4, E], F32)
 
         def load_k(h, jj):
             nc.sync.dma_start(out=k_raw[h, jj][:], in_=k[h].rearrange("(p j) d -> p j d", j=PACK)[:, 2 * jj : 2 * jj + 2, :])
 
         load_k(0, 0)
+        nc.sync.dma_start(out=t_sb[:], in_=t.rearrange("(p j) o -> p (j o)", j=PACK))
+        nc.sync.dma_start(out=ka_sb[:], in_=ka)
         load_k(0, 1)
-        nc.sync.dma_start(out=v_raw[0][:], in_=v[0].rearrange("(p j) e -> p (j e)", j=PACK))
         load_k(1, 0)
         load_k(1, 1)
-        nc.sync.dma_start(out=v_raw[1][:], in_=v[1].rearrange("(p j) e -> p (j e)", j=PACK))
         q_v = q.rearrange("h (c x i) n -> x (h c) i n", x=4, i=2)
-        for x in range(PACK):
-            nc.sync.dma_start(out=q_raw[:, x, :], in_=q_v[x])
+        nc.sync.dma_start(out=q_raw[0][:], in_=q_v[0])
+        nc.sync.dma_start(out=q_raw[1][:], in_=q_v[1])
+        nc.sync.dma_start(out=v_raw[:], in_=v.rearrange("h (p j) e -> p h (j e)", j=PACK))
+        nc.sync.dma_start(out=q_raw[2][:], in_=q_v[2])
+        nc.sync.dma_start(out=q_raw[3][:], in_=q_v[3])
         qa_v = qa.rearrange("(a c x i) o -> a x c (i o)", a=2, x=4, i=2)
         for quad in range(4):
             nc.sync.dma_start(
@@ -73,19 +74,24 @@ def tile_rows_lin_elu1_norm_gate_kernel(tc, q, qa, ka, k, t, v, og, out):
             for jj in range(2):
                 k_neg[h, jj] = sbuf("k_neg%d%d" % (h, jj), [P, 2, D], F32)
                 k_exp[h, jj] = sbuf("k_exp%d%d" % (h, jj), [P, 2, D], F32)
-        v_bf = [sbuf("v_bf%d" % h, [P, E * PACK], BF16) for h in range(H)]
-        kv_codes = sbuf("kv_codes", [P, 3 * D], U32)
-        kv_scales = sbuf("kv_scales", [P, 3 * D], U8)
+        v_bf = sbuf("v_bf", [P, H, E * PACK], BF16)
+        q_neg = [sbuf("q_neg%d" % x, [P, N], F32) for x in range(PACK)]
+        q_exp = [sbuf("q_exp%d" % x, [P, N], F32) for x in range(PACK)]
+        q_phi = sbuf("q_phi", [P, PACK, N], F32)
+        q_rows = sbuf("q_rows", [P, PACK, CHUNKS[1][1]], BF16)
+        k_codes = sbuf("k_codes", [P, PACK * 3 * ROWS], U32)
+        k_scales = sbuf("k_scales", [P, PACK * 3 * ROWS], U8)
+        v_codes = sbuf("v_codes", [P, H * E], U32)
+        v_scales = sbuf("v_scales", [P, H * E], U8)
+        nc.vector.memset(k_codes[:].rearrange("p (x g c) -> p x g c", x=PACK, g=3)[:, :, 1, :], 0)
+        nc.vector.memset(k_scales[:].bitcast(U32).rearrange("p (x g c) -> p x g c", x=PACK, g=3)[:, :, 1, :], 0)
         s_bf = sbuf("s_bf", [P, E, PACK], BF16)
         s_codes = sbuf("s_codes", [P, E], U32)
         s_scales = sbuf("s_scales", [P, E], U8)
-        s_ps = [ps.tile([P, PACK, E], F32, name="s_ps%d" % h) for h in range(H)]
-        q_neg, q_exp, q_phi, q_bf, q_codes, q_scales, y_ps, gate_t, gate, rec, res = {}, {}, {}, {}, {}, {}, {}, {}, {}, {}, {}
+        s_ps = ps.tile([P, PACK, E], F32, name="s_ps")
+        q_bf, q_codes, q_scales, y_ps, gate_t, gate, rec, res = {}, {}, {}, {}, {}, {}, {}, {}
         for c, (n0, w) in enumerate(CHUNKS):
             tiles = w // P
-            q_neg[c] = sbuf("q_neg%d" % c, [P, PACK, w], F32)
-            q_exp[c] = sbuf("q_exp%d" % c, [P, PACK, w], F32)
-            q_phi[c] = sbuf("q_phi%d" % c, [P, PACK, w], F32)
             q_bf[c] = sbuf("q_bf%d" % c, [P, w * PACK], BF16)
             q_codes[c] = sbuf("q_codes%d" % c, [P, w], U32)
             q_scales[c] = sbuf("q_scales%d" % c, [P, w], U8)
@@ -114,72 +120,81 @@ def tile_rows_lin_elu1_norm_gate_kernel(tc, q, qa, ka, k, t, v, og, out):
                 in1=k_exp[h, jj][:], op0=ALU.max, op1=ALU.add,
             )
 
-        def k_weigh(h):
-            for x in range(PACK):
-                nc.vector.tensor_tensor(
-                    out=k_bf[h][:, x, :].rearrange("p (c i j) -> p c j i", i=2, j=PACK),
-                    in0=k_phi[h][:].rearrange("p j (c x i) -> p x c j i", x=PACK, i=2)[:, x],
-                    in1=w_sb[:].rearrange("p j (c x i) -> p x c j i", x=PACK, i=2)[:, x],
-                    op=ALU.mult,
-                )
-
-        def k_quant(h):
-            cols = slice(2 * D * h, 2 * D * h + D)
-            nc.vector.quantize_mx(
-                out=kv_codes[:, cols].bitcast(FP8X4), scales=kv_scales[:, cols], in_=k_bf[h][:].rearrange("p x c -> p (x c)")
+        def k_weigh(h, x):
+            nc.vector.tensor_tensor(
+                out=k_bf[h][:, x, :].rearrange("p (c i j) -> p c j i", i=2, j=PACK),
+                in0=k_phi[h][:].rearrange("p j (c x i) -> p x c j i", x=PACK, i=2)[:, x],
+                in1=w_sb[:].rearrange("p j (c x i) -> p x c j i", x=PACK, i=2)[:, x],
+                op=ALU.mult,
             )
 
-        def v_cast(h):
+        def k_quant(h, x):
+            first = ROWS * (3 * x + 2 * h)
+            cols = slice(first, first + ROWS)
+            nc.vector.quantize_mx(out=k_codes[:, cols].bitcast(FP8X4), scales=k_scales[:, cols], in_=k_bf[h][:, x, :])
+
+        def k_weigh_and_quant(h):
+            for x in range(PACK):
+                k_weigh(h, x)
+                if x > 0:
+                    k_quant(h, x - 1)
+
+        def v_cast():
             nc.scalar.copy(
-                out=v_bf[h][:].rearrange("p (c i j) -> p c j i", i=4, j=PACK),
-                in_=v_raw[h][:].rearrange("p (j c i) -> p c j i", j=PACK, i=4),
+                out=v_bf[:].rearrange("p h (c i j) -> p h c j i", i=4, j=PACK),
+                in_=v_raw[:].rearrange("p h (j c i) -> p h c j i", j=PACK, i=4),
             )
 
-        def v_quant(h):
-            cols = slice(D + E * h, D + E * (h + 1))
-            nc.vector.quantize_mx(out=kv_codes[:, cols].bitcast(FP8X4), scales=kv_scales[:, cols], in_=v_bf[h][:])
+        def v_quant():
+            nc.vector.quantize_mx(out=v_codes[:].bitcast(FP8X4), scales=v_scales[:], in_=v_bf[:].rearrange("p h c -> p (h c)"))
 
-        def state_mm(h):
-            v_cols = slice(D + E * h, D + E * (h + 1))
+        def state_mm():
             for x in range(PACK):
-                first = 2 * D * h + ROWS * (x - h)
-                k_cols = slice(first, first + P)
-                nc.tensor.matmul_mx(
-                    out=s_ps[h][:, x, :],
-                    lhsT=kv_codes[:, k_cols].bitcast(FP8X4), lhsT_scale=kv_scales[:, k_cols],
-                    rhs=kv_codes[:, v_cols].bitcast(FP8X4), rhs_scale=kv_scales[:, v_cols],
-                    start=True, stop=True,
-                )
+                for h in range(H):
+                    first = ROWS * (3 * x + h)
+                    k_cols = slice(first, first + P)
+                    v_cols = slice(E * h, E * (h + 1))
+                    nc.tensor.matmul_mx(
+                        out=s_ps[:, x, :],
+                        lhsT=k_codes[:, k_cols].bitcast(FP8X4), lhsT_scale=k_scales[:, k_cols],
+                        rhs=v_codes[:, v_cols].bitcast(FP8X4), rhs_scale=v_scales[:, v_cols],
+                        start=(h == 0), stop=(h == H - 1),
+                    )
 
-        def state_copy(h):
-            rows = slice(ROWS * h, ROWS * (h + 1))
-            nc.scalar.activation(
-                out=s_bf[rows], in_=s_ps[h][rows].rearrange("p x e -> p e x"), func=ACT.Copy, scale=1.0 / N
-            )
+        def state_copy():
+            nc.scalar.activation(out=s_bf[:], in_=s_ps[:].rearrange("p x e -> p e x"), func=ACT.Copy, scale=1.0 / N)
 
         def state_quant():
             nc.vector.quantize_mx(out=s_codes[:].bitcast(FP8X4), scales=s_scales[:], in_=s_bf[:].rearrange("p e x -> p (e x)"))
 
-        def q_view(c):
-            n0, w = CHUNKS[c]
-            return q_raw[:, :, n0 : n0 + w]
+        def q_exp_step(x):
+            nc.scalar.activation(out=q_neg[x][:], in_=q_raw[x][:], func=ACT.Relu, scale=-1.0)
+            nc.scalar.activation(out=q_exp[x][:], in_=q_neg[x][:], func=ACT.Exp, scale=-1.0)
 
-        def q_exp_step(c):
-            nc.scalar.activation(out=q_neg[c][:], in_=q_view(c), func=ACT.Relu, scale=-1.0)
-            nc.scalar.activation(out=q_exp[c][:], in_=q_neg[c][:], func=ACT.Exp, scale=-1.0)
-
-        def q_phi_step(c):
+        def q_phi_step(x, n0=0, w=N):
+            cols = slice(n0, n0 + w)
             nc.vector.scalar_tensor_tensor(
-                out=q_phi[c][:], in0=q_view(c), scalar=0.0, in1=q_exp[c][:], op0=ALU.max, op1=ALU.add
+                out=q_phi[:, x, cols], in0=q_raw[x][:, cols], scalar=0.0, in1=q_exp[x][:, cols], op0=ALU.max, op1=ALU.add
             )
 
         def q_weigh(c):
-            w = CHUNKS[c][1]
+            n0, w = CHUNKS[c]
             nc.vector.tensor_tensor(
                 out=q_bf[c][:].rearrange("p (m i x) -> p m x i", i=2, x=PACK),
-                in0=q_phi[c][:].rearrange("p x (m i) -> p m x i", i=2),
+                in0=q_phi[:, :, n0 : n0 + w].rearrange("p x (m i) -> p m x i", i=2),
                 in1=qa_cols[:, 0:PACK].unsqueeze(1).unsqueeze(3).to_broadcast([P, w // 2, PACK, 2]),
                 op=ALU.mult,
+            )
+
+        def q_weigh_scalar(c):
+            n0, w = CHUNKS[c]
+            for x in range(PACK):
+                nc.scalar.activation(out=q_rows[:, x, :], in_=q_phi[:, x, n0 : n0 + w], func=ACT.Copy, scale=qa_cols[:, x : x + 1])
+
+        def q_interleave(c):
+            nc.vector.tensor_copy(
+                out=q_bf[c][:].rearrange("p (m i x) -> p m x i", i=4, x=PACK),
+                in_=q_rows[:].rearrange("p x (m i) -> p m x i", i=4),
             )
 
         def q_quant(c):
@@ -215,62 +230,56 @@ def tile_rows_lin_elu1_norm_gate_kernel(tc, q, qa, ka, k, t, v, og, out):
                     out=res[c, h][:, r, :], in0=y_ps[c, h][:, cols], scalar=rec[c, h][:, r : r + 1],
                     in1=gate[c][:, h, cols], op0=ALU.mult, op1=ALU.mult,
                 )
-            nc.sync.dma_start(out=out[h, n0 : n0 + w, :].rearrange("(r p) e -> p r e", p=P), in_=res[c, h][:])
+            queue = nc.scalar if h == 0 else nc.sync
+            queue.dma_start(out=out[h, n0 : n0 + w, :].rearrange("(r p) e -> p r e", p=P), in_=res[c, h][:])
 
-        k_weight(0)
-        k_weight(1)
         k_min_vector(0, 0)
         k_exp_step(0, 0)
-        k_weight(2)
-        k_weight(3)
+        for j in range(PACK):
+            k_weight(j)
         k_min_vector(0, 1)
         k_exp_step(0, 1)
         k_phi_step(0, 0)
         k_phi_step(0, 1)
-        v_cast(0)
-        k_min_vector(1, 0)
+        k_min_scalar(1, 0)
         k_exp_step(1, 0)
-        k_weigh(0)
-        k_min_scalar(1, 1)
+        k_min_vector(1, 1)
         k_exp_step(1, 1)
-        k_phi_step(1, 0)
-        k_quant(0)
-        k_phi_step(1, 1)
-        v_quant(0)
-        state_mm(0)
-        v_cast(1)
-        k_weigh(1)
-        v_quant(1)
-        k_quant(1)
-        state_mm(1)
+        k_weigh_and_quant(0)
         q_exp_step(0)
+        k_phi_step(1, 0)
+        k_phi_step(1, 1)
+        k_quant(0, PACK - 1)
         q_exp_step(1)
-        state_copy(0)
-        state_copy(1)
+        v_cast()
+        k_weigh_and_quant(1)
         q_phi_step(0)
-        nc.vector.transpose(out=qa_cols[:], in_=qa_rows[:])
+        k_quant(1, PACK - 1)
+        v_quant()
+        state_mm()
+        q_exp_step(2)
+        q_exp_step(3)
+        state_copy()
         q_phi_step(1)
+        q_phi_step(2)
+        nc.vector.transpose(out=qa_cols[:], in_=qa_rows[:])
+        q_phi_step(3, *CHUNKS[0])
+        q_phi_step(3, *CHUNKS[1])
+        q_weigh_scalar(1)
+        gate_step(0)
+        gate_step(1)
         q_weigh(0)
         state_quant()
         q_quant(0)
         read_mm(0)
-        q_exp_step(2)
-        gate_step(0)
-        q_weigh(1)
-        q_phi_step(2)
-        q_quant(1)
-        read_mm(1)
-        gate_step(1)
-        gate_step(2)
+        q_interleave(1)
         recip(0, 0)
         recip(0, 1)
-        q_weigh(2)
+        q_quant(1)
+        read_mm(1)
         finish(0, 0)
+        recip(1, 0)
         finish(0, 1)
-        q_quant(2)
-        read_mm(2)
-        for c in (1, 2):
-            recip(c, 0)
-            recip(c, 1)
-            finish(c, 0)
-            finish(c, 1)
+        recip(1, 1)
+        finish(1, 0)
+        finish(1, 1)

@@ -3,7 +3,7 @@ from contextlib import ExitStack
 import concourse.mybir as mybir
 
 H, D, N, E = 2, 256, 512, 128
-FLOPS = 2 * H * (N * D * E) * 2
+FLOPS = 2 * (2 * H * N * D * E)
 
 F32 = mybir.dt.float32
 BF16 = mybir.dt.bfloat16
@@ -15,8 +15,10 @@ ALU = mybir.AluOpType
 
 P = 128
 PACK = 4
-ROWS = 64
-CHUNKS = [(0, 256), (256, 256)]
+ROWS = D // PACK
+QUAD = 32
+HALF = N // 2
+GROUPS = [(0, HALF), (HALF, P), (HALF + P, P)]
 
 
 def tile_rows_lin_elu1_norm_gate_kernel(tc, q, qa, ka, k, t, v, og, out):
@@ -29,126 +31,119 @@ def tile_rows_lin_elu1_norm_gate_kernel(tc, q, qa, ka, k, t, v, og, out):
         def sbuf(name, shape, dtype):
             return sb.tile(shape, dtype, name=name, align_bytes=64)
 
+        pieces = [("k", h, a) for h in range(H) for a in range(2)] + [("q", x) for x in range(PACK)]
+        raw, neg, expo = {}, {}, {}
+        for piece in pieces:
+            label = "".join(map(str, piece))
+            raw[piece] = sbuf("raw_" + label, [P, N], F32)
+            neg[piece] = sbuf("neg_" + label, [P, N], F32)
+            expo[piece] = sbuf("exp_" + label, [P, N], F32)
         t_sb = sbuf("t_sb", [P, PACK], F32)
         ka_sb = sbuf("ka_sb", [P, D], F32)
-
-        qa_rows = sbuf("qa_rows", [P, 32], F32)
-        nc.vector.memset(qa_rows[:], 0.0)
-
-        k_raw = {}
-        for h in range(H):
-            for jj in range(2):
-                k_raw[h, jj] = sbuf("k_raw%d%d" % (h, jj), [P, 2, D], F32)
         v_raw = sbuf("v_raw", [P, H, PACK * E], F32)
-        q_raw = [sbuf("q_raw%d" % x, [P, N], F32) for x in range(PACK)]
-        og_raw = sbuf("og_raw", [P, H, 4, E], F32)
+        qa_rows = sbuf("qa_rows", [P, QUAD], F32)
+        og_raw = sbuf("og_raw", [P, H, N // P, E], F32)
 
-        def load_k(h, jj):
-            nc.sync.dma_start(out=k_raw[h, jj][:], in_=k[h].rearrange("(p j) d -> p j d", j=PACK)[:, 2 * jj : 2 * jj + 2, :])
+        k_view = k.rearrange("h (p a j) d -> h a p (j d)", a=2, j=2)
+        q_view = q.rearrange("h (c x u) n -> x (h c) u n", x=PACK, u=2)
 
-        load_k(0, 0)
+        def load_piece(piece):
+            source = k_view[piece[1], piece[2]] if piece[0] == "k" else q_view[piece[1]]
+            nc.sync.dma_start(out=raw[piece][:], in_=source)
+
+        load_piece(("k", 0, 0))
+        load_piece(("k", 0, 1))
         nc.sync.dma_start(out=t_sb[:], in_=t.rearrange("(p j) o -> p (j o)", j=PACK))
         nc.sync.dma_start(out=ka_sb[:], in_=ka)
-        load_k(0, 1)
-        load_k(1, 0)
-        load_k(1, 1)
-        q_v = q.rearrange("h (c x i) n -> x (h c) i n", x=4, i=2)
-        nc.sync.dma_start(out=q_raw[0][:], in_=q_v[0])
-        nc.sync.dma_start(out=q_raw[1][:], in_=q_v[1])
+        load_piece(("k", 1, 0))
+        load_piece(("k", 1, 1))
+        load_piece(("q", 0))
         nc.sync.dma_start(out=v_raw[:], in_=v.rearrange("h (p j) e -> p h (j e)", j=PACK))
-        nc.sync.dma_start(out=q_raw[2][:], in_=q_v[2])
-        nc.sync.dma_start(out=q_raw[3][:], in_=q_v[3])
-        qa_v = qa.rearrange("(a c x i) o -> a x c (i o)", a=2, x=4, i=2)
-        for quad in range(4):
-            nc.sync.dma_start(
-                out=qa_rows[32 * quad : 32 * quad + 4, :].rearrange("p (c i) -> p c i", i=2), in_=qa_v[quad % 2]
-            )
-        nc.sync.dma_start(out=og_raw[:].rearrange("p h r e -> p (h r) e"), in_=og.rearrange("h (r p) e -> p (h r) e", p=P))
+        for x in range(1, PACK):
+            load_piece(("q", x))
+        nc.vector.memset(qa_rows[:], 0.0)
+        qa_view = qa.rearrange("(a c x u) o -> a x c (u o)", a=2, x=PACK, u=2)
+        for g in range(P // QUAD):
+            rows = qa_rows[QUAD * g : QUAD * g + PACK, :]
+            nc.sync.dma_start(out=rows.rearrange("p (c u) -> p c u", u=2), in_=qa_view[g % 2])
+        nc.sync.dma_start(
+            out=og_raw[:].rearrange("p h r e -> p (h r) e"), in_=og.rearrange("h (r p) e -> p (h r) e", p=P)
+        )
 
-        w_sb = sbuf("w_sb", [P, PACK, D], F32)
-        qa_cols = sbuf("qa_cols", [P, 32], F32)
-        k_neg, k_exp, k_phi, k_bf = {}, {}, {}, {}
-        for h in range(H):
-            k_phi[h] = sbuf("k_phi%d" % h, [P, PACK, D], F32)
-            k_bf[h] = sbuf("k_bf%d" % h, [P, PACK, D], BF16)
-            for jj in range(2):
-                k_neg[h, jj] = sbuf("k_neg%d%d" % (h, jj), [P, 2, D], F32)
-                k_exp[h, jj] = sbuf("k_exp%d%d" % (h, jj), [P, 2, D], F32)
+        k_weights = sbuf("k_weights", [P, PACK, D], F32)
+        k_phi = [sbuf("k_phi%d" % h, [P, PACK, D], F32) for h in range(H)]
+        k_bf = [sbuf("k_bf%d" % h, [P, PACK, D], BF16) for h in range(H)]
         v_bf = sbuf("v_bf", [P, H, E * PACK], BF16)
-        q_neg = [sbuf("q_neg%d" % x, [P, N], F32) for x in range(PACK)]
-        q_exp = [sbuf("q_exp%d" % x, [P, N], F32) for x in range(PACK)]
-        q_phi = sbuf("q_phi", [P, PACK, N], F32)
-        q_rows = sbuf("q_rows", [P, PACK, CHUNKS[1][1]], BF16)
-        k_codes = sbuf("k_codes", [P, PACK * 3 * ROWS], U32)
-        k_scales = sbuf("k_scales", [P, PACK * 3 * ROWS], U8)
         v_codes = sbuf("v_codes", [P, H * E], U32)
         v_scales = sbuf("v_scales", [P, H * E], U8)
+        k_codes = sbuf("k_codes", [P, PACK * 3 * ROWS], U32)
+        k_scales = sbuf("k_scales", [P, PACK * 3 * ROWS], U8)
         nc.vector.memset(k_codes[:].rearrange("p (x g c) -> p x g c", x=PACK, g=3)[:, :, 1, :], 0)
         nc.vector.memset(k_scales[:].bitcast(U32).rearrange("p (x g c) -> p x g c", x=PACK, g=3)[:, :, 1, :], 0)
+        s_ps = ps.tile([P, PACK, E], F32, name="s_ps")
         s_bf = sbuf("s_bf", [P, E, PACK], BF16)
         s_codes = sbuf("s_codes", [P, E], U32)
         s_scales = sbuf("s_scales", [P, E], U8)
-        s_ps = ps.tile([P, PACK, E], F32, name="s_ps")
-        q_bf, q_codes, q_scales, y_ps, gate_t, gate, rec, res = {}, {}, {}, {}, {}, {}, {}, {}
-        for c, (n0, w) in enumerate(CHUNKS):
-            tiles = w // P
-            q_bf[c] = sbuf("q_bf%d" % c, [P, w * PACK], BF16)
-            q_codes[c] = sbuf("q_codes%d" % c, [P, w], U32)
-            q_scales[c] = sbuf("q_scales%d" % c, [P, w], U8)
-            gate_t[c] = sbuf("gate_t%d" % c, [P, H, tiles * E], F32)
-            gate[c] = sbuf("gate%d" % c, [P, H, tiles * E], F32)
+
+        qa_cols = sbuf("qa_cols", [P, QUAD], F32)
+        q_phi = sbuf("q_phi", [P, PACK, N], F32)
+        q_rows = [sbuf("q_rows%d" % a, [P, PACK, HALF], BF16) for a in range(2)]
+        q_bf = [sbuf("q_bf%d" % a, [P, HALF * PACK], BF16) for a in range(2)]
+        gate_tanh = [sbuf("gate_tanh%d" % a, [P, H, HALF // P * E], F32) for a in range(2)]
+        gate = [sbuf("gate%d" % a, [P, H, HALF // P * E], F32) for a in range(2)]
+        q_codes, q_scales, y_ps, inverse, result = {}, {}, {}, {}, {}
+        for g, (first, count) in enumerate(GROUPS):
+            q_codes[g] = sbuf("q_codes%d" % g, [P, count], U32)
+            q_scales[g] = sbuf("q_scales%d" % g, [P, count], U8)
             for h in range(H):
-                y_ps[c, h] = ps.tile([P, 512], F32, name="y_ps%d%d" % (c, h))
-                rec[c, h] = sbuf("rec%d%d" % (c, h), [P, tiles], F32)
-                res[c, h] = sbuf("res%d%d" % (c, h), [P, tiles, E], F32)
+                y_ps[g, h] = ps.tile([P, count // P * E], F32, name="y_ps%d%d" % (g, h))
+                inverse[g, h] = sbuf("inverse%d%d" % (g, h), [P, count // P], F32)
+                result[g, h] = sbuf("result%d%d" % (g, h), [P, count // P, E], F32)
 
-        def k_weight(j):
-            nc.vector.tensor_scalar(out=w_sb[:, j, :], in0=ka_sb[:], scalar1=t_sb[:, j : j + 1], scalar2=None, op0=ALU.mult)
+        def neg_on_vector(piece):
+            nc.vector.tensor_scalar(
+                out=neg[piece][:], in0=raw[piece][:], scalar1=-1.0, scalar2=0.0, op0=ALU.mult, op1=ALU.max
+            )
 
-        def k_min_vector(h, jj):
-            nc.vector.tensor_scalar(out=k_neg[h, jj][:], in0=k_raw[h, jj][:], scalar1=-1.0, scalar2=0.0, op0=ALU.mult, op1=ALU.max)
+        def neg_on_scalar(piece):
+            nc.scalar.activation(out=neg[piece][:], in_=raw[piece][:], func=ACT.Relu, scale=-1.0)
 
-        def k_min_scalar(h, jj):
-            nc.scalar.activation(out=k_neg[h, jj][:], in_=k_raw[h, jj][:], func=ACT.Relu, scale=-1.0)
+        def exp_step(piece):
+            nc.scalar.activation(out=expo[piece][:], in_=neg[piece][:], func=ACT.Exp, scale=-1.0)
 
-        def k_exp_step(h, jj):
-            nc.scalar.activation(out=k_exp[h, jj][:], in_=k_neg[h, jj][:], func=ACT.Exp, scale=-1.0)
-
-        def k_phi_step(h, jj):
+        def phi_step(piece, cols=slice(0, N)):
+            if piece[0] == "k":
+                target = k_phi[piece[1]][:, 2 * piece[2] : 2 * piece[2] + 2, :].rearrange("p j d -> p (j d)")
+            else:
+                target = q_phi[:, piece[1], :]
             nc.vector.scalar_tensor_tensor(
-                out=k_phi[h][:, 2 * jj : 2 * jj + 2, :], in0=k_raw[h, jj][:], scalar=0.0,
-                in1=k_exp[h, jj][:], op0=ALU.max, op1=ALU.add,
+                out=target[:, cols], in0=raw[piece][:, cols], scalar=0.0, in1=expo[piece][:, cols],
+                op0=ALU.max, op1=ALU.add,
             )
 
-        def k_weigh(h, x):
-            nc.vector.tensor_tensor(
-                out=k_bf[h][:, x, :].rearrange("p (c i j) -> p c j i", i=2, j=PACK),
-                in0=k_phi[h][:].rearrange("p j (c x i) -> p x c j i", x=PACK, i=2)[:, x],
-                in1=w_sb[:].rearrange("p j (c x i) -> p x c j i", x=PACK, i=2)[:, x],
-                op=ALU.mult,
-            )
-
-        def k_quant(h, x):
+        def k_quantise(h, x):
             first = ROWS * (3 * x + 2 * h)
             cols = slice(first, first + ROWS)
             nc.vector.quantize_mx(out=k_codes[:, cols].bitcast(FP8X4), scales=k_scales[:, cols], in_=k_bf[h][:, x, :])
 
-        def k_weigh_and_quant(h):
+        def k_weigh(h):
             for x in range(PACK):
-                k_weigh(h, x)
+                nc.vector.tensor_tensor(
+                    out=k_bf[h][:, x, :].rearrange("p (c u j) -> p c j u", u=2, j=PACK),
+                    in0=k_phi[h][:].rearrange("p j (c x u) -> p x c j u", x=PACK, u=2)[:, x],
+                    in1=k_weights[:].rearrange("p j (c x u) -> p x c j u", x=PACK, u=2)[:, x],
+                    op=ALU.mult,
+                )
                 if x > 0:
-                    k_quant(h, x - 1)
+                    k_quantise(h, x - 1)
 
-        def v_cast():
-            nc.scalar.copy(
-                out=v_bf[:].rearrange("p h (c i j) -> p h c j i", i=4, j=PACK),
-                in_=v_raw[:].rearrange("p h (j c i) -> p h c j i", j=PACK, i=4),
+        def interleave(copy, grouped, rows):
+            copy(
+                out=grouped.rearrange("p h (c m j) -> p h c j m", m=4, j=PACK),
+                in_=rows.rearrange("p h (j c m) -> p h c j m", j=PACK, m=4),
             )
 
-        def v_quant():
-            nc.vector.quantize_mx(out=v_codes[:].bitcast(FP8X4), scales=v_scales[:], in_=v_bf[:].rearrange("p h c -> p (h c)"))
-
-        def state_mm():
+        def state_products():
             for x in range(PACK):
                 for h in range(H):
                     first = ROWS * (3 * x + h)
@@ -161,125 +156,122 @@ def tile_rows_lin_elu1_norm_gate_kernel(tc, q, qa, ka, k, t, v, og, out):
                         start=(h == 0), stop=(h == H - 1),
                     )
 
-        def state_copy():
-            nc.scalar.activation(out=s_bf[:], in_=s_ps[:].rearrange("p x e -> p e x"), func=ACT.Copy, scale=1.0 / N)
+        def half_cols(a):
+            return slice(HALF * a, HALF * (a + 1))
 
-        def state_quant():
-            nc.vector.quantize_mx(out=s_codes[:].bitcast(FP8X4), scales=s_scales[:], in_=s_bf[:].rearrange("p e x -> p (e x)"))
-
-        def q_exp_step(x):
-            nc.scalar.activation(out=q_neg[x][:], in_=q_raw[x][:], func=ACT.Relu, scale=-1.0)
-            nc.scalar.activation(out=q_exp[x][:], in_=q_neg[x][:], func=ACT.Exp, scale=-1.0)
-
-        def q_phi_step(x, n0=0, w=N):
-            cols = slice(n0, n0 + w)
-            nc.vector.scalar_tensor_tensor(
-                out=q_phi[:, x, cols], in0=q_raw[x][:, cols], scalar=0.0, in1=q_exp[x][:, cols], op0=ALU.max, op1=ALU.add
+        def q_interleave(a):
+            interleave(
+                nc.vector.tensor_copy, q_bf[a][:].unsqueeze(1), q_rows[a][:].rearrange("p x n -> p (x n)").unsqueeze(1)
             )
 
-        def q_weigh(c):
-            n0, w = CHUNKS[c]
-            nc.vector.tensor_tensor(
-                out=q_bf[c][:].rearrange("p (m i x) -> p m x i", i=2, x=PACK),
-                in0=q_phi[:, :, n0 : n0 + w].rearrange("p x (m i) -> p m x i", i=2),
-                in1=qa_cols[:, 0:PACK].unsqueeze(1).unsqueeze(3).to_broadcast([P, w // 2, PACK, 2]),
-                op=ALU.mult,
+        def q_quantise_and_read(g):
+            first, count = GROUPS[g]
+            start = first % HALF * PACK
+            nc.vector.quantize_mx(
+                out=q_codes[g][:].bitcast(FP8X4), scales=q_scales[g][:],
+                in_=q_bf[first // HALF][:, start : start + count * PACK],
             )
-
-        def q_weigh_scalar(c):
-            n0, w = CHUNKS[c]
-            for x in range(PACK):
-                nc.scalar.activation(out=q_rows[:, x, :], in_=q_phi[:, x, n0 : n0 + w], func=ACT.Copy, scale=qa_cols[:, x : x + 1])
-
-        def q_interleave(c):
-            nc.vector.tensor_copy(
-                out=q_bf[c][:].rearrange("p (m i x) -> p m x i", i=4, x=PACK),
-                in_=q_rows[:].rearrange("p x (m i) -> p m x i", i=4),
-            )
-
-        def q_quant(c):
-            nc.vector.quantize_mx(out=q_codes[c][:].bitcast(FP8X4), scales=q_scales[c][:], in_=q_bf[c][:])
-
-        def read_mm(c):
             for h in range(H):
                 rows = slice(ROWS * h, ROWS * (h + 1))
-                for r in range(CHUNKS[c][1] // P):
+                for r in range(count // P):
                     cols = slice(P * r, P * (r + 1))
                     nc.tensor.matmul_mx(
-                        out=y_ps[c, h][:, cols],
-                        lhsT=q_codes[c][rows, cols].bitcast(FP8X4), lhsT_scale=q_scales[c][rows, cols],
+                        out=y_ps[g, h][:, cols],
+                        lhsT=q_codes[g][rows, cols].bitcast(FP8X4), lhsT_scale=q_scales[g][rows, cols],
                         rhs=s_codes[rows, :].bitcast(FP8X4), rhs_scale=s_scales[rows, :],
                         start=True, stop=True,
                     )
 
-        def gate_step(c):
-            n0, w = CHUNKS[c]
-            src = og_raw[:, :, n0 // P : (n0 + w) // P, :].rearrange("p h r e -> p h (r e)")
-            nc.scalar.activation(out=gate_t[c][:], in_=src, func=ACT.Tanh, scale=0.5)
-            nc.scalar.activation(out=gate[c][:], in_=gate_t[c][:], func=ACT.Identity, scale=0.5, bias=0.5)
+        def tanh_step(a):
+            tiles = og_raw[:, :, HALF // P * a : HALF // P * (a + 1), :]
+            nc.scalar.activation(
+                out=gate_tanh[a][:], in_=tiles.rearrange("p h r e -> p h (r e)"), func=ACT.Tanh, scale=0.5
+            )
 
-        def recip(c, h):
-            w = CHUNKS[c][1]
-            nc.vector.reciprocal(out=rec[c, h][:], in_=y_ps[c, h][:, E - 1 : w : E])
+        def gate_step(a):
+            nc.scalar.activation(out=gate[a][:], in_=gate_tanh[a][:], func=ACT.Identity, scale=0.5, bias=0.5)
 
-        def finish(c, h):
-            n0, w = CHUNKS[c]
-            for r in range(w // P):
-                cols = slice(E * r, E * (r + 1))
+        def invert(g, h):
+            nc.vector.reciprocal(out=inverse[g, h][:], in_=y_ps[g, h][:, E - 1 :: E])
+
+        def finish(g, h):
+            first, count = GROUPS[g]
+            for r in range(count // P):
+                tile = first % HALF // P + r
                 nc.vector.scalar_tensor_tensor(
-                    out=res[c, h][:, r, :], in0=y_ps[c, h][:, cols], scalar=rec[c, h][:, r : r + 1],
-                    in1=gate[c][:, h, cols], op0=ALU.mult, op1=ALU.mult,
+                    out=result[g, h][:, r, :], in0=y_ps[g, h][:, E * r : E * (r + 1)],
+                    scalar=inverse[g, h][:, r : r + 1], in1=gate[first // HALF][:, h, E * tile : E * (tile + 1)],
+                    op0=ALU.mult, op1=ALU.mult,
                 )
             queue = nc.scalar if h == 0 else nc.sync
-            queue.dma_start(out=out[h, n0 : n0 + w, :].rearrange("(r p) e -> p r e", p=P), in_=res[c, h][:])
+            queue.dma_start(out=out[h, first : first + count, :].rearrange("(r p) e -> p r e", p=P), in_=result[g, h][:])
 
-        k_min_vector(0, 0)
-        k_exp_step(0, 0)
+        for a in range(2):
+            neg_on_vector(("k", 0, a))
+            exp_step(("k", 0, a))
         for j in range(PACK):
-            k_weight(j)
-        k_min_vector(0, 1)
-        k_exp_step(0, 1)
-        k_phi_step(0, 0)
-        k_phi_step(0, 1)
-        k_min_scalar(1, 0)
-        k_exp_step(1, 0)
-        k_min_vector(1, 1)
-        k_exp_step(1, 1)
-        k_weigh_and_quant(0)
-        q_exp_step(0)
-        k_phi_step(1, 0)
-        k_phi_step(1, 1)
-        k_quant(0, PACK - 1)
-        q_exp_step(1)
-        v_cast()
-        k_weigh_and_quant(1)
-        q_phi_step(0)
-        k_quant(1, PACK - 1)
-        v_quant()
-        state_mm()
-        q_exp_step(2)
-        q_exp_step(3)
-        state_copy()
-        q_phi_step(1)
-        q_phi_step(2)
+            nc.vector.tensor_scalar(
+                out=k_weights[:, j, :], in0=ka_sb[:], scalar1=t_sb[:, j : j + 1], scalar2=None, op0=ALU.mult
+            )
+        neg_on_scalar(("k", 1, 0))
+        exp_step(("k", 1, 0))
+        neg_on_scalar(("q", 0))
+        phi_step(("k", 0, 0))
+        phi_step(("k", 0, 1))
+        neg_on_vector(("k", 1, 1))
+        exp_step(("k", 1, 1))
+        interleave(nc.scalar.copy, v_bf[:], v_raw[:])
+        k_weigh(0)
+
+        phi_step(("k", 1, 0))
+        phi_step(("k", 1, 1))
+        k_quantise(0, PACK - 1)
+        nc.vector.quantize_mx(out=v_codes[:].bitcast(FP8X4), scales=v_scales[:], in_=v_bf[:].rearrange("p h c -> p (h c)"))
+        exp_step(("q", 0))
+        neg_on_scalar(("q", 1))
+        for x in range(1, PACK):
+            if x + 1 < PACK:
+                neg_on_scalar(("q", x + 1))
+            exp_step(("q", x))
+        k_weigh(1)
+        phi_step(("q", 0))
+        k_quantise(1, PACK - 1)
+
+        state_products()
+        nc.scalar.activation(out=s_bf[:], in_=s_ps[:].rearrange("p x e -> p e x"), func=ACT.Copy, scale=1.0 / N)
+        tanh_step(0)
+
+        phi_step(("q", 1))
         nc.vector.transpose(out=qa_cols[:], in_=qa_rows[:])
-        q_phi_step(3, *CHUNKS[0])
-        q_phi_step(3, *CHUNKS[1])
-        q_weigh_scalar(1)
+        phi_step(("q", 2))
+        phi_step(("q", 3), half_cols(0))
+        for x in range(PACK):
+            nc.vector.tensor_scalar(
+                out=q_rows[0][:, x, :], in0=q_phi[:, x, half_cols(0)], scalar1=qa_cols[:, x : x + 1], scalar2=None,
+                op0=ALU.mult,
+            )
+        phi_step(("q", 3), half_cols(1))
+        for x in range(PACK):
+            nc.scalar.activation(
+                out=q_rows[1][:, x, :], in_=q_phi[:, x, half_cols(1)], func=ACT.Copy, scale=qa_cols[:, x : x + 1]
+            )
+        tanh_step(1)
         gate_step(0)
         gate_step(1)
-        q_weigh(0)
-        state_quant()
-        q_quant(0)
-        read_mm(0)
+        q_interleave(0)
+        nc.vector.quantize_mx(out=s_codes[:].bitcast(FP8X4), scales=s_scales[:], in_=s_bf[:].rearrange("p e x -> p (e x)"))
+        q_quantise_and_read(0)
         q_interleave(1)
-        recip(0, 0)
-        recip(0, 1)
-        q_quant(1)
-        read_mm(1)
-        finish(0, 0)
-        recip(1, 0)
-        finish(0, 1)
-        recip(1, 1)
-        finish(1, 0)
-        finish(1, 1)
+
+        invert(0, 0)
+        q_quantise_and_read(1)
+        q_quantise_and_read(2)
+        invert(0, 1)
+        for h in range(H):
+            finish(0, h)
+        for g in (1, 2):
+            for h in range(H):
+                invert(g, h)
+        for g in (1, 2):
+            for h in range(H):
+                finish(g, h)

@@ -16,7 +16,6 @@ ALU = mybir.AluOpType
 P = 128
 PACK = 4
 ROWS = D // PACK
-QUAD = 32
 HALF = N // 2
 GROUPS = [(0, HALF), (HALF, P), (HALF + P, P)]
 
@@ -31,47 +30,44 @@ def tile_rows_lin_elu1_norm_gate_kernel(tc, q, qa, ka, k, t, v, og, out):
         def sbuf(name, shape, dtype):
             return sb.tile(shape, dtype, name=name, align_bytes=64)
 
-        pieces = [("k", h, a) for h in range(H) for a in range(2)] + [("q", x) for x in range(PACK)]
-        raw, neg, expo = {}, {}, {}
-        for piece in pieces:
-            label = "".join(map(str, piece))
-            raw[piece] = sbuf("raw_" + label, [P, N], F32)
-            neg[piece] = sbuf("neg_" + label, [P, N], F32)
-            expo[piece] = sbuf("exp_" + label, [P, N], F32)
+        k_raw = [sbuf("k_raw%d" % h, [P, PACK * D], F32) for h in range(H)]
+        q_raw = sbuf("q_raw", [P, PACK * N], F32)
         t_sb = sbuf("t_sb", [P, PACK], F32)
         ka_sb = sbuf("ka_sb", [P, D], F32)
         v_raw = sbuf("v_raw", [P, H, PACK * E], F32)
-        qa_rows = sbuf("qa_rows", [P, QUAD], F32)
+        qa_sb = sbuf("qa_sb", [P, 2 * PACK], F32)
         og_raw = sbuf("og_raw", [P, H, N // P, E], F32)
+
+        def piece(a):
+            return slice(2 * D * a, 2 * D * (a + 1))
+
+        def place(x):
+            return slice(N * x, N * (x + 1))
 
         k_view = k.rearrange("h (p a j) d -> h a p (j d)", a=2, j=2)
         q_view = q.rearrange("h (c x u) n -> x (h c) u n", x=PACK, u=2)
-
-        def load_piece(piece):
-            source = k_view[piece[1], piece[2]] if piece[0] == "k" else q_view[piece[1]]
-            nc.sync.dma_start(out=raw[piece][:], in_=source)
-
-        load_piece(("k", 0, 0))
-        load_piece(("k", 0, 1))
-        nc.sync.dma_start(out=t_sb[:], in_=t.rearrange("(p j) o -> p (j o)", j=PACK))
+        nc.sync.dma_start(out=k_raw[0][:, piece(0)], in_=k_view[0, 0])
         nc.sync.dma_start(out=ka_sb[:], in_=ka)
-        load_piece(("k", 1, 0))
-        load_piece(("k", 1, 1))
-        load_piece(("q", 0))
+        nc.sync.dma_start(out=t_sb[:], in_=t.rearrange("(p j) o -> p (j o)", j=PACK))
+        nc.sync.dma_start(out=k_raw[0][:, piece(1)], in_=k_view[0, 1])
+        for a in range(2):
+            nc.sync.dma_start(out=k_raw[1][:, piece(a)], in_=k_view[1, a])
         nc.sync.dma_start(out=v_raw[:], in_=v.rearrange("h (p j) e -> p h (j e)", j=PACK))
-        for x in range(1, PACK):
-            load_piece(("q", x))
-        nc.vector.memset(qa_rows[:], 0.0)
-        qa_view = qa.rearrange("(a c x u) o -> a x c (u o)", a=2, x=PACK, u=2)
-        for g in range(P // QUAD):
-            rows = qa_rows[QUAD * g : QUAD * g + PACK, :]
-            nc.sync.dma_start(out=rows.rearrange("p (c u) -> p c u", u=2), in_=qa_view[g % 2])
+        for x in range(PACK):
+            nc.sync.dma_start(out=q_raw[:, place(x)], in_=q_view[x])
+        qa_view = qa.rearrange("(c m) o -> c (m o)", m=2 * PACK)
+        for u in range(2):
+            nc.sync.dma_start(
+                out=qa_sb[u::2, 0 : 2 * PACK - 1], in_=qa_view[:, u : u + 2 * PACK - 1].partition_broadcast(H)
+            )
         nc.sync.dma_start(
             out=og_raw[:].rearrange("p h r e -> p (h r) e"), in_=og.rearrange("h (r p) e -> p (h r) e", p=P)
         )
 
         k_weights = sbuf("k_weights", [P, PACK, D], F32)
-        k_phi = [sbuf("k_phi%d" % h, [P, PACK, D], F32) for h in range(H)]
+        k_exp = [sbuf("k_exp%d" % h, [P, PACK * D], F32) for h in range(H)]
+        k_pos = [sbuf("k_pos%d" % h, [P, PACK * D], F32) for h in range(H)]
+        k_phi = [sbuf("k_phi%d" % h, [P, PACK * D], F32) for h in range(H)]
         k_bf = [sbuf("k_bf%d" % h, [P, PACK, D], BF16) for h in range(H)]
         v_bf = sbuf("v_bf", [P, H, E * PACK], BF16)
         v_codes = sbuf("v_codes", [P, H * E], U32)
@@ -85,14 +81,14 @@ def tile_rows_lin_elu1_norm_gate_kernel(tc, q, qa, ka, k, t, v, og, out):
         s_codes = sbuf("s_codes", [P, E], U32)
         s_scales = sbuf("s_scales", [P, E], U8)
 
-        qa_cols = sbuf("qa_cols", [P, QUAD], F32)
-        q_phi = sbuf("q_phi", [P, PACK, N], F32)
-        q_rows = [sbuf("q_rows%d" % a, [P, PACK, HALF], BF16) for a in range(2)]
-        q_bf = [sbuf("q_bf%d" % a, [P, HALF * PACK], BF16) for a in range(2)]
+        q_exp = sbuf("q_exp", [P, PACK * N], F32)
+        q_pos = sbuf("q_pos", [P, PACK * N], F32)
+        q_low = sbuf("q_low", [P, PACK * N], F32)
         gate_tanh = [sbuf("gate_tanh%d" % a, [P, H, HALF // P * E], F32) for a in range(2)]
         gate = [sbuf("gate%d" % a, [P, H, HALF // P * E], F32) for a in range(2)]
-        q_codes, q_scales, y_ps, inverse, result = {}, {}, {}, {}, {}
+        q_bf, q_codes, q_scales, y_ps, inverse, result = {}, {}, {}, {}, {}, {}
         for g, (first, count) in enumerate(GROUPS):
+            q_bf[g] = sbuf("q_bf%d" % g, [P, count * PACK], BF16)
             q_codes[g] = sbuf("q_codes%d" % g, [P, count], U32)
             q_scales[g] = sbuf("q_scales%d" % g, [P, count], U8)
             for h in range(H):
@@ -100,25 +96,21 @@ def tile_rows_lin_elu1_norm_gate_kernel(tc, q, qa, ka, k, t, v, og, out):
                 inverse[g, h] = sbuf("inverse%d%d" % (g, h), [P, count // P], F32)
                 result[g, h] = sbuf("result%d%d" % (g, h), [P, count // P, E], F32)
 
-        def neg_on_vector(piece):
+        def k_exp_step(h, a):
+            nc.scalar.activation(out=k_exp[h][:, piece(a)], in_=k_raw[h][:, piece(a)], func=ACT.Exp)
+
+        def k_pos_on_vector(h, a):
             nc.vector.tensor_scalar(
-                out=neg[piece][:], in0=raw[piece][:], scalar1=-1.0, scalar2=0.0, op0=ALU.mult, op1=ALU.max
+                out=k_pos[h][:, piece(a)], in0=k_raw[h][:, piece(a)], scalar1=0.0, scalar2=None, op0=ALU.max
             )
 
-        def neg_on_scalar(piece):
-            nc.scalar.activation(out=neg[piece][:], in_=raw[piece][:], func=ACT.Relu, scale=-1.0)
+        def k_pos_on_scalar(h, a):
+            nc.scalar.activation(out=k_pos[h][:, piece(a)], in_=k_raw[h][:, piece(a)], func=ACT.Relu)
 
-        def exp_step(piece):
-            nc.scalar.activation(out=expo[piece][:], in_=neg[piece][:], func=ACT.Exp, scale=-1.0)
-
-        def phi_step(piece, cols=slice(0, N)):
-            if piece[0] == "k":
-                target = k_phi[piece[1]][:, 2 * piece[2] : 2 * piece[2] + 2, :].rearrange("p j d -> p (j d)")
-            else:
-                target = q_phi[:, piece[1], :]
+        def k_phi_step(h, a):
             nc.vector.scalar_tensor_tensor(
-                out=target[:, cols], in0=raw[piece][:, cols], scalar=0.0, in1=expo[piece][:, cols],
-                op0=ALU.max, op1=ALU.add,
+                out=k_phi[h][:, piece(a)], in0=k_exp[h][:, piece(a)], scalar=1.0, in1=k_pos[h][:, piece(a)],
+                op0=ALU.min, op1=ALU.add,
             )
 
         def k_quantise(h, x):
@@ -130,18 +122,12 @@ def tile_rows_lin_elu1_norm_gate_kernel(tc, q, qa, ka, k, t, v, og, out):
             for x in range(PACK):
                 nc.vector.tensor_tensor(
                     out=k_bf[h][:, x, :].rearrange("p (c u j) -> p c j u", u=2, j=PACK),
-                    in0=k_phi[h][:].rearrange("p j (c x u) -> p x c j u", x=PACK, u=2)[:, x],
+                    in0=k_phi[h][:].rearrange("p (j c x u) -> p x c j u", j=PACK, x=PACK, u=2)[:, x],
                     in1=k_weights[:].rearrange("p j (c x u) -> p x c j u", x=PACK, u=2)[:, x],
                     op=ALU.mult,
                 )
                 if x > 0:
                     k_quantise(h, x - 1)
-
-        def interleave(copy, grouped, rows):
-            copy(
-                out=grouped.rearrange("p h (c m j) -> p h c j m", m=4, j=PACK),
-                in_=rows.rearrange("p h (j c m) -> p h c j m", j=PACK, m=4),
-            )
 
         def state_products():
             for x in range(PACK):
@@ -156,21 +142,36 @@ def tile_rows_lin_elu1_norm_gate_kernel(tc, q, qa, ka, k, t, v, og, out):
                         start=(h == 0), stop=(h == H - 1),
                     )
 
-        def half_cols(a):
-            return slice(HALF * a, HALF * (a + 1))
+        def q_exp_step(x):
+            nc.scalar.activation(out=q_exp[:, place(x)], in_=q_raw[:, place(x)], func=ACT.Exp)
 
-        def q_interleave(a):
-            interleave(
-                nc.vector.tensor_copy, q_bf[a][:].unsqueeze(1), q_rows[a][:].rearrange("p x n -> p (x n)").unsqueeze(1)
+        def q_pos_step(x):
+            nc.vector.tensor_scalar(
+                out=q_pos[:, place(x)], in0=q_raw[:, place(x)], scalar1=0.0, scalar2=qa_sb[:, 2 * x : 2 * x + 1],
+                op0=ALU.max, op1=ALU.mult,
+            )
+
+        def q_low_step(x):
+            nc.vector.tensor_scalar(
+                out=q_low[:, place(x)], in0=q_exp[:, place(x)], scalar1=1.0, scalar2=qa_sb[:, 2 * x : 2 * x + 1],
+                op0=ALU.min, op1=ALU.mult,
+            )
+
+        def q_join(g):
+            first, count = GROUPS[g]
+
+            def pairs(terms):
+                rows = terms[:].rearrange("p (x n) -> p x n", x=PACK)[:, :, first : first + count]
+                return rows.rearrange("p x (c u) -> p c x u", u=2)
+
+            nc.vector.tensor_tensor(
+                out=q_bf[g][:].rearrange("p (c u x) -> p c x u", u=2, x=PACK), in0=pairs(q_pos), in1=pairs(q_low),
+                op=ALU.add,
             )
 
         def q_quantise_and_read(g):
             first, count = GROUPS[g]
-            start = first % HALF * PACK
-            nc.vector.quantize_mx(
-                out=q_codes[g][:].bitcast(FP8X4), scales=q_scales[g][:],
-                in_=q_bf[first // HALF][:, start : start + count * PACK],
-            )
+            nc.vector.quantize_mx(out=q_codes[g][:].bitcast(FP8X4), scales=q_scales[g][:], in_=q_bf[g][:])
             for h in range(H):
                 rows = slice(ROWS * h, ROWS * (h + 1))
                 for r in range(count // P):
@@ -206,67 +207,56 @@ def tile_rows_lin_elu1_norm_gate_kernel(tc, q, qa, ka, k, t, v, og, out):
             queue = nc.scalar if h == 0 else nc.sync
             queue.dma_start(out=out[h, first : first + count, :].rearrange("(r p) e -> p r e", p=P), in_=result[g, h][:])
 
-        for a in range(2):
-            neg_on_vector(("k", 0, a))
-            exp_step(("k", 0, a))
+        k_exp_step(0, 0)
+        k_exp_step(0, 1)
+        k_exp_step(1, 0)
+        k_exp_step(1, 1)
+        k_pos_on_scalar(1, 1)
+        nc.scalar.copy(
+            out=v_bf[:].rearrange("p h (c m j) -> p h c j m", m=4, j=PACK),
+            in_=v_raw[:].rearrange("p h (j c m) -> p h c j m", j=PACK, m=4),
+        )
+        for x in range(PACK):
+            q_exp_step(x)
+
+        k_pos_on_vector(0, 0)
         for j in range(PACK):
             nc.vector.tensor_scalar(
                 out=k_weights[:, j, :], in0=ka_sb[:], scalar1=t_sb[:, j : j + 1], scalar2=None, op0=ALU.mult
             )
-        neg_on_scalar(("k", 1, 0))
-        exp_step(("k", 1, 0))
-        neg_on_scalar(("q", 0))
-        phi_step(("k", 0, 0))
-        phi_step(("k", 0, 1))
-        neg_on_vector(("k", 1, 1))
-        exp_step(("k", 1, 1))
-        interleave(nc.scalar.copy, v_bf[:], v_raw[:])
+        k_pos_on_vector(0, 1)
+        k_phi_step(0, 0)
+        k_phi_step(0, 1)
+        k_pos_on_vector(1, 0)
         k_weigh(0)
-
-        phi_step(("k", 1, 0))
-        phi_step(("k", 1, 1))
+        k_phi_step(1, 0)
         k_quantise(0, PACK - 1)
+        k_phi_step(1, 1)
         nc.vector.quantize_mx(out=v_codes[:].bitcast(FP8X4), scales=v_scales[:], in_=v_bf[:].rearrange("p h c -> p (h c)"))
-        exp_step(("q", 0))
-        neg_on_scalar(("q", 1))
-        for x in range(1, PACK):
-            if x + 1 < PACK:
-                neg_on_scalar(("q", x + 1))
-            exp_step(("q", x))
         k_weigh(1)
-        phi_step(("q", 0))
+        q_pos_step(0)
         k_quantise(1, PACK - 1)
 
         state_products()
-        nc.scalar.activation(out=s_bf[:], in_=s_ps[:].rearrange("p x e -> p e x"), func=ACT.Copy, scale=1.0 / N)
         tanh_step(0)
-
-        phi_step(("q", 1))
-        nc.vector.transpose(out=qa_cols[:], in_=qa_rows[:])
-        phi_step(("q", 2))
-        phi_step(("q", 3), half_cols(0))
-        for x in range(PACK):
-            nc.vector.tensor_scalar(
-                out=q_rows[0][:, x, :], in0=q_phi[:, x, half_cols(0)], scalar1=qa_cols[:, x : x + 1], scalar2=None,
-                op0=ALU.mult,
-            )
-        phi_step(("q", 3), half_cols(1))
-        for x in range(PACK):
-            nc.scalar.activation(
-                out=q_rows[1][:, x, :], in_=q_phi[:, x, half_cols(1)], func=ACT.Copy, scale=qa_cols[:, x : x + 1]
-            )
+        nc.scalar.activation(out=s_bf[:], in_=s_ps[:].rearrange("p x e -> p e x"), func=ACT.Copy, scale=1.0 / N)
         tanh_step(1)
         gate_step(0)
         gate_step(1)
-        q_interleave(0)
-        nc.vector.quantize_mx(out=s_codes[:].bitcast(FP8X4), scales=s_scales[:], in_=s_bf[:].rearrange("p e x -> p (e x)"))
-        q_quantise_and_read(0)
-        q_interleave(1)
 
-        invert(0, 0)
+        for x in range(PACK):
+            q_low_step(x)
+        for x in range(1, PACK):
+            q_pos_step(x)
+        nc.vector.quantize_mx(out=s_codes[:].bitcast(FP8X4), scales=s_scales[:], in_=s_bf[:].rearrange("p e x -> p (e x)"))
+        q_join(0)
+        q_join(1)
+        q_quantise_and_read(0)
+        q_join(2)
         q_quantise_and_read(1)
-        q_quantise_and_read(2)
+        invert(0, 0)
         invert(0, 1)
+        q_quantise_and_read(2)
         for h in range(H):
             finish(0, h)
         for g in (1, 2):

@@ -46,20 +46,22 @@ def tile_rows_lin_elu1_norm_gate_kernel(tc, q, qa, ka, k, t, v, og, out):
 
         k_view = k.rearrange("h (p a j) d -> h a p (j d)", a=2, j=2)
         q_view = q.rearrange("h (c x u) n -> x (h c) u n", x=PACK, u=2)
-        nc.sync.dma_start(out=k_raw[0][:, piece(0)], in_=k_view[0, 0])
+        for a in range(2):
+            nc.sync.dma_start(out=k_raw[0][:, piece(a)], in_=k_view[0, a])
         nc.sync.dma_start(out=ka_sb[:], in_=ka)
         nc.sync.dma_start(out=t_sb[:], in_=t.rearrange("(p j) o -> p (j o)", j=PACK))
-        nc.sync.dma_start(out=k_raw[0][:, piece(1)], in_=k_view[0, 1])
-        for a in range(2):
-            nc.sync.dma_start(out=k_raw[1][:, piece(a)], in_=k_view[1, a])
-        nc.sync.dma_start(out=v_raw[:], in_=v.rearrange("h (p j) e -> p h (j e)", j=PACK))
-        for x in range(PACK):
-            nc.sync.dma_start(out=q_raw[:, place(x)], in_=q_view[x])
         qa_view = qa.rearrange("(c m) o -> c (m o)", m=2 * PACK)
         for u in range(2):
             nc.sync.dma_start(
                 out=qa_sb[u::2, 0 : 2 * PACK - 1], in_=qa_view[:, u : u + 2 * PACK - 1].partition_broadcast(H)
             )
+        for x in range(2):
+            nc.sync.dma_start(out=q_raw[:, place(x)], in_=q_view[x])
+        for a in range(2):
+            nc.sync.dma_start(out=k_raw[1][:, piece(a)], in_=k_view[1, a])
+        nc.sync.dma_start(out=v_raw[:], in_=v.rearrange("h (p j) e -> p h (j e)", j=PACK))
+        for x in range(2, PACK):
+            nc.sync.dma_start(out=q_raw[:, place(x)], in_=q_view[x])
         nc.sync.dma_start(
             out=og_raw[:].rearrange("p h r e -> p (h r) e"), in_=og.rearrange("h (r p) e -> p (h r) e", p=P)
         )
@@ -84,6 +86,7 @@ def tile_rows_lin_elu1_norm_gate_kernel(tc, q, qa, ka, k, t, v, og, out):
         q_exp = sbuf("q_exp", [P, PACK * N], F32)
         q_pos = sbuf("q_pos", [P, PACK * N], F32)
         q_low = sbuf("q_low", [P, PACK * N], F32)
+        q_relu = sbuf("q_relu", [P, N], F32)
         gate_tanh = [sbuf("gate_tanh%d" % a, [P, H, HALF // P * E], F32) for a in range(2)]
         gate = [sbuf("gate%d" % a, [P, H, HALF // P * E], F32) for a in range(2)]
         q_bf, q_codes, q_scales, y_ps, inverse, result = {}, {}, {}, {}, {}, {}
@@ -118,29 +121,24 @@ def tile_rows_lin_elu1_norm_gate_kernel(tc, q, qa, ka, k, t, v, og, out):
             cols = slice(first, first + ROWS)
             nc.vector.quantize_mx(out=k_codes[:, cols].bitcast(FP8X4), scales=k_scales[:, cols], in_=k_bf[h][:, x, :])
 
-        def k_weigh(h):
-            for x in range(PACK):
-                nc.vector.tensor_tensor(
-                    out=k_bf[h][:, x, :].rearrange("p (c u j) -> p c j u", u=2, j=PACK),
-                    in0=k_phi[h][:].rearrange("p (j c x u) -> p x c j u", j=PACK, x=PACK, u=2)[:, x],
-                    in1=k_weights[:].rearrange("p j (c x u) -> p x c j u", x=PACK, u=2)[:, x],
-                    op=ALU.mult,
-                )
-                if x > 0:
-                    k_quantise(h, x - 1)
+        def k_weigh(h, x):
+            nc.vector.tensor_tensor(
+                out=k_bf[h][:, x, :].rearrange("p (c u j) -> p c j u", u=2, j=PACK),
+                in0=k_phi[h][:].rearrange("p (j c x u) -> p x c j u", j=PACK, x=PACK, u=2)[:, x],
+                in1=k_weights[:].rearrange("p j (c x u) -> p x c j u", x=PACK, u=2)[:, x],
+                op=ALU.mult,
+            )
 
-        def state_products():
-            for x in range(PACK):
-                for h in range(H):
-                    first = ROWS * (3 * x + h)
-                    k_cols = slice(first, first + P)
-                    v_cols = slice(E * h, E * (h + 1))
-                    nc.tensor.matmul_mx(
-                        out=s_ps[:, x, :],
-                        lhsT=k_codes[:, k_cols].bitcast(FP8X4), lhsT_scale=k_scales[:, k_cols],
-                        rhs=v_codes[:, v_cols].bitcast(FP8X4), rhs_scale=v_scales[:, v_cols],
-                        start=(h == 0), stop=(h == H - 1),
-                    )
+        def state_product(h, x):
+            first = ROWS * (3 * x + h)
+            k_cols = slice(first, first + P)
+            v_cols = slice(E * h, E * (h + 1))
+            nc.tensor.matmul_mx(
+                out=s_ps[:, x, :],
+                lhsT=k_codes[:, k_cols].bitcast(FP8X4), lhsT_scale=k_scales[:, k_cols],
+                rhs=v_codes[:, v_cols].bitcast(FP8X4), rhs_scale=v_scales[:, v_cols],
+                start=(h == 0 and x == 0), stop=(h == H - 1 and x == PACK - 1),
+            )
 
         def q_exp_step(x):
             nc.scalar.activation(out=q_exp[:, place(x)], in_=q_raw[:, place(x)], func=ACT.Exp)
@@ -151,9 +149,18 @@ def tile_rows_lin_elu1_norm_gate_kernel(tc, q, qa, ka, k, t, v, og, out):
                 op0=ALU.max, op1=ALU.mult,
             )
 
-        def q_low_step(x):
+        def q_pos_on_scalar(x):
+            nc.scalar.activation(out=q_relu[:], in_=q_raw[:, place(x)], func=ACT.Relu)
+
+        def q_pos_weigh_on_scalar(x):
+            nc.scalar.activation(
+                out=q_pos[:, place(x)], in_=q_relu[:], func=ACT.Copy, scale=qa_sb[:, 2 * x : 2 * x + 1]
+            )
+
+        def q_low_step(x, first=0, count=N):
+            cols = slice(N * x + first, N * x + first + count)
             nc.vector.tensor_scalar(
-                out=q_low[:, place(x)], in0=q_exp[:, place(x)], scalar1=1.0, scalar2=qa_sb[:, 2 * x : 2 * x + 1],
+                out=q_low[:, cols], in0=q_exp[:, cols], scalar1=1.0, scalar2=qa_sb[:, 2 * x : 2 * x + 1],
                 op0=ALU.min, op1=ALU.mult,
             )
 
@@ -209,52 +216,71 @@ def tile_rows_lin_elu1_norm_gate_kernel(tc, q, qa, ka, k, t, v, og, out):
 
         k_exp_step(0, 0)
         k_exp_step(0, 1)
+        for j in range(PACK):
+            nc.scalar.activation(out=k_weights[:, j, :], in_=ka_sb[:], func=ACT.Copy, scale=t_sb[:, j : j + 1])
+        q_exp_step(0)
         k_exp_step(1, 0)
+        k_pos_on_scalar(1, 0)
         k_exp_step(1, 1)
-        k_pos_on_scalar(1, 1)
         nc.scalar.copy(
             out=v_bf[:].rearrange("p h (c m j) -> p h c j m", m=4, j=PACK),
             in_=v_raw[:].rearrange("p h (j c m) -> p h c j m", j=PACK, m=4),
         )
-        for x in range(PACK):
+        for x in range(1, PACK - 1):
             q_exp_step(x)
+        q_pos_on_scalar(PACK - 1)
+        q_exp_step(PACK - 1)
+        q_pos_weigh_on_scalar(PACK - 1)
 
         k_pos_on_vector(0, 0)
-        for j in range(PACK):
-            nc.vector.tensor_scalar(
-                out=k_weights[:, j, :], in0=ka_sb[:], scalar1=t_sb[:, j : j + 1], scalar2=None, op0=ALU.mult
-            )
         k_pos_on_vector(0, 1)
         k_phi_step(0, 0)
         k_phi_step(0, 1)
-        k_pos_on_vector(1, 0)
-        k_weigh(0)
-        k_phi_step(1, 0)
-        k_quantise(0, PACK - 1)
-        k_phi_step(1, 1)
-        nc.vector.quantize_mx(out=v_codes[:].bitcast(FP8X4), scales=v_scales[:], in_=v_bf[:].rearrange("p h c -> p (h c)"))
-        k_weigh(1)
         q_pos_step(0)
+        q_pos_step(1)
+        for x in range(PACK):
+            k_weigh(0, x)
+            if x > 0:
+                k_quantise(0, x - 1)
+        k_pos_on_vector(1, 1)
+        k_quantise(0, PACK - 1)
+        q_low_step(0)
+        k_phi_step(1, 0)
+        k_phi_step(1, 1)
+        q_pos_step(2)
+        for x in range(PACK):
+            k_weigh(1, x)
+            if x == 1:
+                nc.vector.quantize_mx(
+                    out=v_codes[:].bitcast(FP8X4), scales=v_scales[:], in_=v_bf[:].rearrange("p h c -> p (h c)")
+                )
+                for y in range(PACK):
+                    state_product(0, y)
+            if x > 0:
+                k_quantise(1, x - 1)
+                state_product(1, x - 1)
+        q_low_step(1, 0, HALF)
+        q_low_step(2, 0, HALF)
         k_quantise(1, PACK - 1)
+        state_product(1, PACK - 1)
 
-        state_products()
-        tanh_step(0)
         nc.scalar.activation(out=s_bf[:], in_=s_ps[:].rearrange("p x e -> p e x"), func=ACT.Copy, scale=1.0 / N)
+        tanh_step(0)
         tanh_step(1)
         gate_step(0)
         gate_step(1)
 
-        for x in range(PACK):
-            q_low_step(x)
-        for x in range(1, PACK):
-            q_pos_step(x)
-        nc.vector.quantize_mx(out=s_codes[:].bitcast(FP8X4), scales=s_scales[:], in_=s_bf[:].rearrange("p e x -> p (e x)"))
+        q_low_step(3, 0, HALF)
+        q_low_step(1, HALF, HALF)
+        q_low_step(2, HALF, HALF)
         q_join(0)
-        q_join(1)
+        q_low_step(3, HALF, HALF)
+        nc.vector.quantize_mx(out=s_codes[:].bitcast(FP8X4), scales=s_scales[:], in_=s_bf[:].rearrange("p e x -> p (e x)"))
         q_quantise_and_read(0)
+        q_join(1)
         q_join(2)
-        q_quantise_and_read(1)
         invert(0, 0)
+        q_quantise_and_read(1)
         invert(0, 1)
         q_quantise_and_read(2)
         for h in range(H):

@@ -46,15 +46,16 @@ def tile_rows_lin_elu1_norm_gate_kernel(tc, q, qa, ka, k, t, v, og, out):
 
         k_view = k.rearrange("h (p a j) d -> h a p (j d)", a=2, j=2)
         q_view = q.rearrange("h (c x u) n -> x (h c) u n", x=PACK, u=2)
+        nc.gpsimd.dma_start(out=t_sb[:], in_=t.rearrange("(p j) o -> p (j o)", j=PACK))
         for a in range(2):
             nc.sync.dma_start(out=k_raw[0][:, piece(a)], in_=k_view[0, a])
         nc.sync.dma_start(out=ka_sb[:], in_=ka)
-        nc.sync.dma_start(out=t_sb[:], in_=t.rearrange("(p j) o -> p (j o)", j=PACK))
         qa_view = qa.rearrange("(c m) o -> c (m o)", m=2 * PACK)
-        for u in range(2):
-            nc.sync.dma_start(
-                out=qa_sb[u::2, 0 : 2 * PACK - 1], in_=qa_view[:, u : u + 2 * PACK - 1].partition_broadcast(H)
-            )
+        for h in range(H):
+            for u in range(2):
+                nc.sync.dma_start(
+                    out=qa_sb[ROWS * h + u : ROWS * (h + 1) : 2, 0 : 2 * PACK - 1], in_=qa_view[:, u : u + 2 * PACK - 1]
+                )
         for x in range(2):
             nc.sync.dma_start(out=q_raw[:, place(x)], in_=q_view[x])
         for a in range(2):

@@ -46,23 +46,21 @@ def tile_rows_lin_elu1_norm_gate_kernel(tc, q, qa, ka, k, t, v, og, out):
 
         k_view = k.rearrange("h (p a j) d -> h a p (j d)", a=2, j=2)
         q_view = q.rearrange("h (c x u) n -> x (h c) u n", x=PACK, u=2)
-        nc.gpsimd.dma_start(out=t_sb[:], in_=t.rearrange("(p j) o -> p (j o)", j=PACK))
         for a in range(2):
             nc.sync.dma_start(out=k_raw[0][:, piece(a)], in_=k_view[0, a])
         nc.sync.dma_start(out=ka_sb[:], in_=ka)
+        nc.sync.dma_start(out=t_sb[:], in_=t.rearrange("(p j) o -> p (j o)", j=PACK))
+        for a in range(2):
+            nc.sync.dma_start(out=k_raw[1][:, piece(a)], in_=k_view[1, a])
+        nc.sync.dma_start(out=v_raw[:], in_=v.rearrange("h (p j) e -> p h (j e)", j=PACK))
+        for x in range(PACK):
+            nc.sync.dma_start(out=q_raw[:, place(x)], in_=q_view[x])
         qa_view = qa.rearrange("(c m) o -> c (m o)", m=2 * PACK)
         for h in range(H):
             for u in range(2):
                 nc.sync.dma_start(
                     out=qa_sb[ROWS * h + u : ROWS * (h + 1) : 2, 0 : 2 * PACK - 1], in_=qa_view[:, u : u + 2 * PACK - 1]
                 )
-        for x in range(2):
-            nc.sync.dma_start(out=q_raw[:, place(x)], in_=q_view[x])
-        for a in range(2):
-            nc.sync.dma_start(out=k_raw[1][:, piece(a)], in_=k_view[1, a])
-        nc.sync.dma_start(out=v_raw[:], in_=v.rearrange("h (p j) e -> p h (j e)", j=PACK))
-        for x in range(2, PACK):
-            nc.sync.dma_start(out=q_raw[:, place(x)], in_=q_view[x])
         nc.sync.dma_start(
             out=og_raw[:].rearrange("p h r e -> p (h r) e"), in_=og.rearrange("h (r p) e -> p (h r) e", p=P)
         )
@@ -87,7 +85,7 @@ def tile_rows_lin_elu1_norm_gate_kernel(tc, q, qa, ka, k, t, v, og, out):
         q_exp = sbuf("q_exp", [P, PACK * N], F32)
         q_pos = sbuf("q_pos", [P, PACK * N], F32)
         q_low = sbuf("q_low", [P, PACK * N], F32)
-        q_relu = sbuf("q_relu", [P, N], F32)
+        q_relu = sbuf("q_relu", [P, PACK * N], F32)
         gate_tanh = [sbuf("gate_tanh%d" % a, [P, H, HALF // P * E], F32) for a in range(2)]
         gate = [sbuf("gate%d" % a, [P, H, HALF // P * E], F32) for a in range(2)]
         q_bf, q_codes, q_scales, y_ps, inverse, result = {}, {}, {}, {}, {}, {}
@@ -144,18 +142,22 @@ def tile_rows_lin_elu1_norm_gate_kernel(tc, q, qa, ka, k, t, v, og, out):
         def q_exp_step(x):
             nc.scalar.activation(out=q_exp[:, place(x)], in_=q_raw[:, place(x)], func=ACT.Exp)
 
-        def q_pos_step(x):
+        def q_pos_step(x, first=0, count=N):
+            cols = slice(N * x + first, N * x + first + count)
             nc.vector.tensor_scalar(
-                out=q_pos[:, place(x)], in0=q_raw[:, place(x)], scalar1=0.0, scalar2=qa_sb[:, 2 * x : 2 * x + 1],
+                out=q_pos[:, cols], in0=q_raw[:, cols], scalar1=0.0, scalar2=qa_sb[:, 2 * x : 2 * x + 1],
                 op0=ALU.max, op1=ALU.mult,
             )
 
-        def q_pos_on_scalar(x):
-            nc.scalar.activation(out=q_relu[:], in_=q_raw[:, place(x)], func=ACT.Relu)
+        def q_cols(x, a):
+            return slice(N * x + HALF * a, N * x + HALF * (a + 1))
 
-        def q_pos_weigh_on_scalar(x):
+        def q_relu_on_scalar(x, a):
+            nc.scalar.activation(out=q_relu[:, q_cols(x, a)], in_=q_raw[:, q_cols(x, a)], func=ACT.Relu)
+
+        def q_pos_on_scalar(x, a):
             nc.scalar.activation(
-                out=q_pos[:, place(x)], in_=q_relu[:], func=ACT.Copy, scale=qa_sb[:, 2 * x : 2 * x + 1]
+                out=q_pos[:, q_cols(x, a)], in_=q_relu[:, q_cols(x, a)], func=ACT.Copy, scale=qa_sb[:, 2 * x : 2 * x + 1]
             )
 
         def q_low_step(x, first=0, count=N):
@@ -219,49 +221,43 @@ def tile_rows_lin_elu1_norm_gate_kernel(tc, q, qa, ka, k, t, v, og, out):
         k_exp_step(0, 1)
         for j in range(PACK):
             nc.scalar.activation(out=k_weights[:, j, :], in_=ka_sb[:], func=ACT.Copy, scale=t_sb[:, j : j + 1])
-        q_exp_step(0)
         k_exp_step(1, 0)
-        k_pos_on_scalar(1, 0)
         k_exp_step(1, 1)
         nc.scalar.copy(
             out=v_bf[:].rearrange("p h (c m j) -> p h c j m", m=4, j=PACK),
             in_=v_raw[:].rearrange("p h (j c m) -> p h c j m", j=PACK, m=4),
         )
-        for x in range(1, PACK - 1):
+        for x in range(PACK):
             q_exp_step(x)
-        q_pos_on_scalar(PACK - 1)
-        q_exp_step(PACK - 1)
-        q_pos_weigh_on_scalar(PACK - 1)
+        q_relu_on_scalar(3, 0)
+        q_relu_on_scalar(3, 1)
+        q_pos_on_scalar(3, 0)
+        q_relu_on_scalar(2, 1)
+        q_pos_on_scalar(3, 1)
+        q_pos_on_scalar(2, 1)
 
         k_pos_on_vector(0, 0)
         k_pos_on_vector(0, 1)
         k_phi_step(0, 0)
         k_phi_step(0, 1)
-        q_pos_step(0)
-        q_pos_step(1)
+        k_pos_on_vector(1, 0)
+        k_pos_on_vector(1, 1)
         for x in range(PACK):
             k_weigh(0, x)
             if x > 0:
                 k_quantise(0, x - 1)
-        k_pos_on_vector(1, 1)
-        k_quantise(0, PACK - 1)
-        q_low_step(0)
         k_phi_step(1, 0)
         k_phi_step(1, 1)
-        q_pos_step(2)
+        k_quantise(0, PACK - 1)
+        nc.vector.quantize_mx(out=v_codes[:].bitcast(FP8X4), scales=v_scales[:], in_=v_bf[:].rearrange("p h c -> p (h c)"))
+        for x in range(PACK):
+            state_product(0, x)
         for x in range(PACK):
             k_weigh(1, x)
-            if x == 1:
-                nc.vector.quantize_mx(
-                    out=v_codes[:].bitcast(FP8X4), scales=v_scales[:], in_=v_bf[:].rearrange("p h c -> p (h c)")
-                )
-                for y in range(PACK):
-                    state_product(0, y)
             if x > 0:
                 k_quantise(1, x - 1)
                 state_product(1, x - 1)
-        q_low_step(1, 0, HALF)
-        q_low_step(2, 0, HALF)
+        q_pos_step(0)
         k_quantise(1, PACK - 1)
         state_product(1, PACK - 1)
 
@@ -271,9 +267,14 @@ def tile_rows_lin_elu1_norm_gate_kernel(tc, q, qa, ka, k, t, v, og, out):
         gate_step(0)
         gate_step(1)
 
+        q_pos_step(1)
+        q_low_step(0)
+        q_low_step(1, 0, HALF)
+        q_pos_step(2, 0, HALF)
+        q_low_step(2, 0, HALF)
         q_low_step(3, 0, HALF)
-        q_low_step(1, HALF, HALF)
         q_low_step(2, HALF, HALF)
+        q_low_step(1, HALF, HALF)
         q_join(0)
         q_low_step(3, HALF, HALF)
         nc.vector.quantize_mx(out=s_codes[:].bitcast(FP8X4), scales=s_scales[:], in_=s_bf[:].rearrange("p e x -> p (e x)"))

@@ -139,13 +139,19 @@ def tile_rows_lin_elu1_norm_gate_kernel(tc, q, qa, ka, k, t, v, og, out):
                 start=(h == 0 and x == 0), stop=(h == H - 1 and x == PACK - 1),
             )
 
+        def fours(row):
+            return row.rearrange("p (c m) -> p c m", m=4)
+
+        def lines(terms, x, first, count):
+            return terms[:].rearrange("p (c x m) -> p x c m", x=PACK, m=4)[:, x, first // 4 : (first + count) // 4, :]
+
         def q_exp_step(x):
             nc.scalar.activation(out=q_exp[:, place(x)], in_=q_raw[:, place(x)], func=ACT.Exp)
 
         def q_pos_step(x, first=0, count=N):
             cols = slice(N * x + first, N * x + first + count)
             nc.vector.tensor_scalar(
-                out=q_pos[:, cols], in0=q_raw[:, cols], scalar1=0.0, scalar2=qa_sb[:, 2 * x : 2 * x + 1],
+                out=lines(q_pos, x, first, count), in0=fours(q_raw[:, cols]), scalar1=0.0, scalar2=qa_sb[:, 2 * x : 2 * x + 1],
                 op0=ALU.max, op1=ALU.mult,
             )
 
@@ -157,25 +163,25 @@ def tile_rows_lin_elu1_norm_gate_kernel(tc, q, qa, ka, k, t, v, og, out):
 
         def q_pos_on_scalar(x, a):
             nc.scalar.activation(
-                out=q_pos[:, q_cols(x, a)], in_=q_relu[:, q_cols(x, a)], func=ACT.Copy, scale=qa_sb[:, 2 * x : 2 * x + 1]
+                out=lines(q_pos, x, HALF * a, HALF), in_=fours(q_relu[:, q_cols(x, a)]), func=ACT.Copy,
+                scale=qa_sb[:, 2 * x : 2 * x + 1],
             )
 
         def q_low_step(x, first=0, count=N):
             cols = slice(N * x + first, N * x + first + count)
             nc.vector.tensor_scalar(
-                out=q_low[:, cols], in0=q_exp[:, cols], scalar1=1.0, scalar2=qa_sb[:, 2 * x : 2 * x + 1],
+                out=lines(q_low, x, first, count), in0=fours(q_exp[:, cols]), scalar1=1.0, scalar2=qa_sb[:, 2 * x : 2 * x + 1],
                 op0=ALU.min, op1=ALU.mult,
             )
 
         def q_join(g):
             first, count = GROUPS[g]
 
-            def pairs(terms):
-                rows = terms[:].rearrange("p (x n) -> p x n", x=PACK)[:, :, first : first + count]
-                return rows.rearrange("p x (c u) -> p c x u", u=2)
+            def block(terms):
+                return terms[:, PACK * first : PACK * (first + count)].rearrange("p (c x m) -> p c x m", x=PACK, m=4)
 
             nc.vector.tensor_tensor(
-                out=q_bf[g][:].rearrange("p (c u x) -> p c x u", u=2, x=PACK), in0=pairs(q_pos), in1=pairs(q_low),
+                out=q_bf[g][:].rearrange("p (c m x) -> p c x m", m=4, x=PACK), in0=block(q_pos), in1=block(q_low),
                 op=ALU.add,
             )
 

@@ -46,15 +46,17 @@ def tile_rows_lin_elu1_norm_gate_kernel(tc, q, qa, ka, k, t, v, og, out):
 
         k_view = k.rearrange("h (p a j) d -> h a p (j d)", a=2, j=2)
         q_view = q.rearrange("h (c x u) n -> x (h c) u n", x=PACK, u=2)
-        for a in range(2):
-            nc.sync.dma_start(out=k_raw[0][:, piece(a)], in_=k_view[0, a])
         nc.sync.dma_start(out=ka_sb[:], in_=ka)
         nc.sync.dma_start(out=t_sb[:], in_=t.rearrange("(p j) o -> p (j o)", j=PACK))
-        for a in range(2):
-            nc.sync.dma_start(out=k_raw[1][:, piece(a)], in_=k_view[1, a])
+        nc.sync.dma_start(out=k_raw[0][:, piece(0)], in_=k_view[0, 0])
+        nc.sync.dma_start(out=k_raw[0][:, piece(1)], in_=k_view[0, 1])
+        nc.sync.dma_start(out=k_raw[1][:, piece(0)], in_=k_view[1, 0])
+        nc.sync.dma_start(out=k_raw[1][:, piece(1)], in_=k_view[1, 1])
         nc.sync.dma_start(out=v_raw[:], in_=v.rearrange("h (p j) e -> p h (j e)", j=PACK))
-        for x in range(PACK):
-            nc.sync.dma_start(out=q_raw[:, place(x)], in_=q_view[x])
+        nc.sync.dma_start(out=q_raw[:, place(0)], in_=q_view[0])
+        nc.sync.dma_start(out=q_raw[:, place(1)], in_=q_view[1])
+        nc.sync.dma_start(out=q_raw[:, place(2)], in_=q_view[2])
+        nc.sync.dma_start(out=q_raw[:, place(3)], in_=q_view[3])
         qa_view = qa.rearrange("(c m) o -> c (m o)", m=2 * PACK)
         for h in range(H):
             for u in range(2):
@@ -62,10 +64,11 @@ def tile_rows_lin_elu1_norm_gate_kernel(tc, q, qa, ka, k, t, v, og, out):
                     out=qa_sb[ROWS * h + u : ROWS * (h + 1) : 2, 0 : 2 * PACK - 1], in_=qa_view[:, u : u + 2 * PACK - 1]
                 )
         nc.sync.dma_start(
-            out=og_raw[:].rearrange("p h r e -> p (h r) e"), in_=og.rearrange("h (r p) e -> p (h r) e", p=P)
+            out=og_raw[:].rearrange("p h (s r) e -> p (h s) (r e)", r=2),
+            in_=og.rearrange("h (s p r) e -> p (h s) (r e)", s=2, r=2),
         )
 
-        k_weights = sbuf("k_weights", [P, PACK, D], F32)
+        k_weights = sbuf("k_weights", [P, 2, D, 2], F32)
         k_exp = [sbuf("k_exp%d" % h, [P, PACK * D], F32) for h in range(H)]
         k_pos = [sbuf("k_pos%d" % h, [P, PACK * D], F32) for h in range(H)]
         k_phi = [sbuf("k_phi%d" % h, [P, PACK * D], F32) for h in range(H)]
@@ -88,7 +91,8 @@ def tile_rows_lin_elu1_norm_gate_kernel(tc, q, qa, ka, k, t, v, og, out):
         q_relu = sbuf("q_relu", [P, PACK * N], F32)
         gate_tanh = [sbuf("gate_tanh%d" % a, [P, H, HALF // P * E], F32) for a in range(2)]
         gate = [sbuf("gate%d" % a, [P, H, HALF // P * E], F32) for a in range(2)]
-        q_bf, q_codes, q_scales, y_ps, inverse, result = {}, {}, {}, {}, {}, {}
+        result = {(a, h): sbuf("result%d%d" % (a, h), [P, HALF // P, E], F32) for a in range(2) for h in range(H)}
+        q_bf, q_codes, q_scales, y_ps, inverse = {}, {}, {}, {}, {}
         for g, (first, count) in enumerate(GROUPS):
             q_bf[g] = sbuf("q_bf%d" % g, [P, count * PACK], BF16)
             q_codes[g] = sbuf("q_codes%d" % g, [P, count], U32)
@@ -96,18 +100,24 @@ def tile_rows_lin_elu1_norm_gate_kernel(tc, q, qa, ka, k, t, v, og, out):
             for h in range(H):
                 y_ps[g, h] = ps.tile([P, count // P * E], F32, name="y_ps%d%d" % (g, h))
                 inverse[g, h] = sbuf("inverse%d%d" % (g, h), [P, count // P], F32)
-                result[g, h] = sbuf("result%d%d" % (g, h), [P, count // P, E], F32)
+
+        def in_pairs(rows):
+            return rows.rearrange("p (b n) -> p n b", b=2)
+
+        def as_pairs(pairs):
+            return pairs.rearrange("p (n b) -> p n b", b=2)
 
         def k_exp_step(h, a):
-            nc.scalar.activation(out=k_exp[h][:, piece(a)], in_=k_raw[h][:, piece(a)], func=ACT.Exp)
+            nc.scalar.activation(out=as_pairs(k_exp[h][:, piece(a)]), in_=in_pairs(k_raw[h][:, piece(a)]), func=ACT.Exp)
 
         def k_pos_on_vector(h, a):
             nc.vector.tensor_scalar(
-                out=k_pos[h][:, piece(a)], in0=k_raw[h][:, piece(a)], scalar1=0.0, scalar2=None, op0=ALU.max
+                out=as_pairs(k_pos[h][:, piece(a)]), in0=in_pairs(k_raw[h][:, piece(a)]), scalar1=0.0, scalar2=None,
+                op0=ALU.max,
             )
 
         def k_pos_on_scalar(h, a):
-            nc.scalar.activation(out=k_pos[h][:, piece(a)], in_=k_raw[h][:, piece(a)], func=ACT.Relu)
+            nc.scalar.activation(out=as_pairs(k_pos[h][:, piece(a)]), in_=in_pairs(k_raw[h][:, piece(a)]), func=ACT.Relu)
 
         def k_phi_step(h, a):
             nc.vector.scalar_tensor_tensor(
@@ -115,16 +125,24 @@ def tile_rows_lin_elu1_norm_gate_kernel(tc, q, qa, ka, k, t, v, og, out):
                 op0=ALU.min, op1=ALU.add,
             )
 
+        def k_weights_step(a):
+            nc.vector.tensor_tensor(
+                out=k_weights[:, a],
+                in0=ka_sb[:].unsqueeze(2).to_broadcast([P, D, 2]),
+                in1=t_sb[:, 2 * a : 2 * a + 2].unsqueeze(1).to_broadcast([P, D, 2]),
+                op=ALU.mult,
+            )
+
         def k_quantise(h, x):
             first = ROWS * (3 * x + 2 * h)
             cols = slice(first, first + ROWS)
             nc.vector.quantize_mx(out=k_codes[:, cols].bitcast(FP8X4), scales=k_scales[:, cols], in_=k_bf[h][:, x, :])
 
-        def k_weigh(h, x):
+        def k_weigh(h):
             nc.vector.tensor_tensor(
-                out=k_bf[h][:, x, :].rearrange("p (c u j) -> p c j u", u=2, j=PACK),
-                in0=k_phi[h][:].rearrange("p (j c x u) -> p x c j u", j=PACK, x=PACK, u=2)[:, x],
-                in1=k_weights[:].rearrange("p j (c x u) -> p x c j u", x=PACK, u=2)[:, x],
+                out=k_bf[h][:].rearrange("p x (c u a b) -> p c x u a b", u=2, a=2, b=2),
+                in0=k_phi[h][:].rearrange("p (a c x u b) -> p c x u a b", a=2, x=PACK, u=2, b=2),
+                in1=k_weights[:].rearrange("p a (c x u) b -> p c x u a b", x=PACK, u=2),
                 op=ALU.mult,
             )
 
@@ -139,11 +157,12 @@ def tile_rows_lin_elu1_norm_gate_kernel(tc, q, qa, ka, k, t, v, og, out):
                 start=(h == 0 and x == 0), stop=(h == H - 1 and x == PACK - 1),
             )
 
-        def fours(row):
-            return row.rearrange("p (c m) -> p c m", m=4)
+        def dealt(rows):
+            return rows.rearrange("p (s c m r) -> p s r c m", c=P // 4, m=4, r=2)
 
         def lines(terms, x, first, count):
-            return terms[:].rearrange("p (c x m) -> p x c m", x=PACK, m=4)[:, x, first // 4 : (first + count) // 4, :]
+            tiles = terms[:].rearrange("p (s r c x m) -> p x s r c m", s=2, r=2, x=PACK, m=4)
+            return tiles[:, x, first // HALF : (first + count) // HALF]
 
         def q_exp_step(x):
             nc.scalar.activation(out=q_exp[:, place(x)], in_=q_raw[:, place(x)], func=ACT.Exp)
@@ -151,26 +170,29 @@ def tile_rows_lin_elu1_norm_gate_kernel(tc, q, qa, ka, k, t, v, og, out):
         def q_pos_step(x, first=0, count=N):
             cols = slice(N * x + first, N * x + first + count)
             nc.vector.tensor_scalar(
-                out=lines(q_pos, x, first, count), in0=fours(q_raw[:, cols]), scalar1=0.0, scalar2=qa_sb[:, 2 * x : 2 * x + 1],
+                out=lines(q_pos, x, first, count), in0=dealt(q_raw[:, cols]), scalar1=0.0, scalar2=qa_sb[:, 2 * x : 2 * x + 1],
                 op0=ALU.max, op1=ALU.mult,
             )
 
         def q_cols(x, a):
             return slice(N * x + HALF * a, N * x + HALF * (a + 1))
 
-        def q_relu_on_scalar(x, a):
-            nc.scalar.activation(out=q_relu[:, q_cols(x, a)], in_=q_raw[:, q_cols(x, a)], func=ACT.Relu)
+        def q_relu_on_scalar(a):
+            def half(rows):
+                return rows[:].rearrange("p (x n) -> p x n", x=PACK)[:, :, HALF * a : HALF * (a + 1)]
+
+            nc.scalar.activation(out=half(q_relu), in_=half(q_raw), func=ACT.Relu)
 
         def q_pos_on_scalar(x, a):
             nc.scalar.activation(
-                out=lines(q_pos, x, HALF * a, HALF), in_=fours(q_relu[:, q_cols(x, a)]), func=ACT.Copy,
+                out=lines(q_pos, x, HALF * a, HALF), in_=dealt(q_relu[:, q_cols(x, a)]), func=ACT.Copy,
                 scale=qa_sb[:, 2 * x : 2 * x + 1],
             )
 
         def q_low_step(x, first=0, count=N):
             cols = slice(N * x + first, N * x + first + count)
             nc.vector.tensor_scalar(
-                out=lines(q_low, x, first, count), in0=fours(q_exp[:, cols]), scalar1=1.0, scalar2=qa_sb[:, 2 * x : 2 * x + 1],
+                out=lines(q_low, x, first, count), in0=dealt(q_exp[:, cols]), scalar1=1.0, scalar2=qa_sb[:, 2 * x : 2 * x + 1],
                 op0=ALU.min, op1=ALU.mult,
             )
 
@@ -213,74 +235,84 @@ def tile_rows_lin_elu1_norm_gate_kernel(tc, q, qa, ka, k, t, v, og, out):
 
         def finish(g, h):
             first, count = GROUPS[g]
+            half = first // HALF
             for r in range(count // P):
                 tile = first % HALF // P + r
                 nc.vector.scalar_tensor_tensor(
-                    out=result[g, h][:, r, :], in0=y_ps[g, h][:, E * r : E * (r + 1)],
-                    scalar=inverse[g, h][:, r : r + 1], in1=gate[first // HALF][:, h, E * tile : E * (tile + 1)],
+                    out=result[half, h][:, tile, :], in0=y_ps[g, h][:, E * r : E * (r + 1)],
+                    scalar=inverse[g, h][:, r : r + 1], in1=gate[half][:, h, E * tile : E * (tile + 1)],
                     op0=ALU.mult, op1=ALU.mult,
                 )
+
+        def store(half, h):
             queue = nc.scalar if h == 0 else nc.sync
-            queue.dma_start(out=out[h, first : first + count, :].rearrange("(r p) e -> p r e", p=P), in_=result[g, h][:])
+            rows = out[h, HALF * half : HALF * (half + 1), :]
+            queue.dma_start(out=rows.rearrange("(p r) e -> p r e", r=2), in_=result[half, h][:])
 
         k_exp_step(0, 0)
         k_exp_step(0, 1)
-        for j in range(PACK):
-            nc.scalar.activation(out=k_weights[:, j, :], in_=ka_sb[:], func=ACT.Copy, scale=t_sb[:, j : j + 1])
         k_exp_step(1, 0)
         k_exp_step(1, 1)
+        k_pos_on_scalar(1, 1)
         nc.scalar.copy(
             out=v_bf[:].rearrange("p h (c m j) -> p h c j m", m=4, j=PACK),
             in_=v_raw[:].rearrange("p h (j c m) -> p h c j m", j=PACK, m=4),
         )
-        for x in range(PACK):
-            q_exp_step(x)
-        q_relu_on_scalar(3, 0)
-        q_relu_on_scalar(3, 1)
-        q_pos_on_scalar(3, 0)
-        q_relu_on_scalar(2, 1)
-        q_pos_on_scalar(3, 1)
-        q_pos_on_scalar(2, 1)
-
+        q_exp_step(0)
+        q_exp_step(1)
+        q_exp_step(2)
+        q_exp_step(3)
+        q_relu_on_scalar(1)
+        nc.vector.tensor_tensor(
+            out=k_weights[:],
+            in0=ka_sb[:].unsqueeze(1).unsqueeze(3).to_broadcast([P, 2, D, 2]),
+            in1=t_sb[:].rearrange("p (a b) -> p a b", a=2).unsqueeze(2).to_broadcast([P, 2, D, 2]),
+            op=ALU.mult,
+        )
         k_pos_on_vector(0, 0)
         k_pos_on_vector(0, 1)
         k_phi_step(0, 0)
         k_phi_step(0, 1)
         k_pos_on_vector(1, 0)
-        k_pos_on_vector(1, 1)
-        for x in range(PACK):
-            k_weigh(0, x)
-            if x > 0:
-                k_quantise(0, x - 1)
+        k_weigh(0)
         k_phi_step(1, 0)
+        k_quantise(0, 0)
+        k_quantise(0, 1)
+        k_quantise(0, 2)
+        k_quantise(0, 3)
         k_phi_step(1, 1)
-        k_quantise(0, PACK - 1)
         nc.vector.quantize_mx(out=v_codes[:].bitcast(FP8X4), scales=v_scales[:], in_=v_bf[:].rearrange("p h c -> p (h c)"))
-        for x in range(PACK):
-            state_product(0, x)
-        for x in range(PACK):
-            k_weigh(1, x)
-            if x > 0:
-                k_quantise(1, x - 1)
-                state_product(1, x - 1)
-        q_pos_step(0)
-        k_quantise(1, PACK - 1)
-        state_product(1, PACK - 1)
-
+        state_product(0, 0)
+        state_product(0, 1)
+        state_product(0, 2)
+        state_product(0, 3)
+        k_weigh(1)
+        q_pos_step(0, 0, HALF)
+        q_pos_step(1, 0, HALF)
+        k_quantise(1, 0)
+        state_product(1, 0)
+        k_quantise(1, 1)
+        state_product(1, 1)
+        k_quantise(1, 2)
+        state_product(1, 2)
+        k_quantise(1, 3)
+        state_product(1, 3)
         nc.scalar.activation(out=s_bf[:], in_=s_ps[:].rearrange("p x e -> p e x"), func=ACT.Copy, scale=1.0 / N)
+        q_pos_on_scalar(0, 1)
+        q_pos_on_scalar(1, 1)
+        q_pos_on_scalar(2, 1)
+        q_pos_on_scalar(3, 1)
         tanh_step(0)
         tanh_step(1)
         gate_step(0)
         gate_step(1)
-
-        q_pos_step(1)
-        q_low_step(0)
-        q_low_step(1, 0, HALF)
         q_pos_step(2, 0, HALF)
+        q_pos_step(3, 0, HALF)
+        q_low_step(0)
+        q_low_step(1)
         q_low_step(2, 0, HALF)
         q_low_step(3, 0, HALF)
         q_low_step(2, HALF, HALF)
-        q_low_step(1, HALF, HALF)
         q_join(0)
         q_low_step(3, HALF, HALF)
         nc.vector.quantize_mx(out=s_codes[:].bitcast(FP8X4), scales=s_scales[:], in_=s_bf[:].rearrange("p e x -> p (e x)"))
@@ -291,11 +323,17 @@ def tile_rows_lin_elu1_norm_gate_kernel(tc, q, qa, ka, k, t, v, og, out):
         q_quantise_and_read(1)
         invert(0, 1)
         q_quantise_and_read(2)
-        for h in range(H):
-            finish(0, h)
-        for g in (1, 2):
-            for h in range(H):
-                invert(g, h)
-        for g in (1, 2):
-            for h in range(H):
-                finish(g, h)
+        finish(0, 0)
+        store(0, 0)
+        finish(0, 1)
+        store(0, 1)
+        invert(1, 0)
+        invert(1, 1)
+        invert(2, 0)
+        finish(1, 0)
+        invert(2, 1)
+        finish(2, 0)
+        store(1, 0)
+        finish(1, 1)
+        finish(2, 1)
+        store(1, 1)

@@ -125,14 +125,6 @@ def tile_rows_lin_elu1_norm_gate_kernel(tc, q, qa, ka, k, t, v, og, out):
                 op0=ALU.min, op1=ALU.add,
             )
 
-        def k_weights_step(a):
-            nc.vector.tensor_tensor(
-                out=k_weights[:, a],
-                in0=ka_sb[:].unsqueeze(2).to_broadcast([P, D, 2]),
-                in1=t_sb[:, 2 * a : 2 * a + 2].unsqueeze(1).to_broadcast([P, D, 2]),
-                op=ALU.mult,
-            )
-
         def k_quantise(h, x):
             first = ROWS * (3 * x + 2 * h)
             cols = slice(first, first + ROWS)
@@ -177,9 +169,9 @@ def tile_rows_lin_elu1_norm_gate_kernel(tc, q, qa, ka, k, t, v, og, out):
         def q_cols(x, a):
             return slice(N * x + HALF * a, N * x + HALF * (a + 1))
 
-        def q_relu_on_scalar(a):
+        def q_relu_pair(b):
             def half(rows):
-                return rows[:].rearrange("p (x n) -> p x n", x=PACK)[:, :, HALF * a : HALF * (a + 1)]
+                return rows[:].rearrange("p (x n) -> p x n", x=PACK)[:, 2 * b : 2 * b + 2, HALF:]
 
             nc.scalar.activation(out=half(q_relu), in_=half(q_raw), func=ACT.Relu)
 
@@ -262,7 +254,8 @@ def tile_rows_lin_elu1_norm_gate_kernel(tc, q, qa, ka, k, t, v, og, out):
         q_exp_step(1)
         q_exp_step(2)
         q_exp_step(3)
-        q_relu_on_scalar(1)
+        q_relu_pair(0)
+        q_relu_pair(1)
         nc.vector.tensor_tensor(
             out=k_weights[:],
             in0=ka_sb[:].unsqueeze(1).unsqueeze(3).to_broadcast([P, 2, D, 2]),
@@ -297,9 +290,9 @@ def tile_rows_lin_elu1_norm_gate_kernel(tc, q, qa, ka, k, t, v, og, out):
         state_product(1, 2)
         k_quantise(1, 3)
         state_product(1, 3)
-        nc.scalar.activation(out=s_bf[:], in_=s_ps[:].rearrange("p x e -> p e x"), func=ACT.Copy, scale=1.0 / N)
         q_pos_on_scalar(0, 1)
         q_pos_on_scalar(1, 1)
+        nc.scalar.activation(out=s_bf[:], in_=s_ps[:].rearrange("p x e -> p e x"), func=ACT.Copy, scale=1.0 / N)
         q_pos_on_scalar(2, 1)
         q_pos_on_scalar(3, 1)
         tanh_step(0)
@@ -309,9 +302,10 @@ def tile_rows_lin_elu1_norm_gate_kernel(tc, q, qa, ka, k, t, v, og, out):
         q_pos_step(2, 0, HALF)
         q_pos_step(3, 0, HALF)
         q_low_step(0)
-        q_low_step(1)
+        q_low_step(1, 0, HALF)
         q_low_step(2, 0, HALF)
         q_low_step(3, 0, HALF)
+        q_low_step(1, HALF, HALF)
         q_low_step(2, HALF, HALF)
         q_join(0)
         q_low_step(3, HALF, HALF)

@@ -112,8 +112,8 @@ def tile_rows_lin_elu1_norm_gate_kernel(tc, q, qa, ka, k, t, v, og, out):
 
         def k_pos_on_vector(h, a):
             nc.vector.tensor_scalar(
-                out=as_pairs(k_pos[h][:, piece(a)]), in0=in_pairs(k_raw[h][:, piece(a)]), scalar1=0.0, scalar2=None,
-                op0=ALU.max,
+                out=as_pairs(k_pos[h][:, piece(a)]), in0=in_pairs(k_raw[h][:, piece(a)]), scalar1=0.0, scalar2=1.0,
+                op0=ALU.max, op1=ALU.add,
             )
 
         def k_pos_on_scalar(h, a):
@@ -123,6 +123,11 @@ def tile_rows_lin_elu1_norm_gate_kernel(tc, q, qa, ka, k, t, v, og, out):
             nc.vector.scalar_tensor_tensor(
                 out=k_phi[h][:, piece(a)], in0=k_exp[h][:, piece(a)], scalar=1.0, in1=k_pos[h][:, piece(a)],
                 op0=ALU.min, op1=ALU.add,
+            )
+
+        def k_phi_by_min(h, a):
+            nc.vector.tensor_tensor(
+                out=k_phi[h][:, piece(a)], in0=k_exp[h][:, piece(a)], in1=k_pos[h][:, piece(a)], op=ALU.min
             )
 
         def k_quantise(h, x):
@@ -264,11 +269,11 @@ def tile_rows_lin_elu1_norm_gate_kernel(tc, q, qa, ka, k, t, v, og, out):
         )
         k_pos_on_vector(0, 0)
         k_pos_on_vector(0, 1)
-        k_phi_step(0, 0)
-        k_phi_step(0, 1)
+        k_phi_by_min(0, 0)
+        k_phi_by_min(0, 1)
         k_pos_on_vector(1, 0)
         k_weigh(0)
-        k_phi_step(1, 0)
+        k_phi_by_min(1, 0)
         k_quantise(0, 0)
         k_quantise(0, 1)
         k_quantise(0, 2)

@@ -46,27 +46,46 @@ def tile_rows_lin_elu1_norm_gate_kernel(tc, q, qa, ka, k, t, v, og, out):
 
         k_view = k.rearrange("h (p a j) d -> h a p (j d)", a=2, j=2)
         q_view = q.rearrange("h (c x u) n -> x (h c) u n", x=PACK, u=2)
+        v_view = v.rearrange("h (p j) e -> p h (j e)", j=PACK)
+        qa_view = qa.rearrange("(c m) o -> c (m o)", m=2 * PACK)
+
+        def load_k(h, a):
+            nc.sync.dma_start(out=k_raw[h][:, piece(a)], in_=k_view[h, a])
+
+        def load_v(heads):
+            nc.sync.dma_start(out=v_raw[:, heads], in_=v_view[:, heads])
+
+        def load_q(x):
+            nc.sync.dma_start(out=q_raw[:, place(x)], in_=q_view[x])
+
+        def load_qa():
+            for h in range(H):
+                for u in range(2):
+                    nc.sync.dma_start(
+                        out=qa_sb[ROWS * h + u : ROWS * (h + 1) : 2, 0 : 2 * PACK - 1],
+                        in_=qa_view[:, u : u + 2 * PACK - 1],
+                    )
+
+        def load_og():
+            nc.sync.dma_start(
+                out=og_raw[:].rearrange("p h (s r) e -> p (h s) (r e)", r=2),
+                in_=og.rearrange("h (s p r) e -> p (h s) (r e)", s=2, r=2),
+            )
+
+        both = slice(0, 2)
         nc.sync.dma_start(out=ka_sb[:], in_=ka)
         nc.sync.dma_start(out=t_sb[:], in_=t.rearrange("(p j) o -> p (j o)", j=PACK))
-        nc.sync.dma_start(out=k_raw[0][:, piece(0)], in_=k_view[0, 0])
-        nc.sync.dma_start(out=k_raw[0][:, piece(1)], in_=k_view[0, 1])
-        nc.sync.dma_start(out=k_raw[1][:, piece(0)], in_=k_view[1, 0])
-        nc.sync.dma_start(out=k_raw[1][:, piece(1)], in_=k_view[1, 1])
-        nc.sync.dma_start(out=v_raw[:], in_=v.rearrange("h (p j) e -> p h (j e)", j=PACK))
-        nc.sync.dma_start(out=q_raw[:, place(0)], in_=q_view[0])
-        nc.sync.dma_start(out=q_raw[:, place(1)], in_=q_view[1])
-        nc.sync.dma_start(out=q_raw[:, place(2)], in_=q_view[2])
-        nc.sync.dma_start(out=q_raw[:, place(3)], in_=q_view[3])
-        qa_view = qa.rearrange("(c m) o -> c (m o)", m=2 * PACK)
-        for h in range(H):
-            for u in range(2):
-                nc.sync.dma_start(
-                    out=qa_sb[ROWS * h + u : ROWS * (h + 1) : 2, 0 : 2 * PACK - 1], in_=qa_view[:, u : u + 2 * PACK - 1]
-                )
-        nc.sync.dma_start(
-            out=og_raw[:].rearrange("p h (s r) e -> p (h s) (r e)", r=2),
-            in_=og.rearrange("h (s p r) e -> p (h s) (r e)", s=2, r=2),
-        )
+        load_k(0, 0)
+        load_k(0, 1)
+        load_k(1, 0)
+        load_k(1, 1)
+        load_v(both)
+        load_q(0)
+        load_q(1)
+        load_q(2)
+        load_q(3)
+        load_qa()
+        load_og()
 
         k_weights = sbuf("k_weights", [P, 2, D, 2], F32)
         k_exp = [sbuf("k_exp%d" % h, [P, PACK * D], F32) for h in range(H)]
@@ -119,27 +138,32 @@ def tile_rows_lin_elu1_norm_gate_kernel(tc, q, qa, ka, k, t, v, og, out):
         def k_pos_on_scalar(h, a):
             nc.scalar.activation(out=as_pairs(k_pos[h][:, piece(a)]), in_=in_pairs(k_raw[h][:, piece(a)]), func=ACT.Relu)
 
-        def k_phi_step(h, a):
+        def features(a, part):
+            first, count = (0, D) if part is None else (D // 2 * part, D // 2)
+            return slice(2 * (D * a + first), 2 * (D * a + first + count))
+
+        def k_phi_step(h, a, part=None):
+            cols = features(a, part)
             nc.vector.scalar_tensor_tensor(
-                out=k_phi[h][:, piece(a)], in0=k_exp[h][:, piece(a)], scalar=1.0, in1=k_pos[h][:, piece(a)],
+                out=k_phi[h][:, cols], in0=k_exp[h][:, cols], scalar=1.0, in1=k_pos[h][:, cols],
                 op0=ALU.min, op1=ALU.add,
             )
 
-        def k_phi_by_min(h, a):
-            nc.vector.tensor_tensor(
-                out=k_phi[h][:, piece(a)], in0=k_exp[h][:, piece(a)], in1=k_pos[h][:, piece(a)], op=ALU.min
-            )
+        def k_phi_by_min(h, a, part=None):
+            cols = features(a, part)
+            nc.vector.tensor_tensor(out=k_phi[h][:, cols], in0=k_exp[h][:, cols], in1=k_pos[h][:, cols], op=ALU.min)
 
         def k_quantise(h, x):
             first = ROWS * (3 * x + 2 * h)
             cols = slice(first, first + ROWS)
             nc.vector.quantize_mx(out=k_codes[:, cols].bitcast(FP8X4), scales=k_scales[:, cols], in_=k_bf[h][:, x, :])
 
-        def k_weigh(h):
+        def k_weigh(h, part=None):
+            c = slice(0, 32) if part is None else slice(16 * part, 16 * (part + 1))
             nc.vector.tensor_tensor(
-                out=k_bf[h][:].rearrange("p x (c u a b) -> p c x u a b", u=2, a=2, b=2),
-                in0=k_phi[h][:].rearrange("p (a c x u b) -> p c x u a b", a=2, x=PACK, u=2, b=2),
-                in1=k_weights[:].rearrange("p a (c x u) b -> p c x u a b", x=PACK, u=2),
+                out=k_bf[h][:].rearrange("p x (c u a b) -> p c x u a b", u=2, a=2, b=2)[:, c],
+                in0=k_phi[h][:].rearrange("p (a c x u b) -> p c x u a b", a=2, x=PACK, u=2, b=2)[:, c],
+                in1=k_weights[:].rearrange("p a (c x u) b -> p c x u a b", x=PACK, u=2)[:, c],
                 op=ALU.mult,
             )
 
@@ -207,10 +231,10 @@ def tile_rows_lin_elu1_norm_gate_kernel(tc, q, qa, ka, k, t, v, og, out):
         def q_quantise_and_read(g):
             first, count = GROUPS[g]
             nc.vector.quantize_mx(out=q_codes[g][:].bitcast(FP8X4), scales=q_scales[g][:], in_=q_bf[g][:])
-            for h in range(H):
-                rows = slice(ROWS * h, ROWS * (h + 1))
-                for r in range(count // P):
-                    cols = slice(P * r, P * (r + 1))
+            for r in range(count // P):
+                cols = slice(P * r, P * (r + 1))
+                for h in range(H):
+                    rows = slice(ROWS * h, ROWS * (h + 1))
                     nc.tensor.matmul_mx(
                         out=y_ps[g, h][:, cols],
                         lhsT=q_codes[g][rows, cols].bitcast(FP8X4), lhsT_scale=q_scales[g][rows, cols],
@@ -218,28 +242,57 @@ def tile_rows_lin_elu1_norm_gate_kernel(tc, q, qa, ka, k, t, v, og, out):
                         start=True, stop=True,
                     )
 
-        def tanh_step(a):
-            tiles = og_raw[:, :, HALF // P * a : HALF // P * (a + 1), :]
+        def tanh_step(a, heads=slice(0, H)):
+            tiles = og_raw[:, heads, HALF // P * a : HALF // P * (a + 1), :]
             nc.scalar.activation(
-                out=gate_tanh[a][:], in_=tiles.rearrange("p h r e -> p h (r e)"), func=ACT.Tanh, scale=0.5
+                out=gate_tanh[a][:, heads], in_=tiles.rearrange("p h r e -> p h (r e)"), func=ACT.Tanh, scale=0.5
             )
 
-        def gate_step(a):
-            nc.scalar.activation(out=gate[a][:], in_=gate_tanh[a][:], func=ACT.Identity, scale=0.5, bias=0.5)
+        def gate_step(a, heads=slice(0, H)):
+            nc.scalar.activation(
+                out=gate[a][:, heads], in_=gate_tanh[a][:, heads], func=ACT.Identity, scale=0.5, bias=0.5
+            )
+
+        def v_round(heads):
+            nc.scalar.copy(
+                out=v_bf[:, heads].rearrange("p h (c m j) -> p h c j m", m=4, j=PACK),
+                in_=v_raw[:, heads].rearrange("p h (j c m) -> p h c j m", j=PACK, m=4),
+            )
+
+        def v_quantise(heads):
+            cols = slice(E * heads.start, E * heads.stop)
+            nc.vector.quantize_mx(
+                out=v_codes[:, cols].bitcast(FP8X4), scales=v_scales[:, cols],
+                in_=v_bf[:, heads].rearrange("p h c -> p (h c)"),
+            )
+
+        def k_weights_step():
+            nc.vector.tensor_tensor(
+                out=k_weights[:],
+                in0=ka_sb[:].unsqueeze(1).unsqueeze(3).to_broadcast([P, 2, D, 2]),
+                in1=t_sb[:].rearrange("p (a b) -> p a b", a=2).unsqueeze(2).to_broadcast([P, 2, D, 2]),
+                op=ALU.mult,
+            )
+
+        def state_round():
+            nc.scalar.activation(out=s_bf[:], in_=s_ps[:].rearrange("p x e -> p e x"), func=ACT.Copy, scale=1.0 / N)
+
+        def state_quantise():
+            nc.vector.quantize_mx(
+                out=s_codes[:].bitcast(FP8X4), scales=s_scales[:], in_=s_bf[:].rearrange("p e x -> p (e x)")
+            )
 
         def invert(g, h):
             nc.vector.reciprocal(out=inverse[g, h][:], in_=y_ps[g, h][:, E - 1 :: E])
 
-        def finish(g, h):
+        def finish(g, h, r=0):
             first, count = GROUPS[g]
-            half = first // HALF
-            for r in range(count // P):
-                tile = first % HALF // P + r
-                nc.vector.scalar_tensor_tensor(
-                    out=result[half, h][:, tile, :], in0=y_ps[g, h][:, E * r : E * (r + 1)],
-                    scalar=inverse[g, h][:, r : r + 1], in1=gate[half][:, h, E * tile : E * (tile + 1)],
-                    op0=ALU.mult, op1=ALU.mult,
-                )
+            half, tile = first // HALF, first % HALF // P + r
+            nc.vector.scalar_tensor_tensor(
+                out=result[half, h][:, tile, :], in0=y_ps[g, h][:, E * r : E * (r + 1)],
+                scalar=inverse[g, h][:, r : r + 1], in1=gate[half][:, h, E * tile : E * (tile + 1)],
+                op0=ALU.mult, op1=ALU.mult,
+            )
 
         def store(half, h):
             queue = nc.scalar if h == 0 else nc.sync
@@ -249,42 +302,38 @@ def tile_rows_lin_elu1_norm_gate_kernel(tc, q, qa, ka, k, t, v, og, out):
         k_exp_step(0, 0)
         k_exp_step(0, 1)
         k_exp_step(1, 0)
+        k_pos_on_scalar(1, 0)
         k_exp_step(1, 1)
         k_pos_on_scalar(1, 1)
-        nc.scalar.copy(
-            out=v_bf[:].rearrange("p h (c m j) -> p h c j m", m=4, j=PACK),
-            in_=v_raw[:].rearrange("p h (j c m) -> p h c j m", j=PACK, m=4),
-        )
+        v_round(both)
         q_exp_step(0)
         q_exp_step(1)
         q_exp_step(2)
         q_exp_step(3)
         q_relu_pair(0)
         q_relu_pair(1)
-        nc.vector.tensor_tensor(
-            out=k_weights[:],
-            in0=ka_sb[:].unsqueeze(1).unsqueeze(3).to_broadcast([P, 2, D, 2]),
-            in1=t_sb[:].rearrange("p (a b) -> p a b", a=2).unsqueeze(2).to_broadcast([P, 2, D, 2]),
-            op=ALU.mult,
-        )
+        k_weights_step()
         k_pos_on_vector(0, 0)
         k_pos_on_vector(0, 1)
         k_phi_by_min(0, 0)
-        k_phi_by_min(0, 1)
-        k_pos_on_vector(1, 0)
-        k_weigh(0)
-        k_phi_by_min(1, 0)
+        k_phi_by_min(0, 1, 0)
+        k_phi_by_min(0, 1, 1)
+        k_weigh(0, 0)
+        k_weigh(0, 1)
+        k_phi_step(1, 0)
         k_quantise(0, 0)
         k_quantise(0, 1)
         k_quantise(0, 2)
         k_quantise(0, 3)
-        k_phi_step(1, 1)
-        nc.vector.quantize_mx(out=v_codes[:].bitcast(FP8X4), scales=v_scales[:], in_=v_bf[:].rearrange("p h c -> p (h c)"))
+        k_phi_step(1, 1, 0)
+        k_phi_step(1, 1, 1)
+        k_weigh(1, 0)
+        v_quantise(both)
         state_product(0, 0)
         state_product(0, 1)
         state_product(0, 2)
         state_product(0, 3)
-        k_weigh(1)
+        k_weigh(1, 1)
         q_pos_step(0, 0, HALF)
         q_pos_step(1, 0, HALF)
         k_quantise(1, 0)
@@ -297,13 +346,15 @@ def tile_rows_lin_elu1_norm_gate_kernel(tc, q, qa, ka, k, t, v, og, out):
         state_product(1, 3)
         q_pos_on_scalar(0, 1)
         q_pos_on_scalar(1, 1)
-        nc.scalar.activation(out=s_bf[:], in_=s_ps[:].rearrange("p x e -> p e x"), func=ACT.Copy, scale=1.0 / N)
+        state_round()
         q_pos_on_scalar(2, 1)
         q_pos_on_scalar(3, 1)
         tanh_step(0)
-        tanh_step(1)
+        tanh_step(1, slice(0, 1))
         gate_step(0)
-        gate_step(1)
+        tanh_step(1, slice(1, 2))
+        gate_step(1, slice(0, 1))
+        gate_step(1, slice(1, 2))
         q_pos_step(2, 0, HALF)
         q_pos_step(3, 0, HALF)
         q_low_step(0)
@@ -314,20 +365,22 @@ def tile_rows_lin_elu1_norm_gate_kernel(tc, q, qa, ka, k, t, v, og, out):
         q_low_step(2, HALF, HALF)
         q_join(0)
         q_low_step(3, HALF, HALF)
-        nc.vector.quantize_mx(out=s_codes[:].bitcast(FP8X4), scales=s_scales[:], in_=s_bf[:].rearrange("p e x -> p (e x)"))
+        state_quantise()
         q_quantise_and_read(0)
         q_join(1)
         q_join(2)
-        invert(0, 0)
         q_quantise_and_read(1)
+        invert(0, 0)
         invert(0, 1)
         q_quantise_and_read(2)
-        finish(0, 0)
+        finish(0, 0, 0)
+        finish(0, 0, 1)
         store(0, 0)
-        finish(0, 1)
-        store(0, 1)
+        finish(0, 1, 0)
         invert(1, 0)
         invert(1, 1)
+        finish(0, 1, 1)
+        store(0, 1)
         invert(2, 0)
         finish(1, 0)
         invert(2, 1)

@@ -46,46 +46,26 @@ def tile_rows_lin_elu1_norm_gate_kernel(tc, q, qa, ka, k, t, v, og, out):
 
         k_view = k.rearrange("h (p a j) d -> h a p (j d)", a=2, j=2)
         q_view = q.rearrange("h (c x u) n -> x (h c) u n", x=PACK, u=2)
-        v_view = v.rearrange("h (p j) e -> p h (j e)", j=PACK)
-        qa_view = qa.rearrange("(c m) o -> c (m o)", m=2 * PACK)
-
-        def load_k(h, a):
-            nc.sync.dma_start(out=k_raw[h][:, piece(a)], in_=k_view[h, a])
-
-        def load_v(heads):
-            nc.sync.dma_start(out=v_raw[:, heads], in_=v_view[:, heads])
-
-        def load_q(x):
-            nc.sync.dma_start(out=q_raw[:, place(x)], in_=q_view[x])
-
-        def load_qa():
-            for h in range(H):
-                for u in range(2):
-                    nc.sync.dma_start(
-                        out=qa_sb[ROWS * h + u : ROWS * (h + 1) : 2, 0 : 2 * PACK - 1],
-                        in_=qa_view[:, u : u + 2 * PACK - 1],
-                    )
-
-        def load_og():
-            nc.sync.dma_start(
-                out=og_raw[:].rearrange("p h (s r) e -> p (h s) (r e)", r=2),
-                in_=og.rearrange("h (s p r) e -> p (h s) (r e)", s=2, r=2),
-            )
-
-        both = slice(0, 2)
         nc.sync.dma_start(out=ka_sb[:], in_=ka)
         nc.sync.dma_start(out=t_sb[:], in_=t.rearrange("(p j) o -> p (j o)", j=PACK))
-        load_k(0, 0)
-        load_k(0, 1)
-        load_k(1, 0)
-        load_k(1, 1)
-        load_v(both)
-        load_q(0)
-        load_q(1)
-        load_q(2)
-        load_q(3)
-        load_qa()
-        load_og()
+        for h in range(H):
+            for a in range(2):
+                nc.sync.dma_start(out=k_raw[h][:, piece(a)], in_=k_view[h, a])
+        nc.sync.dma_start(out=v_raw[:], in_=v.rearrange("h (p j) e -> p h (j e)", j=PACK))
+        for x in range(0, 2):
+            nc.sync.dma_start(out=q_raw[:, place(x)], in_=q_view[x])
+        qa_view = qa.rearrange("(c m) o -> c (m o)", m=2 * PACK)
+        for h in range(H):
+            for u in range(2):
+                nc.sync.dma_start(
+                    out=qa_sb[ROWS * h + u : ROWS * (h + 1) : 2, 0 : 2 * PACK - 1], in_=qa_view[:, u : u + 2 * PACK - 1]
+                )
+        for x in range(2, 4):
+            nc.sync.dma_start(out=q_raw[:, place(x)], in_=q_view[x])
+        nc.sync.dma_start(
+            out=og_raw[:].rearrange("p h (s r) e -> p (h s) (r e)", r=2),
+            in_=og.rearrange("h (s p r) e -> p (h s) (r e)", s=2, r=2),
+        )
 
         k_weights = sbuf("k_weights", [P, 2, D, 2], F32)
         k_exp = [sbuf("k_exp%d" % h, [P, PACK * D], F32) for h in range(H)]
@@ -104,13 +84,20 @@ def tile_rows_lin_elu1_norm_gate_kernel(tc, q, qa, ka, k, t, v, og, out):
         s_codes = sbuf("s_codes", [P, E], U32)
         s_scales = sbuf("s_scales", [P, E], U8)
 
-        q_exp = sbuf("q_exp", [P, PACK * N], F32)
-        q_pos = sbuf("q_pos", [P, PACK * N], F32)
-        q_low = sbuf("q_low", [P, PACK * N], F32)
-        q_relu = sbuf("q_relu", [P, PACK * N], F32)
-        gate_tanh = [sbuf("gate_tanh%d" % a, [P, H, HALF // P * E], F32) for a in range(2)]
-        gate = [sbuf("gate%d" % a, [P, H, HALF // P * E], F32) for a in range(2)]
-        result = {(a, h): sbuf("result%d%d" % (a, h), [P, HALF // P, E], F32) for a in range(2) for h in range(H)}
+        q_exp = sbuf("q_exp", [P, 2, PACK, HALF], F32)
+        qa_size = sbuf("qa_size", [P, 2 * PACK], F32)
+        qa_half_sign = sbuf("qa_half_sign", [P, 2 * PACK], F32)
+        q_line = sbuf("q_line", [P, PACK, HALF], BF16)
+        q_curve = sbuf("q_curve", [P, PACK, HALF], BF16)
+        q_larger = sbuf("q_larger", [P, PACK, HALF], BF16)
+        q_signed = sbuf("q_signed", [P, PACK, HALF], BF16)
+        q_pos = sbuf("q_pos", [P, PACK * HALF], F32)
+        q_low = sbuf("q_low", [P, PACK * HALF], F32)
+        gate_tanh = [sbuf("gate_tanh%d" % half, [P, H, HALF // P * E], F32) for half in range(2)]
+        gate = [sbuf("gate%d" % half, [P, H, HALF // P * E], F32) for half in range(2)]
+        result = {
+            (half, h): sbuf("result%d%d" % (half, h), [P, HALF // P, E], F32) for half in range(2) for h in range(H)
+        }
         q_bf, q_codes, q_scales, y_ps, inverse = {}, {}, {}, {}, {}
         for g, (first, count) in enumerate(GROUPS):
             q_bf[g] = sbuf("q_bf%d" % g, [P, count * PACK], BF16)
@@ -126,45 +113,59 @@ def tile_rows_lin_elu1_norm_gate_kernel(tc, q, qa, ka, k, t, v, og, out):
         def as_pairs(pairs):
             return pairs.rearrange("p (n b) -> p n b", b=2)
 
+        def k_weights_step():
+            nc.vector.tensor_tensor(
+                out=k_weights[:],
+                in0=ka_sb[:].unsqueeze(1).unsqueeze(3).to_broadcast([P, 2, D, 2]),
+                in1=t_sb[:].rearrange("p (a b) -> p a b", a=2).unsqueeze(2).to_broadcast([P, 2, D, 2]),
+                op=ALU.mult,
+            )
+
         def k_exp_step(h, a):
             nc.scalar.activation(out=as_pairs(k_exp[h][:, piece(a)]), in_=in_pairs(k_raw[h][:, piece(a)]), func=ACT.Exp)
 
-        def k_pos_on_vector(h, a):
+        def k_pos_on_vector(a):
             nc.vector.tensor_scalar(
-                out=as_pairs(k_pos[h][:, piece(a)]), in0=in_pairs(k_raw[h][:, piece(a)]), scalar1=0.0, scalar2=1.0,
+                out=as_pairs(k_pos[0][:, piece(a)]), in0=in_pairs(k_raw[0][:, piece(a)]), scalar1=0.0, scalar2=1.0,
                 op0=ALU.max, op1=ALU.add,
             )
 
-        def k_pos_on_scalar(h, a):
-            nc.scalar.activation(out=as_pairs(k_pos[h][:, piece(a)]), in_=in_pairs(k_raw[h][:, piece(a)]), func=ACT.Relu)
+        def k_pos_on_scalar(a):
+            nc.scalar.activation(out=as_pairs(k_pos[1][:, piece(a)]), in_=in_pairs(k_raw[1][:, piece(a)]), func=ACT.Relu)
 
-        def features(a, part):
-            first, count = (0, D) if part is None else (D // 2 * part, D // 2)
-            return slice(2 * (D * a + first), 2 * (D * a + first + count))
-
-        def k_phi_step(h, a, part=None):
-            cols = features(a, part)
-            nc.vector.scalar_tensor_tensor(
-                out=k_phi[h][:, cols], in0=k_exp[h][:, cols], scalar=1.0, in1=k_pos[h][:, cols],
-                op0=ALU.min, op1=ALU.add,
-            )
-
-        def k_phi_by_min(h, a, part=None):
-            cols = features(a, part)
-            nc.vector.tensor_tensor(out=k_phi[h][:, cols], in0=k_exp[h][:, cols], in1=k_pos[h][:, cols], op=ALU.min)
+        def k_phi_step(h, a, first=0, count=D):
+            cols = slice(2 * (D * a + first), 2 * (D * a + first + count))
+            if h == 0:
+                nc.vector.tensor_tensor(out=k_phi[h][:, cols], in0=k_exp[h][:, cols], in1=k_pos[h][:, cols], op=ALU.min)
+            else:
+                nc.vector.scalar_tensor_tensor(
+                    out=k_phi[h][:, cols], in0=k_exp[h][:, cols], scalar=1.0, in1=k_pos[h][:, cols],
+                    op0=ALU.min, op1=ALU.add,
+                )
 
         def k_quantise(h, x):
             first = ROWS * (3 * x + 2 * h)
             cols = slice(first, first + ROWS)
             nc.vector.quantize_mx(out=k_codes[:, cols].bitcast(FP8X4), scales=k_scales[:, cols], in_=k_bf[h][:, x, :])
 
-        def k_weigh(h, part=None):
-            c = slice(0, 32) if part is None else slice(16 * part, 16 * (part + 1))
+        def k_weigh(h, first, count):
+            c = slice(first // (2 * PACK), (first + count) // (2 * PACK))
             nc.vector.tensor_tensor(
                 out=k_bf[h][:].rearrange("p x (c u a b) -> p c x u a b", u=2, a=2, b=2)[:, c],
                 in0=k_phi[h][:].rearrange("p (a c x u b) -> p c x u a b", a=2, x=PACK, u=2, b=2)[:, c],
                 in1=k_weights[:].rearrange("p a (c x u) b -> p c x u a b", x=PACK, u=2)[:, c],
                 op=ALU.mult,
+            )
+
+        def v_round():
+            nc.scalar.copy(
+                out=v_bf[:].rearrange("p h (c m j) -> p h c j m", m=4, j=PACK),
+                in_=v_raw[:].rearrange("p h (j c m) -> p h c j m", j=PACK, m=4),
+            )
+
+        def v_quantise():
+            nc.vector.quantize_mx(
+                out=v_codes[:].bitcast(FP8X4), scales=v_scales[:], in_=v_bf[:].rearrange("p h c -> p (h c)")
             )
 
         def state_product(h, x):
@@ -178,60 +179,100 @@ def tile_rows_lin_elu1_norm_gate_kernel(tc, q, qa, ka, k, t, v, og, out):
                 start=(h == 0 and x == 0), stop=(h == H - 1 and x == PACK - 1),
             )
 
-        def dealt(rows):
-            return rows.rearrange("p (s c m r) -> p s r c m", c=P // 4, m=4, r=2)
+        def state_round():
+            nc.scalar.activation(out=s_bf[:], in_=s_ps[:].rearrange("p x e -> p e x"), func=ACT.Copy, scale=1.0 / N)
 
-        def lines(terms, x, first, count):
-            tiles = terms[:].rearrange("p (s r c x m) -> p x s r c m", s=2, r=2, x=PACK, m=4)
-            return tiles[:, x, first // HALF : (first + count) // HALF]
-
-        def q_exp_step(x):
-            nc.scalar.activation(out=q_exp[:, place(x)], in_=q_raw[:, place(x)], func=ACT.Exp)
-
-        def q_pos_step(x, first=0, count=N):
-            cols = slice(N * x + first, N * x + first + count)
-            nc.vector.tensor_scalar(
-                out=lines(q_pos, x, first, count), in0=dealt(q_raw[:, cols]), scalar1=0.0, scalar2=qa_sb[:, 2 * x : 2 * x + 1],
-                op0=ALU.max, op1=ALU.mult,
+        def state_quantise():
+            nc.vector.quantize_mx(
+                out=s_codes[:].bitcast(FP8X4), scales=s_scales[:], in_=s_bf[:].rearrange("p e x -> p (e x)")
             )
 
-        def q_cols(x, a):
-            return slice(N * x + HALF * a, N * x + HALF * (a + 1))
+        def weight(weights, x):
+            return weights[:, 2 * x : 2 * x + 1]
 
-        def q_relu_pair(b):
-            def half(rows):
-                return rows[:].rearrange("p (x n) -> p x n", x=PACK)[:, 2 * b : 2 * b + 2, HALF:]
+        def q_exp_step(places, halves):
+            rows = q_raw[:].rearrange("p (x s n) -> p s x n", x=PACK, s=2)
+            nc.scalar.activation(out=q_exp[:, halves, places, :], in_=rows[:, halves, places, :], func=ACT.Exp)
 
-            nc.scalar.activation(out=half(q_relu), in_=half(q_raw), func=ACT.Relu)
+        def qa_size_step():
+            used = slice(0, 2 * PACK - 1)
+            nc.vector.scalar_tensor_tensor(
+                out=qa_size[:, used], in0=qa_sb[:, used], scalar=-1.0, in1=qa_sb[:, used], op0=ALU.mult, op1=ALU.max
+            )
 
-        def q_pos_on_scalar(x, a):
+        def qa_sign_step():
+            used = slice(0, 2 * PACK - 1)
+            nc.vector.tensor_scalar(
+                out=qa_half_sign[:, used], in0=qa_sb[:, used], scalar1=0.0, scalar2=0.5,
+                op0=ALU.is_ge, op1=ALU.subtract,
+            )
+
+        def q_line_step(x):
             nc.scalar.activation(
-                out=lines(q_pos, x, HALF * a, HALF), in_=dealt(q_relu[:, q_cols(x, a)]), func=ACT.Copy,
-                scale=qa_sb[:, 2 * x : 2 * x + 1],
+                out=q_line[:, x, :], in_=q_raw[:, N * x : N * x + HALF], func=ACT.Identity,
+                scale=weight(qa_size, x), bias=weight(qa_size, x),
             )
 
-        def q_low_step(x, first=0, count=N):
-            cols = slice(N * x + first, N * x + first + count)
+        def q_curve_step(x):
             nc.vector.tensor_scalar(
-                out=lines(q_low, x, first, count), in0=dealt(q_exp[:, cols]), scalar1=1.0, scalar2=qa_sb[:, 2 * x : 2 * x + 1],
+                out=q_curve[:, x, :], in0=q_exp[:, 0, x, :], scalar1=1.0, scalar2=weight(qa_size, x),
                 op0=ALU.min, op1=ALU.mult,
             )
 
-        def q_join(g):
+        def q_larger_step(places):
+            nc.vector.tensor_tensor(
+                out=q_larger[:, places, :], in0=q_line[:, places, :], in1=q_curve[:, places, :], op=ALU.max
+            )
+
+        def q_sign_step(x):
+            nc.vector.tensor_scalar(
+                out=q_signed[:, x, :], in0=q_larger[:, x, :], scalar1=weight(qa_half_sign, x), scalar2=2.0,
+                op0=ALU.mult, op1=ALU.mult,
+            )
+
+        def q_interleave(tiles):
+            nc.scalar.copy(
+                out=q_bf[0][:].rearrange("p (r c m x) -> p r c x m", r=2, m=4, x=PACK)[:, tiles],
+                in_=q_signed[:].rearrange("p x (c m r) -> p r c x m", m=4, r=2)[:, tiles],
+            )
+
+        def dealt(rows):
+            return rows.rearrange("p (c m r) -> p r c m", m=4, r=2)
+
+        def lines(terms, x):
+            return terms[:].rearrange("p (r c x m) -> p x r c m", r=2, x=PACK, m=4)[:, x]
+
+        def q_pos_step(x):
+            nc.vector.tensor_scalar(
+                out=lines(q_pos, x), in0=dealt(q_raw[:, N * x + HALF : N * (x + 1)]), scalar1=0.0,
+                scalar2=weight(qa_sb, x), op0=ALU.max, op1=ALU.mult,
+            )
+
+        def q_low_step(x, tiles):
+            nc.vector.tensor_scalar(
+                out=lines(q_low, x)[:, tiles], in0=dealt(q_exp[:, 1, x, :])[:, tiles], scalar1=1.0,
+                scalar2=weight(qa_sb, x), op0=ALU.min, op1=ALU.mult,
+            )
+
+        def q_join(g, columns=slice(0, P)):
             first, count = GROUPS[g]
 
             def block(terms):
-                return terms[:, PACK * first : PACK * (first + count)].rearrange("p (c x m) -> p c x m", x=PACK, m=4)
+                cols = slice(PACK * (first - HALF + columns.start), PACK * (first - HALF + columns.stop))
+                return terms[:, cols].rearrange("p (c x m) -> p c x m", x=PACK, m=4)
 
             nc.vector.tensor_tensor(
-                out=q_bf[g][:].rearrange("p (c m x) -> p c x m", m=4, x=PACK), in0=block(q_pos), in1=block(q_low),
-                op=ALU.add,
+                out=q_bf[g][:, PACK * columns.start : PACK * columns.stop].rearrange("p (c m x) -> p c x m", m=4, x=PACK),
+                in0=block(q_pos), in1=block(q_low), op=ALU.add,
             )
 
-        def q_quantise_and_read(g):
-            first, count = GROUPS[g]
-            nc.vector.quantize_mx(out=q_codes[g][:].bitcast(FP8X4), scales=q_scales[g][:], in_=q_bf[g][:])
-            for r in range(count // P):
+        def q_quantise_and_read(g, tiles):
+            cols = slice(P * tiles.start, P * tiles.stop)
+            nc.vector.quantize_mx(
+                out=q_codes[g][:, cols].bitcast(FP8X4), scales=q_scales[g][:, cols],
+                in_=q_bf[g][:, PACK * cols.start : PACK * cols.stop],
+            )
+            for r in range(tiles.start, tiles.stop):
                 cols = slice(P * r, P * (r + 1))
                 for h in range(H):
                     rows = slice(ROWS * h, ROWS * (h + 1))
@@ -242,50 +283,21 @@ def tile_rows_lin_elu1_norm_gate_kernel(tc, q, qa, ka, k, t, v, og, out):
                         start=True, stop=True,
                     )
 
-        def tanh_step(a, heads=slice(0, H)):
-            tiles = og_raw[:, heads, HALF // P * a : HALF // P * (a + 1), :]
+        def tanh_step(half, heads):
+            tiles = og_raw[:, heads, HALF // P * half : HALF // P * (half + 1), :]
             nc.scalar.activation(
-                out=gate_tanh[a][:, heads], in_=tiles.rearrange("p h r e -> p h (r e)"), func=ACT.Tanh, scale=0.5
+                out=gate_tanh[half][:, heads], in_=tiles.rearrange("p h r e -> p h (r e)"), func=ACT.Tanh, scale=0.5
             )
 
-        def gate_step(a, heads=slice(0, H)):
+        def gate_step(half, heads):
             nc.scalar.activation(
-                out=gate[a][:, heads], in_=gate_tanh[a][:, heads], func=ACT.Identity, scale=0.5, bias=0.5
-            )
-
-        def v_round(heads):
-            nc.scalar.copy(
-                out=v_bf[:, heads].rearrange("p h (c m j) -> p h c j m", m=4, j=PACK),
-                in_=v_raw[:, heads].rearrange("p h (j c m) -> p h c j m", j=PACK, m=4),
-            )
-
-        def v_quantise(heads):
-            cols = slice(E * heads.start, E * heads.stop)
-            nc.vector.quantize_mx(
-                out=v_codes[:, cols].bitcast(FP8X4), scales=v_scales[:, cols],
-                in_=v_bf[:, heads].rearrange("p h c -> p (h c)"),
-            )
-
-        def k_weights_step():
-            nc.vector.tensor_tensor(
-                out=k_weights[:],
-                in0=ka_sb[:].unsqueeze(1).unsqueeze(3).to_broadcast([P, 2, D, 2]),
-                in1=t_sb[:].rearrange("p (a b) -> p a b", a=2).unsqueeze(2).to_broadcast([P, 2, D, 2]),
-                op=ALU.mult,
-            )
-
-        def state_round():
-            nc.scalar.activation(out=s_bf[:], in_=s_ps[:].rearrange("p x e -> p e x"), func=ACT.Copy, scale=1.0 / N)
-
-        def state_quantise():
-            nc.vector.quantize_mx(
-                out=s_codes[:].bitcast(FP8X4), scales=s_scales[:], in_=s_bf[:].rearrange("p e x -> p (e x)")
+                out=gate[half][:, heads], in_=gate_tanh[half][:, heads], func=ACT.Identity, scale=0.5, bias=0.5
             )
 
         def invert(g, h):
             nc.vector.reciprocal(out=inverse[g, h][:], in_=y_ps[g, h][:, E - 1 :: E])
 
-        def finish(g, h, r=0):
+        def finish(g, h, r):
             first, count = GROUPS[g]
             half, tile = first // HALF, first % HALF // P + r
             nc.vector.scalar_tensor_tensor(
@@ -299,80 +311,87 @@ def tile_rows_lin_elu1_norm_gate_kernel(tc, q, qa, ka, k, t, v, og, out):
             rows = out[h, HALF * half : HALF * (half + 1), :]
             queue.dma_start(out=rows.rearrange("(p r) e -> p r e", r=2), in_=result[half, h][:])
 
-        k_exp_step(0, 0)
-        k_exp_step(0, 1)
-        k_exp_step(1, 0)
-        k_pos_on_scalar(1, 0)
-        k_exp_step(1, 1)
-        k_pos_on_scalar(1, 1)
-        v_round(both)
-        q_exp_step(0)
-        q_exp_step(1)
-        q_exp_step(2)
-        q_exp_step(3)
-        q_relu_pair(0)
-        q_relu_pair(1)
+        head0, head1, both_heads = slice(0, 1), slice(1, 2), slice(0, H)
+        low_features, high_features = (0, D // 2), (D // 2, D // 2)
+        low_places, high_places = slice(0, 2), slice(2, 4)
+        first_half, second_half, both_halves = slice(0, 1), slice(1, 2), slice(0, 2)
+        tile0, tile1, both_tiles = slice(0, 1), slice(1, 2), slice(0, 2)
+
+        for h in range(H):
+            for a in range(2):
+                k_exp_step(h, a)
+                if h == 1:
+                    k_pos_on_scalar(a)
+        v_round()
         k_weights_step()
-        k_pos_on_vector(0, 0)
-        k_pos_on_vector(0, 1)
-        k_phi_by_min(0, 0)
-        k_phi_by_min(0, 1, 0)
-        k_phi_by_min(0, 1, 1)
-        k_weigh(0, 0)
-        k_weigh(0, 1)
+        k_pos_on_vector(0)
+        k_pos_on_vector(1)
+        k_phi_step(0, 0)
+        k_phi_step(0, 1, *low_features)
+        k_phi_step(0, 1, *high_features)
+        k_weigh(0, *low_features)
+        k_weigh(0, *high_features)
         k_phi_step(1, 0)
-        k_quantise(0, 0)
-        k_quantise(0, 1)
-        k_quantise(0, 2)
-        k_quantise(0, 3)
-        k_phi_step(1, 1, 0)
-        k_phi_step(1, 1, 1)
-        k_weigh(1, 0)
-        v_quantise(both)
-        state_product(0, 0)
-        state_product(0, 1)
-        state_product(0, 2)
-        state_product(0, 3)
-        k_weigh(1, 1)
-        q_pos_step(0, 0, HALF)
-        q_pos_step(1, 0, HALF)
-        k_quantise(1, 0)
-        state_product(1, 0)
-        k_quantise(1, 1)
-        state_product(1, 1)
-        k_quantise(1, 2)
-        state_product(1, 2)
-        k_quantise(1, 3)
-        state_product(1, 3)
-        q_pos_on_scalar(0, 1)
-        q_pos_on_scalar(1, 1)
+        for x in range(PACK):
+            k_quantise(0, x)
+        k_phi_step(1, 1, *low_features)
+        k_phi_step(1, 1, *high_features)
+        k_weigh(1, *low_features)
+        qa_size_step()
+        v_quantise()
+        for x in range(PACK):
+            state_product(0, x)
+        k_weigh(1, *high_features)
+        q_exp_step(slice(0, 1), both_halves)
+        q_exp_step(slice(1, 2), both_halves)
+        q_line_step(0)
+        q_line_step(1)
+        q_exp_step(high_places, first_half)
+        q_line_step(2)
+        q_line_step(3)
+        q_exp_step(high_places, second_half)
+        q_curve_step(0)
+        q_curve_step(1)
+        for x in range(PACK):
+            k_quantise(1, x)
+            state_product(1, x)
+        q_larger_step(low_places)
+        qa_sign_step()
+        q_curve_step(2)
+        q_curve_step(3)
+        q_sign_step(0)
+        q_sign_step(1)
+        q_pos_step(0)
+        q_larger_step(high_places)
+        q_pos_step(1)
+        q_pos_step(2)
+        q_sign_step(2)
+        q_sign_step(3)
         state_round()
-        q_pos_on_scalar(2, 1)
-        q_pos_on_scalar(3, 1)
-        tanh_step(0)
-        tanh_step(1, slice(0, 1))
-        gate_step(0)
-        tanh_step(1, slice(1, 2))
-        gate_step(1, slice(0, 1))
-        gate_step(1, slice(1, 2))
-        q_pos_step(2, 0, HALF)
-        q_pos_step(3, 0, HALF)
-        q_low_step(0)
-        q_low_step(1, 0, HALF)
-        q_low_step(2, 0, HALF)
-        q_low_step(3, 0, HALF)
-        q_low_step(1, HALF, HALF)
-        q_low_step(2, HALF, HALF)
-        q_join(0)
-        q_low_step(3, HALF, HALF)
+        q_interleave(tile0)
+        q_interleave(tile1)
+        tanh_step(0, head0)
+        tanh_step(0, head1)
+        gate_step(0, head0)
+        gate_step(0, head1)
+        tanh_step(1, head0)
+        tanh_step(1, head1)
+        gate_step(1, head0)
+        gate_step(1, head1)
+        q_pos_step(3)
+        for x in range(PACK - 1):
+            q_low_step(x, both_tiles)
+        q_low_step(PACK - 1, tile0)
+        q_low_step(PACK - 1, tile1)
         state_quantise()
-        q_quantise_and_read(0)
         q_join(1)
+        q_quantise_and_read(0, tile0)
+        q_quantise_and_read(0, tile1)
         q_join(2)
-        q_quantise_and_read(1)
+        q_quantise_and_read(1, tile0)
         invert(0, 0)
+        q_quantise_and_read(2, tile0)
         invert(0, 1)
-        q_quantise_and_read(2)
         finish(0, 0, 0)
         finish(0, 0, 1)
         store(0, 0)
@@ -382,10 +401,10 @@ def tile_rows_lin_elu1_norm_gate_kernel(tc, q, qa, ka, k, t, v, og, out):
         finish(0, 1, 1)
         store(0, 1)
         invert(2, 0)
-        finish(1, 0)
+        finish(1, 0, 0)
         invert(2, 1)
-        finish(2, 0)
+        finish(2, 0, 0)
         store(1, 0)
-        finish(1, 1)
-        finish(2, 1)
+        finish(1, 1, 0)
+        finish(2, 1, 0)
         store(1, 1)

@@ -52,7 +52,7 @@ def tile_rows_lin_elu1_norm_gate_kernel(tc, q, qa, ka, k, t, v, og, out):
             for a in range(2):
                 nc.sync.dma_start(out=k_raw[h][:, piece(a)], in_=k_view[h, a])
         nc.sync.dma_start(out=v_raw[:], in_=v.rearrange("h (p j) e -> p h (j e)", j=PACK))
-        for x in range(0, 2):
+        for x in range(PACK // 2):
             nc.sync.dma_start(out=q_raw[:, place(x)], in_=q_view[x])
         qa_view = qa.rearrange("(c m) o -> c (m o)", m=2 * PACK)
         for h in range(H):
@@ -60,7 +60,7 @@ def tile_rows_lin_elu1_norm_gate_kernel(tc, q, qa, ka, k, t, v, og, out):
                 nc.sync.dma_start(
                     out=qa_sb[ROWS * h + u : ROWS * (h + 1) : 2, 0 : 2 * PACK - 1], in_=qa_view[:, u : u + 2 * PACK - 1]
                 )
-        for x in range(2, 4):
+        for x in range(PACK // 2, PACK):
             nc.sync.dma_start(out=q_raw[:, place(x)], in_=q_view[x])
         nc.sync.dma_start(
             out=og_raw[:].rearrange("p h (s r) e -> p (h s) (r e)", r=2),
@@ -187,6 +187,8 @@ def tile_rows_lin_elu1_norm_gate_kernel(tc, q, qa, ka, k, t, v, og, out):
                 out=s_codes[:].bitcast(FP8X4), scales=s_scales[:], in_=s_bf[:].rearrange("p e x -> p (e x)")
             )
 
+        qa_columns = slice(0, 2 * PACK - 1)
+
         def weight(weights, x):
             return weights[:, 2 * x : 2 * x + 1]
 
@@ -195,15 +197,14 @@ def tile_rows_lin_elu1_norm_gate_kernel(tc, q, qa, ka, k, t, v, og, out):
             nc.scalar.activation(out=q_exp[:, halves, places, :], in_=rows[:, halves, places, :], func=ACT.Exp)
 
         def qa_size_step():
-            used = slice(0, 2 * PACK - 1)
             nc.vector.scalar_tensor_tensor(
-                out=qa_size[:, used], in0=qa_sb[:, used], scalar=-1.0, in1=qa_sb[:, used], op0=ALU.mult, op1=ALU.max
+                out=qa_size[:, qa_columns], in0=qa_sb[:, qa_columns], scalar=-1.0, in1=qa_sb[:, qa_columns],
+                op0=ALU.mult, op1=ALU.max,
             )
 
         def qa_sign_step():
-            used = slice(0, 2 * PACK - 1)
             nc.vector.tensor_scalar(
-                out=qa_half_sign[:, used], in0=qa_sb[:, used], scalar1=0.0, scalar2=0.5,
+                out=qa_half_sign[:, qa_columns], in0=qa_sb[:, qa_columns], scalar1=0.0, scalar2=0.5,
                 op0=ALU.is_ge, op1=ALU.subtract,
             )
 
@@ -242,10 +243,11 @@ def tile_rows_lin_elu1_norm_gate_kernel(tc, q, qa, ka, k, t, v, og, out):
         def lines(terms, x):
             return terms[:].rearrange("p (r c x m) -> p x r c m", r=2, x=PACK, m=4)[:, x]
 
-        def q_pos_step(x):
+        def q_pos_step(places):
             nc.vector.tensor_scalar(
-                out=lines(q_pos, x), in0=dealt(q_raw[:, N * x + HALF : N * (x + 1)]), scalar1=0.0,
-                scalar2=weight(qa_sb, x), op0=ALU.max, op1=ALU.mult,
+                out=q_pos[:].rearrange("p (r c x m) -> p x r c m", r=2, x=PACK, m=4)[:, places],
+                in0=q_raw[:].rearrange("p (x s c m r) -> p s x r c m", x=PACK, s=2, m=4, r=2)[:, 1, places],
+                scalar1=0.0, scalar2=1.0, op0=ALU.max, op1=ALU.add,
             )
 
         def q_low_step(x, tiles):
@@ -254,45 +256,39 @@ def tile_rows_lin_elu1_norm_gate_kernel(tc, q, qa, ka, k, t, v, og, out):
                 scalar2=weight(qa_sb, x), op0=ALU.min, op1=ALU.mult,
             )
 
-        def q_join(g, columns=slice(0, P)):
+        def q_join(g):
             first, count = GROUPS[g]
-
-            def block(terms):
-                cols = slice(PACK * (first - HALF + columns.start), PACK * (first - HALF + columns.stop))
-                return terms[:, cols].rearrange("p (c x m) -> p c x m", x=PACK, m=4)
-
+            cols = slice(PACK * (first - HALF), PACK * (first - HALF + count))
             nc.vector.tensor_tensor(
-                out=q_bf[g][:, PACK * columns.start : PACK * columns.stop].rearrange("p (c m x) -> p c x m", m=4, x=PACK),
-                in0=block(q_pos), in1=block(q_low), op=ALU.add,
+                out=q_bf[g][:].rearrange("p (c m x) -> p c x m", m=4, x=PACK),
+                in0=q_pos[:, cols].rearrange("p (c x m) -> p c x m", x=PACK, m=4),
+                in1=q_low[:, cols].rearrange("p (c x m) -> p c x m", x=PACK, m=4),
+                op=ALU.mult,
             )
 
-        def q_quantise_and_read(g, tiles):
-            cols = slice(P * tiles.start, P * tiles.stop)
+        def q_quantise_and_read(g, r):
+            cols = slice(P * r, P * (r + 1))
             nc.vector.quantize_mx(
                 out=q_codes[g][:, cols].bitcast(FP8X4), scales=q_scales[g][:, cols],
-                in_=q_bf[g][:, PACK * cols.start : PACK * cols.stop],
+                in_=q_bf[g][:, PACK * P * r : PACK * P * (r + 1)],
             )
-            for r in range(tiles.start, tiles.stop):
-                cols = slice(P * r, P * (r + 1))
-                for h in range(H):
-                    rows = slice(ROWS * h, ROWS * (h + 1))
-                    nc.tensor.matmul_mx(
-                        out=y_ps[g, h][:, cols],
-                        lhsT=q_codes[g][rows, cols].bitcast(FP8X4), lhsT_scale=q_scales[g][rows, cols],
-                        rhs=s_codes[rows, :].bitcast(FP8X4), rhs_scale=s_scales[rows, :],
-                        start=True, stop=True,
-                    )
+            for h in range(H):
+                rows = slice(ROWS * h, ROWS * (h + 1))
+                nc.tensor.matmul_mx(
+                    out=y_ps[g, h][:, cols],
+                    lhsT=q_codes[g][rows, cols].bitcast(FP8X4), lhsT_scale=q_scales[g][rows, cols],
+                    rhs=s_codes[rows, :].bitcast(FP8X4), rhs_scale=s_scales[rows, :],
+                    start=True, stop=True,
+                )
 
-        def tanh_step(half, heads):
-            tiles = og_raw[:, heads, HALF // P * half : HALF // P * (half + 1), :]
+        def tanh_step(half, h):
+            tiles = og_raw[:, h, HALF // P * half : HALF // P * (half + 1), :]
             nc.scalar.activation(
-                out=gate_tanh[half][:, heads], in_=tiles.rearrange("p h r e -> p h (r e)"), func=ACT.Tanh, scale=0.5
+                out=gate_tanh[half][:, h], in_=tiles.rearrange("p r e -> p (r e)"), func=ACT.Tanh, scale=0.5
             )
 
-        def gate_step(half, heads):
-            nc.scalar.activation(
-                out=gate[half][:, heads], in_=gate_tanh[half][:, heads], func=ACT.Identity, scale=0.5, bias=0.5
-            )
+        def gate_step(half, h):
+            nc.scalar.activation(out=gate[half][:, h], in_=gate_tanh[half][:, h], func=ACT.Identity, scale=0.5, bias=0.5)
 
         def invert(g, h):
             nc.vector.reciprocal(out=inverse[g, h][:], in_=y_ps[g, h][:, E - 1 :: E])
@@ -311,7 +307,6 @@ def tile_rows_lin_elu1_norm_gate_kernel(tc, q, qa, ka, k, t, v, og, out):
             rows = out[h, HALF * half : HALF * (half + 1), :]
             queue.dma_start(out=rows.rearrange("(p r) e -> p r e", r=2), in_=result[half, h][:])
 
-        head0, head1, both_heads = slice(0, 1), slice(1, 2), slice(0, H)
         low_features, high_features = (0, D // 2), (D // 2, D // 2)
         low_places, high_places = slice(0, 2), slice(2, 4)
         first_half, second_half, both_halves = slice(0, 1), slice(1, 2), slice(0, 2)
@@ -323,6 +318,7 @@ def tile_rows_lin_elu1_norm_gate_kernel(tc, q, qa, ka, k, t, v, og, out):
                 if h == 1:
                     k_pos_on_scalar(a)
         v_round()
+
         k_weights_step()
         k_pos_on_vector(0)
         k_pos_on_vector(1)
@@ -342,14 +338,16 @@ def tile_rows_lin_elu1_norm_gate_kernel(tc, q, qa, ka, k, t, v, og, out):
         for x in range(PACK):
             state_product(0, x)
         k_weigh(1, *high_features)
+
         q_exp_step(slice(0, 1), both_halves)
-        q_exp_step(slice(1, 2), both_halves)
+        q_exp_step(slice(1, 2), first_half)
         q_line_step(0)
         q_line_step(1)
         q_exp_step(high_places, first_half)
         q_line_step(2)
         q_line_step(3)
-        q_exp_step(high_places, second_half)
+        q_exp_step(slice(1, PACK), second_half)
+
         q_curve_step(0)
         q_curve_step(1)
         for x in range(PACK):
@@ -361,37 +359,35 @@ def tile_rows_lin_elu1_norm_gate_kernel(tc, q, qa, ka, k, t, v, og, out):
         q_curve_step(3)
         q_sign_step(0)
         q_sign_step(1)
-        q_pos_step(0)
+        q_pos_step(low_places)
         q_larger_step(high_places)
-        q_pos_step(1)
-        q_pos_step(2)
+        q_pos_step(high_places)
         q_sign_step(2)
         q_sign_step(3)
+
         state_round()
         q_interleave(tile0)
         q_interleave(tile1)
-        tanh_step(0, head0)
-        tanh_step(0, head1)
-        gate_step(0, head0)
-        gate_step(0, head1)
-        tanh_step(1, head0)
-        tanh_step(1, head1)
-        gate_step(1, head0)
-        gate_step(1, head1)
-        q_pos_step(3)
+        for half in range(2):
+            for h in range(H):
+                tanh_step(half, h)
+            for h in range(H):
+                gate_step(half, h)
+
         for x in range(PACK - 1):
             q_low_step(x, both_tiles)
         q_low_step(PACK - 1, tile0)
         q_low_step(PACK - 1, tile1)
         state_quantise()
         q_join(1)
-        q_quantise_and_read(0, tile0)
-        q_quantise_and_read(0, tile1)
+        q_quantise_and_read(0, 0)
+        q_quantise_and_read(0, 1)
         q_join(2)
-        q_quantise_and_read(1, tile0)
+        q_quantise_and_read(1, 0)
         invert(0, 0)
-        q_quantise_and_read(2, tile0)
+        q_quantise_and_read(2, 0)
         invert(0, 1)
+
         finish(0, 0, 0)
         finish(0, 0, 1)
         store(0, 0)

@@ -131,7 +131,7 @@ def tile_rows_lin_elu1_norm_gate_kernel(tc, q, qa, ka, k, t, v, og, out):
             )
 
         def k_pos_on_scalar(a):
-            nc.scalar.activation(out=as_pairs(k_pos[1][:, piece(a)]), in_=in_pairs(k_raw[1][:, piece(a)]), func=ACT.Relu)
+            nc.scalar.activation(out=as_pairs(k_pos[1][:, piece(a)]), in_=in_pairs(k_raw[1][:, piece(a)]), func=ACT.Identity, bias=1.0)
 
         def k_phi_step(h, a, first=0, count=D):
             cols = slice(2 * (D * a + first), 2 * (D * a + first + count))
@@ -140,7 +140,7 @@ def tile_rows_lin_elu1_norm_gate_kernel(tc, q, qa, ka, k, t, v, og, out):
             else:
                 nc.vector.scalar_tensor_tensor(
                     out=k_phi[h][:, cols], in0=k_exp[h][:, cols], scalar=1.0, in1=k_pos[h][:, cols],
-                    op0=ALU.min, op1=ALU.add,
+                    op0=ALU.min, op1=ALU.max,
                 )
 
         def k_quantise(h, x):
@@ -158,10 +158,11 @@ def tile_rows_lin_elu1_norm_gate_kernel(tc, q, qa, ka, k, t, v, og, out):
             )
 
         def v_round():
-            nc.scalar.copy(
-                out=v_bf[:].rearrange("p h (c m j) -> p h c j m", m=4, j=PACK),
-                in_=v_raw[:].rearrange("p h (j c m) -> p h c j m", j=PACK, m=4),
-            )
+            for h in range(H):
+                nc.scalar.activation(
+                    out=v_bf[:, h].rearrange("p (c m j) -> p c j m", m=4, j=PACK),
+                    in_=v_raw[:, h].rearrange("p (j c m) -> p c j m", j=PACK, m=4), func=ACT.Identity,
+                )
 
         def v_quantise():
             nc.vector.quantize_mx(
@@ -180,7 +181,7 @@ def tile_rows_lin_elu1_norm_gate_kernel(tc, q, qa, ka, k, t, v, og, out):
             )
 
         def state_round():
-            nc.scalar.activation(out=s_bf[:], in_=s_ps[:].rearrange("p x e -> p e x"), func=ACT.Copy, scale=1.0 / N)
+            nc.scalar.activation(out=s_bf[:], in_=s_ps[:].rearrange("p x e -> p e x"), func=ACT.Identity, scale=1.0 / N)
 
         def state_quantise():
             nc.vector.quantize_mx(
@@ -231,10 +232,10 @@ def tile_rows_lin_elu1_norm_gate_kernel(tc, q, qa, ka, k, t, v, og, out):
                 op0=ALU.mult, op1=ALU.mult,
             )
 
-        def q_interleave(tiles):
-            nc.scalar.copy(
-                out=q_bf[0][:].rearrange("p (r c m x) -> p r c x m", r=2, m=4, x=PACK)[:, tiles],
-                in_=q_signed[:].rearrange("p x (c m r) -> p r c x m", m=4, r=2)[:, tiles],
+        def q_interleave(r):
+            nc.scalar.activation(
+                out=q_bf[0][:].rearrange("p (r c m x) -> p r c x m", r=2, m=4, x=PACK)[:, r],
+                in_=q_signed[:].rearrange("p x (c m r) -> p r c x m", m=4, r=2)[:, r], func=ACT.Identity,
             )
 
         def dealt(rows):
@@ -281,10 +282,10 @@ def tile_rows_lin_elu1_norm_gate_kernel(tc, q, qa, ka, k, t, v, og, out):
                     start=True, stop=True,
                 )
 
-        def tanh_step(half, h):
-            tiles = og_raw[:, h, HALF // P * half : HALF // P * (half + 1), :]
+        def tanh_step(half):
+            tiles = og_raw[:, :, HALF // P * half : HALF // P * (half + 1), :]
             nc.scalar.activation(
-                out=gate_tanh[half][:, h], in_=tiles.rearrange("p r e -> p (r e)"), func=ACT.Tanh, scale=0.5
+                out=gate_tanh[half][:], in_=tiles.rearrange("p h r e -> p h (r e)"), func=ACT.Tanh, scale=0.5
             )
 
         def gate_step(half, h):
@@ -315,8 +316,8 @@ def tile_rows_lin_elu1_norm_gate_kernel(tc, q, qa, ka, k, t, v, og, out):
         for h in range(H):
             for a in range(2):
                 k_exp_step(h, a)
-                if h == 1:
-                    k_pos_on_scalar(a)
+        for a in range(2):
+            k_pos_on_scalar(a)
         v_round()
 
         k_weights_step()
@@ -341,40 +342,41 @@ def tile_rows_lin_elu1_norm_gate_kernel(tc, q, qa, ka, k, t, v, og, out):
 
         q_exp_step(slice(0, 1), both_halves)
         q_exp_step(slice(1, 2), first_half)
+        q_exp_step(high_places, first_half)
         q_line_step(0)
         q_line_step(1)
-        q_exp_step(high_places, first_half)
         q_line_step(2)
         q_line_step(3)
         q_exp_step(slice(1, PACK), second_half)
 
         q_curve_step(0)
         q_curve_step(1)
+        qa_sign_step()
         for x in range(PACK):
             k_quantise(1, x)
             state_product(1, x)
-        q_larger_step(low_places)
-        qa_sign_step()
         q_curve_step(2)
         q_curve_step(3)
-        q_sign_step(0)
-        q_sign_step(1)
+        q_larger_step(low_places)
         q_pos_step(low_places)
         q_larger_step(high_places)
-        q_pos_step(high_places)
+        q_sign_step(0)
+        q_sign_step(1)
+        q_low_step(0, both_tiles)
         q_sign_step(2)
         q_sign_step(3)
+        q_pos_step(high_places)
 
         state_round()
-        q_interleave(tile0)
-        q_interleave(tile1)
+        q_interleave(0)
+        q_interleave(1)
         for half in range(2):
-            for h in range(H):
-                tanh_step(half, h)
+            tanh_step(half)
+        for half in range(2):
             for h in range(H):
                 gate_step(half, h)
 
-        for x in range(PACK - 1):
+        for x in range(1, PACK - 1):
             q_low_step(x, both_tiles)
         q_low_step(PACK - 1, tile0)
         q_low_step(PACK - 1, tile1)

@@ -282,10 +282,10 @@ def tile_rows_lin_elu1_norm_gate_kernel(tc, q, qa, ka, k, t, v, og, out):
                     start=True, stop=True,
                 )
 
-        def tanh_step(half):
-            tiles = og_raw[:, :, HALF // P * half : HALF // P * (half + 1), :]
+        def tanh_step(half, h):
+            tiles = og_raw[:, h, HALF // P * half : HALF // P * (half + 1), :]
             nc.scalar.activation(
-                out=gate_tanh[half][:], in_=tiles.rearrange("p h r e -> p h (r e)"), func=ACT.Tanh, scale=0.5
+                out=gate_tanh[half][:, h], in_=tiles.rearrange("p r e -> p (r e)"), func=ACT.Tanh, scale=0.5
             )
 
         def gate_step(half, h):
@@ -304,7 +304,7 @@ def tile_rows_lin_elu1_norm_gate_kernel(tc, q, qa, ka, k, t, v, og, out):
             )
 
         def store(half, h):
-            queue = nc.scalar if h == 0 else nc.sync
+            queue = nc.scalar if (half, h) == (1, 0) else nc.sync
             rows = out[h, HALF * half : HALF * (half + 1), :]
             queue.dma_start(out=rows.rearrange("(p r) e -> p r e", r=2), in_=result[half, h][:])
 
@@ -316,8 +316,8 @@ def tile_rows_lin_elu1_norm_gate_kernel(tc, q, qa, ka, k, t, v, og, out):
         for h in range(H):
             for a in range(2):
                 k_exp_step(h, a)
-        for a in range(2):
-            k_pos_on_scalar(a)
+                if h == 1:
+                    k_pos_on_scalar(a)
         v_round()
 
         k_weights_step()
@@ -342,9 +342,9 @@ def tile_rows_lin_elu1_norm_gate_kernel(tc, q, qa, ka, k, t, v, og, out):
 
         q_exp_step(slice(0, 1), both_halves)
         q_exp_step(slice(1, 2), first_half)
-        q_exp_step(high_places, first_half)
         q_line_step(0)
         q_line_step(1)
+        q_exp_step(high_places, first_half)
         q_line_step(2)
         q_line_step(3)
         q_exp_step(slice(1, PACK), second_half)
@@ -355,28 +355,28 @@ def tile_rows_lin_elu1_norm_gate_kernel(tc, q, qa, ka, k, t, v, og, out):
         for x in range(PACK):
             k_quantise(1, x)
             state_product(1, x)
+        q_larger_step(low_places)
         q_curve_step(2)
         q_curve_step(3)
-        q_larger_step(low_places)
-        q_pos_step(low_places)
-        q_larger_step(high_places)
         q_sign_step(0)
         q_sign_step(1)
-        q_low_step(0, both_tiles)
+        q_pos_step(slice(0, 1))
+        q_larger_step(high_places)
+        q_pos_step(slice(1, 3))
         q_sign_step(2)
         q_sign_step(3)
-        q_pos_step(high_places)
+        q_pos_step(slice(3, 4))
 
         state_round()
         q_interleave(0)
         q_interleave(1)
         for half in range(2):
-            tanh_step(half)
-        for half in range(2):
+            for h in range(H):
+                tanh_step(half, h)
             for h in range(H):
                 gate_step(half, h)
 
-        for x in range(1, PACK - 1):
+        for x in range(PACK - 1):
             q_low_step(x, both_tiles)
         q_low_step(PACK - 1, tile0)
         q_low_step(PACK - 1, tile1)

@@ -86,7 +86,7 @@ def tile_rows_lin_elu1_norm_gate_kernel(tc, q, qa, ka, k, t, v, og, out):
 
         q_exp = sbuf("q_exp", [P, 2, PACK, HALF], F32)
         qa_size = sbuf("qa_size", [P, 2 * PACK], F32)
-        qa_half_sign = sbuf("qa_half_sign", [P, 2 * PACK], F32)
+        qa_sign = sbuf("qa_sign", [P, 2 * PACK], F32)
         q_line = sbuf("q_line", [P, PACK, HALF], BF16)
         q_curve = sbuf("q_curve", [P, PACK, HALF], BF16)
         q_larger = sbuf("q_larger", [P, PACK, HALF], BF16)
@@ -197,17 +197,9 @@ def tile_rows_lin_elu1_norm_gate_kernel(tc, q, qa, ka, k, t, v, og, out):
             rows = q_raw[:].rearrange("p (x s n) -> p s x n", x=PACK, s=2)
             nc.scalar.activation(out=q_exp[:, halves, places, :], in_=rows[:, halves, places, :], func=ACT.Exp)
 
-        def qa_size_step():
-            nc.vector.scalar_tensor_tensor(
-                out=qa_size[:, qa_columns], in0=qa_sb[:, qa_columns], scalar=-1.0, in1=qa_sb[:, qa_columns],
-                op0=ALU.mult, op1=ALU.max,
-            )
-
-        def qa_sign_step():
-            nc.vector.tensor_scalar(
-                out=qa_half_sign[:, qa_columns], in0=qa_sb[:, qa_columns], scalar1=0.0, scalar2=0.5,
-                op0=ALU.is_ge, op1=ALU.subtract,
-            )
+        def qa_steps():
+            nc.scalar.activation(out=qa_size[:, qa_columns], in_=qa_sb[:, qa_columns], func=ACT.Abs)
+            nc.scalar.activation(out=qa_sign[:, qa_columns], in_=qa_sb[:, qa_columns], func=ACT.Sign)
 
         def q_line_step(x):
             nc.scalar.activation(
@@ -228,7 +220,7 @@ def tile_rows_lin_elu1_norm_gate_kernel(tc, q, qa, ka, k, t, v, og, out):
 
         def q_sign_step(x):
             nc.vector.tensor_scalar(
-                out=q_signed[:, x, :], in0=q_larger[:, x, :], scalar1=weight(qa_half_sign, x), scalar2=2.0,
+                out=q_signed[:, x, :], in0=q_larger[:, x, :], scalar1=weight(qa_sign, x), scalar2=1.0,
                 op0=ALU.mult, op1=ALU.mult,
             )
 
@@ -304,9 +296,8 @@ def tile_rows_lin_elu1_norm_gate_kernel(tc, q, qa, ka, k, t, v, og, out):
             )
 
         def store(half, h):
-            queue = nc.scalar if (half, h) == (1, 0) else nc.sync
             rows = out[h, HALF * half : HALF * (half + 1), :]
-            queue.dma_start(out=rows.rearrange("(p r) e -> p r e", r=2), in_=result[half, h][:])
+            nc.sync.dma_start(out=rows.rearrange("(p r) e -> p r e", r=2), in_=result[half, h][:])
 
         low_features, high_features = (0, D // 2), (D // 2, D // 2)
         low_places, high_places = slice(0, 2), slice(2, 4)
@@ -334,13 +325,13 @@ def tile_rows_lin_elu1_norm_gate_kernel(tc, q, qa, ka, k, t, v, og, out):
         k_phi_step(1, 1, *low_features)
         k_phi_step(1, 1, *high_features)
         k_weigh(1, *low_features)
-        qa_size_step()
         v_quantise()
         for x in range(PACK):
             state_product(0, x)
         k_weigh(1, *high_features)
 
         q_exp_step(slice(0, 1), both_halves)
+        qa_steps()
         q_exp_step(slice(1, 2), first_half)
         q_line_step(0)
         q_line_step(1)
@@ -351,7 +342,6 @@ def tile_rows_lin_elu1_norm_gate_kernel(tc, q, qa, ka, k, t, v, og, out):
 
         q_curve_step(0)
         q_curve_step(1)
-        qa_sign_step()
         for x in range(PACK):
             k_quantise(1, x)
             state_product(1, x)

@@ -63,9 +63,11 @@ def tile_rows_lin_elu1_norm_gate_kernel(tc, q, qa, ka, k, t, v, og, out):
         for x in range(PACK // 2, PACK):
             nc.sync.dma_start(out=q_raw[:, place(x)], in_=q_view[x])
         nc.sync.dma_start(
-            out=og_raw[:].rearrange("p h (s r) e -> p (h s) (r e)", r=2),
-            in_=og.rearrange("h (s p r) e -> p (h s) (r e)", s=2, r=2),
+            out=og_raw[:, :, 0:2, :].rearrange("p h r e -> p h (r e)"),
+            in_=og[:, 0:HALF, :].rearrange("h (p r) e -> p h (r e)", r=2),
         )
+        for h in range(H):
+            nc.sync.dma_start(out=og_raw[:, h, 2:4, :], in_=og[h, HALF:N, :].rearrange("(r p) e -> p r e", r=2))
 
         k_weights = sbuf("k_weights", [P, 2, D, 2], F32)
         k_exp = [sbuf("k_exp%d" % h, [P, PACK * D], F32) for h in range(H)]
@@ -231,7 +233,7 @@ def tile_rows_lin_elu1_norm_gate_kernel(tc, q, qa, ka, k, t, v, og, out):
             )
 
         def dealt(rows):
-            return rows.rearrange("p (c m r) -> p r c m", m=4, r=2)
+            return rows.rearrange("p (r c m) -> p r c m", m=4, r=2)
 
         def lines(terms, x):
             return terms[:].rearrange("p (r c x m) -> p x r c m", r=2, x=PACK, m=4)[:, x]
@@ -239,7 +241,7 @@ def tile_rows_lin_elu1_norm_gate_kernel(tc, q, qa, ka, k, t, v, og, out):
         def q_pos_step(places):
             nc.vector.tensor_scalar(
                 out=q_pos[:].rearrange("p (r c x m) -> p x r c m", r=2, x=PACK, m=4)[:, places],
-                in0=q_raw[:].rearrange("p (x s c m r) -> p s x r c m", x=PACK, s=2, m=4, r=2)[:, 1, places],
+                in0=q_raw[:].rearrange("p (x s r c m) -> p s x r c m", x=PACK, s=2, m=4, r=2)[:, 1, places],
                 scalar1=0.0, scalar2=1.0, op0=ALU.max, op1=ALU.add,
             )
 
@@ -295,9 +297,10 @@ def tile_rows_lin_elu1_norm_gate_kernel(tc, q, qa, ka, k, t, v, og, out):
                 op0=ALU.mult, op1=ALU.mult,
             )
 
-        def store(half, h):
+        def store(half, h, tiles=slice(0, 2)):
             rows = out[h, HALF * half : HALF * (half + 1), :]
-            nc.sync.dma_start(out=rows.rearrange("(p r) e -> p r e", r=2), in_=result[half, h][:])
+            order = "(p r) e -> p r e" if half == 0 else "(r p) e -> p r e"
+            nc.sync.dma_start(out=rows.rearrange(order, r=2)[:, tiles], in_=result[half, h][:, tiles])
 
         low_features, high_features = (0, D // 2), (D // 2, D // 2)
         low_places, high_places = slice(0, 2), slice(2, 4)
@@ -394,5 +397,6 @@ def tile_rows_lin_elu1_norm_gate_kernel(tc, q, qa, ka, k, t, v, og, out):
         finish(2, 0, 0)
         store(1, 0)
         finish(1, 1, 0)
+        store(1, 1, tile0)
         finish(2, 1, 0)
-        store(1, 1)
+        store(1, 1, tile1)

from contextlib import ExitStack

import concourse.mybir as mybir

H, D, N, E = 2, 256, 512, 128
FLOPS = 2 * (2 * H * N * D * E)

F32 = mybir.dt.float32
BF16 = mybir.dt.bfloat16
U32 = mybir.dt.uint32
U8 = mybir.dt.uint8
FP8X4 = mybir.dt.float8_e4m3fn_x4
ACT = mybir.ActivationFunctionType
ALU = mybir.AluOpType

P = 128
PACK = 4
ROWS = D // PACK
HALF = N // 2
GROUPS = [(0, HALF), (HALF, P), (HALF + P, P)]


def tile_rows_lin_elu1_norm_gate_kernel(tc, q, qa, ka, k, t, v, og, out):
    nc = tc.nc
    with ExitStack() as ctx:
        sb = ctx.enter_context(tc.tile_pool(name="sb", bufs=1))
        ps = ctx.enter_context(tc.psum_pool(name="ps", bufs=1))
        ctx.enter_context(tc.manual_schedule())

        def sbuf(name, shape, dtype):
            return sb.tile(shape, dtype, name=name, align_bytes=64)

        k_raw = [sbuf("k_raw%d" % h, [P, PACK * D], F32) for h in range(H)]
        q_raw = sbuf("q_raw", [P, PACK * N], F32)
        t_sb = sbuf("t_sb", [P, PACK], F32)
        ka_sb = sbuf("ka_sb", [P, D], F32)
        v_raw = sbuf("v_raw", [P, H, PACK * E], F32)
        qa_sb = sbuf("qa_sb", [P, 2 * PACK], F32)
        og_raw = sbuf("og_raw", [P, H, N // P, E], F32)

        def piece(a):
            return slice(2 * D * a, 2 * D * (a + 1))

        def place(x):
            return slice(N * x, N * (x + 1))

        k_view = k.rearrange("h (p a j) d -> h a p (j d)", a=2, j=2)
        q_view = q.rearrange("h (c x u) n -> x (h c) u n", x=PACK, u=2)
        nc.sync.dma_start(out=ka_sb[:], in_=ka)
        nc.sync.dma_start(out=t_sb[:], in_=t.rearrange("(p j) o -> p (j o)", j=PACK))
        for h in range(H):
            for a in range(2):
                nc.sync.dma_start(out=k_raw[h][:, piece(a)], in_=k_view[h, a])
        nc.sync.dma_start(out=v_raw[:], in_=v.rearrange("h (p j) e -> p h (j e)", j=PACK))
        for x in range(PACK // 2):
            nc.sync.dma_start(out=q_raw[:, place(x)], in_=q_view[x])
        qa_view = qa.rearrange("(c m) o -> c (m o)", m=2 * PACK)
        for h in range(H):
            for u in range(2):
                nc.sync.dma_start(
                    out=qa_sb[ROWS * h + u : ROWS * (h + 1) : 2, 0 : 2 * PACK - 1], in_=qa_view[:, u : u + 2 * PACK - 1]
                )
        for x in range(PACK // 2, PACK):
            nc.sync.dma_start(out=q_raw[:, place(x)], in_=q_view[x])
        nc.sync.dma_start(
            out=og_raw[:, :, 0:2, :].rearrange("p h r e -> p h (r e)"),
            in_=og[:, 0:HALF, :].rearrange("h (p r) e -> p h (r e)", r=2),
        )
        for h in range(H):
            nc.sync.dma_start(out=og_raw[:, h, 2:4, :], in_=og[h, HALF:N, :].rearrange("(r p) e -> p r e", r=2))

        k_weights = sbuf("k_weights", [P, 2, D, 2], F32)
        k_exp = [sbuf("k_exp%d" % h, [P, PACK * D], F32) for h in range(H)]
        k_pos = [sbuf("k_pos%d" % h, [P, PACK * D], F32) for h in range(H)]
        k_phi = [sbuf("k_phi%d" % h, [P, PACK * D], F32) for h in range(H)]
        k_bf = [sbuf("k_bf%d" % h, [P, PACK, D], BF16) for h in range(H)]
        v_bf = sbuf("v_bf", [P, H, E * PACK], BF16)
        v_codes = sbuf("v_codes", [P, H * E], U32)
        v_scales = sbuf("v_scales", [P, H * E], U8)
        k_codes = sbuf("k_codes", [P, PACK * 3 * ROWS], U32)
        k_scales = sbuf("k_scales", [P, PACK * 3 * ROWS], U8)
        nc.vector.memset(k_codes[:].rearrange("p (x g c) -> p x g c", x=PACK, g=3)[:, :, 1, :], 0)
        nc.vector.memset(k_scales[:].bitcast(U32).rearrange("p (x g c) -> p x g c", x=PACK, g=3)[:, :, 1, :], 0)
        s_ps = ps.tile([P, PACK, E], F32, name="s_ps")
        s_bf = sbuf("s_bf", [P, E, PACK], BF16)
        s_codes = sbuf("s_codes", [P, E], U32)
        s_scales = sbuf("s_scales", [P, E], U8)

        q_exp = sbuf("q_exp", [P, 2, PACK, HALF], F32)
        qa_size = sbuf("qa_size", [P, 2 * PACK], F32)
        qa_sign = sbuf("qa_sign", [P, 2 * PACK], F32)
        q_line = sbuf("q_line", [P, PACK, HALF], BF16)
        q_curve = sbuf("q_curve", [P, PACK, HALF], BF16)
        q_larger = sbuf("q_larger", [P, PACK, HALF], BF16)
        q_signed = sbuf("q_signed", [P, PACK, HALF], BF16)
        q_pos = sbuf("q_pos", [P, PACK * HALF], F32)
        q_low = sbuf("q_low", [P, PACK * HALF], F32)
        gate_tanh = [sbuf("gate_tanh%d" % half, [P, H, HALF // P * E], F32) for half in range(2)]
        gate = [sbuf("gate%d" % half, [P, H, HALF // P * E], F32) for half in range(2)]
        result = {
            (half, h): sbuf("result%d%d" % (half, h), [P, HALF // P, E], F32) for half in range(2) for h in range(H)
        }
        q_bf, q_codes, q_scales, y_ps, inverse = {}, {}, {}, {}, {}
        for g, (first, count) in enumerate(GROUPS):
            q_bf[g] = sbuf("q_bf%d" % g, [P, count * PACK], BF16)
            q_codes[g] = sbuf("q_codes%d" % g, [P, count], U32)
            q_scales[g] = sbuf("q_scales%d" % g, [P, count], U8)
            for h in range(H):
                y_ps[g, h] = ps.tile([P, count // P * E], F32, name="y_ps%d%d" % (g, h))
                inverse[g, h] = sbuf("inverse%d%d" % (g, h), [P, count // P], F32)

        def in_pairs(rows):
            return rows.rearrange("p (b n) -> p n b", b=2)

        def as_pairs(pairs):
            return pairs.rearrange("p (n b) -> p n b", b=2)

        def k_weights_step():
            nc.vector.tensor_tensor(
                out=k_weights[:],
                in0=ka_sb[:].unsqueeze(1).unsqueeze(3).to_broadcast([P, 2, D, 2]),
                in1=t_sb[:].rearrange("p (a b) -> p a b", a=2).unsqueeze(2).to_broadcast([P, 2, D, 2]),
                op=ALU.mult,
            )

        def k_exp_step(h, a):
            nc.scalar.activation(out=as_pairs(k_exp[h][:, piece(a)]), in_=in_pairs(k_raw[h][:, piece(a)]), func=ACT.Exp)

        def k_pos_on_vector(a):
            nc.vector.tensor_scalar(
                out=as_pairs(k_pos[0][:, piece(a)]), in0=in_pairs(k_raw[0][:, piece(a)]), scalar1=0.0, scalar2=1.0,
                op0=ALU.max, op1=ALU.add,
            )

        def k_pos_on_scalar(a):
            nc.scalar.activation(out=as_pairs(k_pos[1][:, piece(a)]), in_=in_pairs(k_raw[1][:, piece(a)]), func=ACT.Identity, bias=1.0)

        def k_phi_step(h, a, first=0, count=D):
            cols = slice(2 * (D * a + first), 2 * (D * a + first + count))
            if h == 0:
                nc.vector.tensor_tensor(out=k_phi[h][:, cols], in0=k_exp[h][:, cols], in1=k_pos[h][:, cols], op=ALU.min)
            else:
                nc.vector.scalar_tensor_tensor(
                    out=k_phi[h][:, cols], in0=k_exp[h][:, cols], scalar=1.0, in1=k_pos[h][:, cols],
                    op0=ALU.min, op1=ALU.max,
                )

        def k_quantise(h, x):
            first = ROWS * (3 * x + 2 * h)
            cols = slice(first, first + ROWS)
            nc.vector.quantize_mx(out=k_codes[:, cols].bitcast(FP8X4), scales=k_scales[:, cols], in_=k_bf[h][:, x, :])

        def k_weigh(h, first, count):
            c = slice(first // (2 * PACK), (first + count) // (2 * PACK))
            nc.vector.tensor_tensor(
                out=k_bf[h][:].rearrange("p x (c u a b) -> p c x u a b", u=2, a=2, b=2)[:, c],
                in0=k_phi[h][:].rearrange("p (a c x u b) -> p c x u a b", a=2, x=PACK, u=2, b=2)[:, c],
                in1=k_weights[:].rearrange("p a (c x u) b -> p c x u a b", x=PACK, u=2)[:, c],
                op=ALU.mult,
            )

        def v_round():
            for h in range(H):
                nc.scalar.activation(
                    out=v_bf[:, h].rearrange("p (c m j) -> p c j m", m=4, j=PACK),
                    in_=v_raw[:, h].rearrange("p (j c m) -> p c j m", j=PACK, m=4), func=ACT.Identity,
                )

        def v_quantise():
            nc.vector.quantize_mx(
                out=v_codes[:].bitcast(FP8X4), scales=v_scales[:], in_=v_bf[:].rearrange("p h c -> p (h c)")
            )

        def state_product(h, x):
            first = ROWS * (3 * x + h)
            k_cols = slice(first, first + P)
            v_cols = slice(E * h, E * (h + 1))
            nc.tensor.matmul_mx(
                out=s_ps[:, x, :],
                lhsT=k_codes[:, k_cols].bitcast(FP8X4), lhsT_scale=k_scales[:, k_cols],
                rhs=v_codes[:, v_cols].bitcast(FP8X4), rhs_scale=v_scales[:, v_cols],
                start=(h == 0 and x == 0), stop=(h == H - 1 and x == PACK - 1),
            )

        def state_round():
            nc.scalar.activation(out=s_bf[:], in_=s_ps[:].rearrange("p x e -> p e x"), func=ACT.Identity, scale=1.0 / N)

        def state_quantise():
            nc.vector.quantize_mx(
                out=s_codes[:].bitcast(FP8X4), scales=s_scales[:], in_=s_bf[:].rearrange("p e x -> p (e x)")
            )

        qa_columns = slice(0, 2 * PACK - 1)

        def weight(weights, x):
            return weights[:, 2 * x : 2 * x + 1]

        def q_exp_step(places, halves):
            rows = q_raw[:].rearrange("p (x s n) -> p s x n", x=PACK, s=2)
            nc.scalar.activation(out=q_exp[:, halves, places, :], in_=rows[:, halves, places, :], func=ACT.Exp)

        def qa_steps():
            nc.scalar.activation(out=qa_size[:, qa_columns], in_=qa_sb[:, qa_columns], func=ACT.Abs)
            nc.scalar.activation(out=qa_sign[:, qa_columns], in_=qa_sb[:, qa_columns], func=ACT.Sign)

        def q_line_step(x):
            nc.scalar.activation(
                out=q_line[:, x, :], in_=q_raw[:, N * x : N * x + HALF], func=ACT.Identity,
                scale=weight(qa_size, x), bias=weight(qa_size, x),
            )

        def q_curve_step(x):
            nc.vector.tensor_scalar(
                out=q_curve[:, x, :], in0=q_exp[:, 0, x, :], scalar1=1.0, scalar2=weight(qa_size, x),
                op0=ALU.min, op1=ALU.mult,
            )

        def q_larger_step(places):
            nc.vector.tensor_tensor(
                out=q_larger[:, places, :], in0=q_line[:, places, :], in1=q_curve[:, places, :], op=ALU.max
            )

        def q_sign_step(x):
            nc.vector.tensor_scalar(
                out=q_signed[:, x, :], in0=q_larger[:, x, :], scalar1=weight(qa_sign, x), scalar2=1.0,
                op0=ALU.mult, op1=ALU.mult,
            )

        def q_interleave(r):
            nc.scalar.activation(
                out=q_bf[0][:].rearrange("p (r c m x) -> p r c x m", r=2, m=4, x=PACK)[:, r],
                in_=q_signed[:].rearrange("p x (c m r) -> p r c x m", m=4, r=2)[:, r], func=ACT.Identity,
            )

        def dealt(rows):
            return rows.rearrange("p (r c m) -> p r c m", m=4, r=2)

        def lines(terms, x):
            return terms[:].rearrange("p (r c x m) -> p x r c m", r=2, x=PACK, m=4)[:, x]

        def q_pos_step(places):
            nc.vector.tensor_scalar(
                out=q_pos[:].rearrange("p (r c x m) -> p x r c m", r=2, x=PACK, m=4)[:, places],
                in0=q_raw[:].rearrange("p (x s r c m) -> p s x r c m", x=PACK, s=2, m=4, r=2)[:, 1, places],
                scalar1=0.0, scalar2=1.0, op0=ALU.max, op1=ALU.add,
            )

        def q_low_step(x, tiles):
            nc.vector.tensor_scalar(
                out=lines(q_low, x)[:, tiles], in0=dealt(q_exp[:, 1, x, :])[:, tiles], scalar1=1.0,
                scalar2=weight(qa_sb, x), op0=ALU.min, op1=ALU.mult,
            )

        def q_join(g):
            first, count = GROUPS[g]
            cols = slice(PACK * (first - HALF), PACK * (first - HALF + count))
            nc.vector.tensor_tensor(
                out=q_bf[g][:].rearrange("p (c m x) -> p c x m", m=4, x=PACK),
                in0=q_pos[:, cols].rearrange("p (c x m) -> p c x m", x=PACK, m=4),
                in1=q_low[:, cols].rearrange("p (c x m) -> p c x m", x=PACK, m=4),
                op=ALU.mult,
            )

        def q_quantise_and_read(g, r):
            cols = slice(P * r, P * (r + 1))
            nc.vector.quantize_mx(
                out=q_codes[g][:, cols].bitcast(FP8X4), scales=q_scales[g][:, cols],
                in_=q_bf[g][:, PACK * P * r : PACK * P * (r + 1)],
            )
            for h in range(H):
                rows = slice(ROWS * h, ROWS * (h + 1))
                nc.tensor.matmul_mx(
                    out=y_ps[g, h][:, cols],
                    lhsT=q_codes[g][rows, cols].bitcast(FP8X4), lhsT_scale=q_scales[g][rows, cols],
                    rhs=s_codes[rows, :].bitcast(FP8X4), rhs_scale=s_scales[rows, :],
                    start=True, stop=True,
                )

        def tanh_step(half, h):
            tiles = og_raw[:, h, HALF // P * half : HALF // P * (half + 1), :]
            nc.scalar.activation(
                out=gate_tanh[half][:, h], in_=tiles.rearrange("p r e -> p (r e)"), func=ACT.Tanh, scale=0.5
            )

        def gate_step(half, h):
            nc.scalar.activation(out=gate[half][:, h], in_=gate_tanh[half][:, h], func=ACT.Identity, scale=0.5, bias=0.5)

        def invert(g, h):
            nc.vector.reciprocal(out=inverse[g, h][:], in_=y_ps[g, h][:, E - 1 :: E])

        def finish(g, h, r):
            first, count = GROUPS[g]
            half, tile = first // HALF, first % HALF // P + r
            nc.vector.scalar_tensor_tensor(
                out=result[half, h][:, tile, :], in0=y_ps[g, h][:, E * r : E * (r + 1)],
                scalar=inverse[g, h][:, r : r + 1], in1=gate[half][:, h, E * tile : E * (tile + 1)],
                op0=ALU.mult, op1=ALU.mult,
            )

        def store(half, h, tiles=slice(0, 2)):
            rows = out[h, HALF * half : HALF * (half + 1), :]
            order = "(p r) e -> p r e" if half == 0 else "(r p) e -> p r e"
            nc.sync.dma_start(out=rows.rearrange(order, r=2)[:, tiles], in_=result[half, h][:, tiles])

        low_features, high_features = (0, D // 2), (D // 2, D // 2)
        low_places, high_places = slice(0, 2), slice(2, 4)
        first_half, second_half, both_halves = slice(0, 1), slice(1, 2), slice(0, 2)
        tile0, tile1, both_tiles = slice(0, 1), slice(1, 2), slice(0, 2)

        for h in range(H):
            for a in range(2):
                k_exp_step(h, a)
                if h == 1:
                    k_pos_on_scalar(a)
        v_round()

        k_weights_step()
        k_pos_on_vector(0)
        k_pos_on_vector(1)
        k_phi_step(0, 0)
        k_phi_step(0, 1, *low_features)
        k_phi_step(0, 1, *high_features)
        k_weigh(0, *low_features)
        k_weigh(0, *high_features)
        k_phi_step(1, 0)
        for x in range(PACK):
            k_quantise(0, x)
        k_phi_step(1, 1, *low_features)
        k_phi_step(1, 1, *high_features)
        k_weigh(1, *low_features)
        v_quantise()
        for x in range(PACK):
            state_product(0, x)
        k_weigh(1, *high_features)

        q_exp_step(slice(0, 1), both_halves)
        qa_steps()
        q_exp_step(slice(1, 2), first_half)
        q_line_step(0)
        q_line_step(1)
        q_exp_step(high_places, first_half)
        q_line_step(2)
        q_line_step(3)
        q_exp_step(slice(1, PACK), second_half)

        q_curve_step(0)
        q_curve_step(1)
        for x in range(PACK):
            k_quantise(1, x)
            state_product(1, x)
        q_larger_step(low_places)
        q_curve_step(2)
        q_curve_step(3)
        q_sign_step(0)
        q_sign_step(1)
        q_pos_step(slice(0, 1))
        q_larger_step(high_places)
        q_pos_step(slice(1, 3))
        q_sign_step(2)
        q_sign_step(3)
        q_pos_step(slice(3, 4))

        state_round()
        q_interleave(0)
        q_interleave(1)
        for half in range(2):
            for h in range(H):
                tanh_step(half, h)
            for h in range(H):
                gate_step(half, h)

        for x in range(PACK - 1):
            q_low_step(x, both_tiles)
        q_low_step(PACK - 1, tile0)
        q_low_step(PACK - 1, tile1)
        state_quantise()
        q_join(1)
        q_quantise_and_read(0, 0)
        q_quantise_and_read(0, 1)
        q_join(2)
        q_quantise_and_read(1, 0)
        invert(0, 0)
        q_quantise_and_read(2, 0)
        invert(0, 1)

        finish(0, 0, 0)
        finish(0, 0, 1)
        store(0, 0)
        finish(0, 1, 0)
        invert(1, 0)
        invert(1, 1)
        finish(0, 1, 1)
        store(0, 1)
        invert(2, 0)
        finish(1, 0, 0)
        invert(2, 1)
        finish(2, 0, 0)
        store(1, 0)
        finish(1, 1, 0)
        store(1, 1, tile0)
        finish(2, 1, 0)
        store(1, 1, tile1)
